import numpy as np, ml_dtypes
CORES = [2,3,42,43,82,83,122,123]
N = 8
BF = ml_dtypes.bfloat16
W, K, T, S, ND = 4096, 256, 3, 3, 3
def stir(rng, a, n):
    r = rng.random(a.shape, dtype=np.float32)
    s = np.concatenate([np.sort(r, axis=-1), np.full(r.shape[:-1] + (1,), 2, np.float32)], axis=-1)
    return np.where(r < np.take_along_axis(s, n[..., None], -1), (a + rng.integers(1, 64, a.shape)) & 63, a)
def near(rng, pro, n, counts):
    a = pro[np.arange(8)[None, :, None], rng.integers(0, pro.shape[1], (N, 8, n))]
    return stir(rng, a, rng.choice(np.array(counts), (N, 8, n)))
def protos(rng, first):
    return stir(rng, np.repeat(first, 2, axis=1), np.full((8, 2), 3))
def parts(rng):
    pro = protos(rng, rng.integers(0, 64, (8, 1, 16)))
    return (near(rng, pro, K, [0, 1, 1, 2, 2, 3, 16]), rng.integers(0, 256, (N, 8, K, 16)), near(rng, pro, W, [0, 1, 1, 2, 3, 16]), rng.integers(0, 256, (N, 8, W, 16)),
            rng.integers(0, 256, (8, 16, 2)), rng.integers(900, 1900, (N, 8, 16)))
def tile(a):
    return np.ascontiguousarray(a.transpose(0, 1, 3, 2)).reshape(N, 128, -1).astype(np.float32).astype(BF)
def pack(x, g, lx, lm, w, lim):
    return {"xw": tile(x), "gw": tile(g), "lex": tile(lx), "mng": tile(lm),
            "wts": np.ascontiguousarray(np.broadcast_to(w.reshape(1, 128, 2), (N, 128, 2))).astype(np.int32), "th": lim.reshape(N, 128, 1).astype(np.int32)}
def setup_inputs(rng):
    return pack(*parts(rng))
def setup_inputs_spread(rng):
    pro = protos(rng, (64 * rng.random((8, 1, 16)) ** 3).astype(np.int64))
    x = near(rng, pro, K, [0, 1, 1, 2, 3, 4, 16]); lx = near(rng, pro, W, [0, 1, 1, 2, 4, 16])
    g = np.floor(256 * rng.random((N, 8, K, 1)) ** 2 * rng.random((N, 8, K, 16))).astype(np.int64)
    lm = np.floor(256 * rng.random((N, 8, W, 1)) ** 2 * rng.random((N, 8, W, 16))).astype(np.int64)
    w = np.exp2(8 * rng.random((8, 16, 2))).astype(np.int64) - 1; w = np.where(rng.random(w.shape) < 0.25, rng.integers(0, 256, w.shape), w)
    lim = np.minimum(np.exp2(4 + 8.2 * rng.random((N, 8, 16))).astype(np.int64), 4081)
    return pack(x, g, lx, lm, w, lim)
def setup_inputs_ends(rng):
    base = np.repeat(63 * rng.integers(0, 2, (8, 1, 16)), 2, axis=1); base[:, 1] = np.where(rng.random((8, 16)) < 0.15, 63 - base[:, 1], base[:, 1])
    def some(n, share):
        a = base[np.arange(8)[None, :, None], rng.integers(0, 2, (N, 8, n))]
        return np.where(rng.random(a.shape) < share, np.where(rng.random(a.shape) < 0.6, 63 - a, rng.choice(np.array([1, 31, 62]), a.shape)), a)
    def both(n):
        return 255 * np.where(rng.random((N, 8, n, 1)) < 0.5, rng.integers(0, 2, (N, 8, n, 1)), rng.integers(0, 2, (N, 8, n, 16)))
    x = some(K, 0.08); lx = some(W, 0.1); g = both(K); lm = both(W)
    w = 255 * rng.integers(0, 2, (8, 16, 2)); w[:5, 15] = 65; w[5, :, 0] = 255; w[6, 0] = 65; w[7, 14:, 0] = 65; w[7, 14:, 1] = 0
    w[4, 13, 0] = 89; w[4, 13, 1] = 0; w[4, 14, 0] = 0; w[4, 14, 1] = 227
    lim = np.full((N, 8, 16), 4081); odd = np.arange(N) % 2 == 1
    lim = np.where(odd[:, None, None] & (rng.random(lim.shape) < 0.25), 0, lim); lim[:, 0, 0] = 0
    x[:, 0, :, 0] = 63; lx[:, 0, :, 0] = 63
    x[:, 5, 1] = 63; x[:, 5, K - 1] = 63
    for i in (3, K - 2):
        x[:, 1:5, i] = 0; x[:, 1:5, i, 15] = 63
    p = (((W - 1) ** 2 >> 5) + W - 1) & (W - 1)
    lx[:, 1:5, p] = 0; lx[:, 1:5, p, 15] = 63; lx[:, 1:5, p, 13] = 63
    x[:, 4, 4] = 0; x[:, 4, 4, 13] = 46; x[:, 4, 4, 14] = 36; x[:, 4, 4, 15] = 63
    p = ((4093 * 4075 >> 5) + 4093) & (W - 1)
    lx[:, 4, p] = x[:, 4, 4]; lx[:, 4, p, 0] = 63; lx[:, 4, p + 1] = 63; lm[:, 4, p] = 255; g[:, 4, 4] = 0
    x[:, 7, 4] = 0; x[:, 7, 4, 14] = 63; g[:, 7, 4] = 0
    for i in (5, K - 1):
        x[:, 7, i] = 0; x[:, 7, i, 15] = 63; g[:, 7, i] = 255 if i == 5 else 0
    lx[:, 7, 0] = 63; lx[:, 7, W - 1] = 0; lx[:, 7, W - 1, 14:] = 63; lm[:, 7, W - 1] = 255
    g[:, 6, :, 15] = 255; lm[:, 6, :, 15] = 255; g[:, 6, :, 14] = 0; lm[:, 6, :, 14] = 0
    return pack(x, g, lx, lm, w, lim)
def setup_inputs_corners(rng):
    pro = rng.integers(0, 64, (8, 1, 16)); lx = near(rng, pro, W, [0, 0, 1]); lx[:, :, 0] = pro[:, 0]
    x = near(rng, pro, K, [0, 1, ND, ND + 1, ND + 2, 16])
    w = rng.integers(0, 256, (8, 16, 2)); w[0] = 0; w[1] = 255; w[2, :, 0] = 0; w[2, :, 1] = 255; w[3, :, 1] = w[3, :, 0]; w[4, :15] = 0; w[4, 15] = 255; w[5, 1:] = 0; w[5, 0] = 255
    w[6] = 255 * rng.integers(0, 2, (16, 2)); w = w[rng.permutation(8)]
    def mean(n):
        return np.where(rng.random((N, 8, n, 1)) < 0.6, 255 * rng.integers(0, 2, (N, 8, n, 1)), rng.integers(0, 256, (N, 8, n, 16)))
    case = (np.arange(8)[None, :] + np.arange(N)[:, None] + rng.integers(0, 5)) % 5; case = case[:, :, None]
    lim = np.where(case == 0, 0, np.where(case == 1, 4081, np.where(case == 2, 4081 * rng.integers(0, 2, (N, 8, 16)), np.where(case == 3, 1, rng.integers(900, 1900, (N, 8, 16))))))
    return pack(x, mean(K), lx, mean(W), w, lim)
def setup_inputs_ties(rng):
    pro = rng.integers(0, 64, (8, 1, 16)); far = np.where(rng.permutation(8) < 4, 0, rng.integers(130, 251, 8)).reshape(8, 1, 1)
    b = rng.integers(0, 255 - far, (8, 1, 16)); side = rng.integers(0, 2, (8, 1, 16))
    x = near(rng, pro, K, [0, 1, 1, 1]); lx = near(rng, pro, W, [0, ND, ND, ND + 1])
    g = b + far * side + rng.integers(0, 2, (N, 8, K, 16)); lm = b + far * (1 - side) + rng.integers(0, 2, (N, 8, W, 16))
    lim = np.where(far[:, 0] == 0, rng.integers(5, 13, (N, 8, 16)), 16 * far[:, 0] + rng.integers(-3, 5, (N, 8, 16)))
    return pack(x, g, lx, lm, rng.integers(0, 256, (8, 16, 2)), lim)
def setup_inputs_alike(rng):
    o = rng.permutation(64); al = o[:4]; kinds = (rng.integers(0, 4, (8, 1, 16)) + (rng.random((8, 6, 16)) < 0.12) * rng.integers(1, 4, (8, 6, 16))) & 3
    pro = al[kinds]; x = near(rng, pro, K, [0]); lx = near(rng, pro, W, [0])
    g = rng.integers(0, 256, (N, 8, K, 16)); lm = rng.integers(0, 256, (N, 8, W, 16)); w = rng.integers(0, 256, (8, 16, 2))
    even = (np.arange(N) % 2 == 0)[:, None, None]
    lim = np.where((rng.random((N, 8, 1)) < 0.6) | even, 4081, rng.integers(900, 1900, (N, 8, 16)))
    two = np.sort(o[4:12].reshape(4, 2), axis=1); spot = np.arange(W); four = [int(e) for e in rng.permutation(8)[:4]]
    for e in four:
        lx[:, e] = pro[e, 0]; lx[:, e, :, 0] = two[spot & 3, 1]; lx[:, e, :, 14] = spot & 63; lx[:, e, :, 15] = spot >> 6
        w[e] = 0; w[e, 14, 0] = 1; w[e, 15, 0] = 64; lim[:, e] = 4081
    for r in range(N):
        j = rng.permutation(W >> 1)[:K]
        put = [4 * (j >> 1) + 2 + (j & 1),
               np.full(K, 4 * rng.integers(0, W >> 2) + 2 + rng.integers(0, 2)),
               4 * rng.permutation(W >> 2)[:K] + (np.arange(K) >= 256),
               np.repeat(4 * rng.permutation(W >> 2)[:K >> 1] + (np.arange(K >> 1) & 3), 2)]
        for e, p in zip(four, put):
            x[r, e] = pro[e, 0]; x[r, e, :, 0] = two[p & 3, 0]; x[r, e, :, 14] = p & 63; x[r, e, :, 15] = p >> 6
    e = four[2]
    g[:, e] = rng.integers(0, 41, (N, K, 16)) + 200 * even; lm[:, e] = rng.integers(0, 41, (N, W, 16)); lim[:, e] = rng.integers(700, 2500, (N, 16))
    return pack(x, g, lx, lm, w, lim)
def check_inputs(d):
    bad = []
    for k, lo, hi in (("xw", 0, 63), ("gw", 0, 255), ("lex", 0, 63), ("mng", 0, 255), ("wts", 0, 255), ("th", 0, 4081)):
        a = np.asarray(d[k]).astype(np.float64)
        if not (np.min(a) >= lo and np.max(a) <= hi): bad.append("range of " + k)
        elif np.any(a != np.floor(a)): bad.append("whole numbers of " + k)
    a = np.asarray(d["wts"])
    if np.any(a != a[:1]): bad.append("wts alike on all ranks")
    return bad
def visit(t, x, g, lx, lm, w, lim):
    p = w[..., :1] * x; u = (np.add.reduce(p, axis=1, keepdims=True) - p) & (W - 1)
    p = w[..., 1:] * x; u2 = (np.add.reduce(p, axis=1, keepdims=True) - p) & (W - 1)
    h = (((u * u2) >> 5) + u) & (W - 1)
    c = np.take_along_axis(lx, h.reshape(8, 1, 16 * K), 2).reshape(8, 16, 16, K)
    m = np.take_along_axis(lm, h.reshape(8, 1, 16 * K), 2).reshape(8, 16, 16, K)
    differ = np.add.reduce((c != x[:, :, None, :]).astype(np.int32), axis=1)
    far = np.add.reduce(np.abs(m - g[:, :, None, :]), axis=1)
    lane = np.arange(16); b = c[:, lane, lane, :]
    pair = (b != x) & (differ <= ND + 1)
    has = np.any(pair, axis=1); f = np.argmax(pair, axis=1)[:, None, :]
    def at(a):
        return np.take_along_axis(a, f, 1)[:, 0]
    xa, xb, hf = at(x), at(b), at(h)
    free = at((far < lim).astype(np.int32)) == 1
    pc = 64 * np.minimum(xa, xb) + np.maximum(xa, xb)
    flag = np.zeros(4096, bool); flag[pc[has & ~free]] = True
    merge = has & free & ~flag[pc]
    mf = np.take_along_axis(lm, hf[:, None, :], 2)
    row = lane[None, :, None]
    xn = np.where((row == f) & merge[:, None, :], np.minimum(x, b), x)
    xn = np.where((row == t) & ~has[:, None, :], b, xn)
    gn = np.where(merge[:, None, :], (g + mf) >> 1, g)
    for e in range(8):
        for i in np.flatnonzero(merge[e])[::-1]:
            lx[e, :, hf[e, i]] = xn[e, :, i]; lm[e, :, hf[e, i]] = gn[e, :, i]
    x[...] = xn; g[...] = gn
def reference(xw, gw, lex, mng, wts, th):
    x = xw.astype(np.float32).astype(np.int32).reshape(N, 8, 16, K); g = gw.astype(np.float32).astype(np.int32).reshape(N, 8, 16, K)
    lx = lex.astype(np.float32).astype(np.int32).reshape(N, 8, 16, W); lm = mng.astype(np.float32).astype(np.int32).reshape(N, 8, 16, W)
    w = wts.astype(np.int32).reshape(N, 8, 16, 2); lim = th.astype(np.int32).reshape(N, 8, 16, 1)
    for t in range(T):
        for r in range(N):
            v = (r + S * t) % N; visit(t, x[r], g[r], lx[v], lm[v], w[v], lim[v])
    return {"yx": x.reshape(N, 128, K).astype(np.float32).astype(BF), "yg": g.reshape(N, 128, K).astype(np.float32).astype(BF),
            "yl": lx.reshape(N, 128, W).astype(np.float32).astype(BF), "ym": np.add.reduce(lm, axis=3).reshape(N, 128, 1).astype(np.float32)}

@@ -1,0 +1,452 @@
+from concourse.mybir import AluOpType, AxisListType, ActivationFunctionType
+
+OP = AluOpType
+AF = ActivationFunctionType
+W, K = 4096, 256
+
+_S = {}
+
+
+def _sb(name, cols, dtype="bfloat16"):
+    _S[name] = ("sbuf", [128, cols], dtype)
+
+
+_sb("LX", W + K)
+_sb("LM", W + K)
+for _n in ("X0", "M0", "X1", "M1", "X2", "M2", "X3", "M3", "XN0", "XN1", "XN2", "MN0", "MN1", "MN2"):
+    _sb(_n, K)
+for _n in ("MG", "MI"):
+    _sb(_n, 128, "float32")
+_sb("PI", 4, "int32")
+_sb("PF", 8, "float32")
+_sb("THR", 4, "float32")
+_sb("SQB", 1, "float32")
+_sb("WI", 2, "int32")
+_sb("WF", 2, "float32")
+_sb("THI", 1, "int32")
+_sb("THF", 1, "float32")
+_CB = ("BO", "BO64", "BO8192", "ID", "IDN", "ID2", "IDN128", "ID128", "ID64", "ID8192", "SL", "MNE", "BOX", "W1", "W2",
+       "BASE", "C2", "LT0", "LT1", "LT2", "BN8")
+for _n in _CB:
+    _sb(_n, 128)
+for _n in ("BOH", "IDH", "THB"):
+    _sb(_n, 128, "float16")
+_sb("SK", 2048)
+_sb("RXI", 512, "float32")
+_sb("RX", 512)
+_sb("IO64", 64)
+_S["TRI"] = ("sbuf", [128, 16, 16], "bfloat16")
+_S["TRII"] = ("sbuf", [128, 256], "float32")
+_sb("IDX0", 16, "float32")
+_sb("IDX2", 16, "float32")
+_sb("QB", 144)
+_sb("Q512", 144)
+_sb("QH", 144, "float16")
+_sb("Q16", 144, "float16")
+_sb("UI", 512, "int32")
+_sb("PR", 256, "int32")
+_sb("HQ", 256, "int32")
+_sb("HI", 256, "int32")
+_sb("HU", 256, "uint16")
+_sb("H16", 256, "float16")
+_sb("CB", 4096)
+_sb("EB", 4096)
+_sb("PB", 256)
+_sb("FB", 256, "float16")
+_sb("FH", 256, "float16")
+_sb("FX", 256)
+_sb("FC", 256)
+_sb("NH", 256)
+_sb("XA", 256)
+_sb("LF", 16, "uint16")
+_sb("SUB", 256)
+_sb("ABS", 256)
+_sb("XTS", 16, "float32")
+_sb("CTS", 16, "float32")
+_sb("NTS", 16, "float32")
+_sb("OHX", 1024)
+_sb("OHC", 1024)
+_sb("XL", 16, "int32")
+_sb("XLF", 16, "float32")
+_sb("CLF", 16, "float32")
+_sb("CL", 16, "uint16")
+_sb("SQ", 256)
+_sb("MK", 256)
+_sb("TB", 64)
+_sb("TW", 256)
+_sb("HN", 256)
+_sb("GT", 256)
+_sb("DMI", 256, "int32")
+_sb("DM", 256)
+_sb("MGR", 256)
+_sb("DT", 256)
+_sb("DK", 256, "float16")
+_sb("KLS", 16, "float32")
+_S["EQ"] = ("sbuf", [128, 16, 256], "bfloat16")
+_sb("LS", 256)
+_sb("OFF", 16, "float32")
+_sb("OFU", 16, "uint16")
+_sb("SUM", 4, "float32")
+_sb("YM", 1, "float32")
+for _i in range(8):
+    _S["B%d" % _i] = ("psum", [128, 512], "float32")
+SCRATCH = _S
+SEMAPHORES = (["qv", "qs", "qt", "qg", "ls"] + ["d%d" % _i for _i in range(12)]
+              + ["ax%d" % _i for _i in range(1, 4)] + ["am%d" % _i for _i in range(1, 4)])
+
+
+def rank_program(g, core, T, topo):
+    rank = T.rank_of(core)
+    if rank is None:
+        return
+    n_ranks = len(T.cores)
+    que = {"v": g.vector, "s": g.scalar, "t": g.tensor, "g": g, "y": g.sync}
+    clock = {q: {} for q in que}
+    count = {"qv": 0, "qs": 0, "qt": 0, "qg": 0}
+    lastw, readers, touch = {}, {}, {}
+    dmas = []
+
+    def wait(q, tok):
+        sem, n, snap = tok[0], tok[1], tok[2]
+        if clock[q].get(sem, 0) >= n:
+            return
+        que[q].wait_ge(T.sem[sem], n)
+        for s, m in snap.items():
+            if clock[q].get(s, 0) < m:
+                clock[q][s] = m
+        clock[q][sem] = n
+
+    def before(q, reads, writes, dma=False):
+        toks = {}
+
+        def need(tok):
+            if tok[0] not in toks or toks[tok[0]][1] < tok[1]:
+                toks[tok[0]] = tok
+        for k in reads:
+            if k in lastw:
+                need(lastw[k])
+        for k in writes:
+            if k in lastw and (dma or lastw[k][3] != q):
+                need(lastw[k])
+            for tok in readers.get(k, {}).values():
+                if dma or tok[3] != q:
+                    need(tok)
+        for k in list(reads) + list(writes):
+            for e, tok in touch.get(k, {}).items():
+                if e != q:
+                    need(tok)
+        for tok in toks.values():
+            wait(q, tok)
+
+    def after(tok, reads, writes):
+        for k in writes:
+            lastw[k] = tok
+            readers[k] = {}
+        for k in reads:
+            if k not in writes:
+                readers.setdefault(k, {})[tok[0]] = tok
+        for k in list(reads) + list(writes):
+            if k in BANKS:
+                touch.setdefault(k, {})[tok[3]] = tok
+
+    BANKS = ["B%d" % i for i in range(8)]
+
+    def do(q, reads, writes, name, **kw):
+        before(q, reads, writes)
+        sem = "q" + q
+        count[sem] += 1
+        ins = None
+        if name == "copy":
+            ins = g.vector.tensor_copy(**kw)
+        elif name == "tt":
+            ins = g.vector.tensor_tensor(**kw)
+        elif name == "ts":
+            ins = g.vector.tensor_scalar(**kw)
+        elif name == "act":
+            ins = g.scalar.activation(**kw)
+        elif name == "mm":
+            ins = g.tensor.matmul(kw["out"], kw["l"], kw["r"], kw["start"], kw["stop"])
+        elif name == "fill":
+            ins = g.vector.memset(kw["ap"], kw["c"])
+        elif name == "iota":
+            ins = g.iota(**kw)
+        elif name == "reduce":
+            ins = g.vector.tensor_reduce(**kw)
+        ins.then_inc(T.sem[sem], 1)
+        after((sem, count[sem], dict(clock[q]), q), reads, writes)
+
+    def dma(q, out, in_, reads, writes):
+        before(q, reads, writes, True)
+        sem = "d%d" % len(dmas)
+        que[q].dma_start(out, in_).then_inc(T.sem[sem], 16)
+        tok = (sem, 16, dict(clock[q]), "dma")
+        dmas.append(tok)
+        after(tok, reads, writes)
+
+    def cp(out, in_, r, w):
+        do("v", r, w, "copy", out=out, in_=in_)
+
+    def tt(out, a, b, op, r, w):
+        do("v", r, w, "tt", out=out, in0=a, in1=b, op=op)
+
+    def ts(out, a, s1, op0, r, w, s2=None, op1=None):
+        if op1 is None:
+            do("v", r, w, "ts", out=out, in0=a, scalar1=s1, scalar2=None, op0=op0)
+        else:
+            do("v", r, w, "ts", out=out, in0=a, scalar1=s1, scalar2=s2, op0=op0, op1=op1)
+
+    def act(out, in_, r, w, func=AF.Copy, **kw):
+        do("s", r, w, "act", out=out, in_=in_, func=func, **kw)
+
+    def mm(out, l, r, start, stop, rd, wr):
+        do("t", rd, wr, "mm", out=out, l=l, r=r, start=start, stop=stop)
+
+    def iota(out, pattern, base, cm, w, small=True):
+        if small:
+            do("g", [], w, "iota", out=out, pattern=pattern, base=base, channel_multiplier=cm,
+               allow_small_or_imprecise_dtypes=True)
+        else:
+            do("g", [], w, "iota", out=out, pattern=pattern, base=base, channel_multiplier=cm)
+
+    dma("y", T.X0[:], T.xw[:], [], ["X0"])
+    dma("s", T.WI[:], T.wts[:], [], ["WI"])
+    dma("y", T.LX[:, 0:W], T.lex[:], [], ["LX"])
+    dma("s", T.THI[:], T.th[:], [], ["THI"])
+    dma("y", T.M0[:], T.gw[:], [], ["M0"])
+    dma("y", T.LM[:, 0:W], T.mng[:], [], ["LM"])
+
+    iota(T.PI[:, 0:1], [[0, 1]], 0, 1, ["PI"], False)
+    iota(T.MG[:], [[1, 8], [0, 16]], 0, 0, ["MG"])
+    iota(T.MI[:], [[1, 128]], 0, 0, ["MI"])
+    iota(T.IO64[:], [[1, 64]], 0, 0, ["IO64"])
+    iota(T.IDX0[:], [[16, 16]], 2048, 0, ["IDX0"])
+    iota(T.TRII[:], [[0, 16], [1, 16]], 0, 0, ["TRII"])
+    iota(T.RXI[:], [[1, 4], [0, 8], [4, 16]], 0, 0, ["RXI"])
+    do("v", [], ["SK"], "fill", ap=T.SK[:], c=0.0)
+    for nm in ("QB", "Q512"):
+        do("v", [], [nm], "fill", ap=T[nm][:], c=0.0)
+    ts(T.PI[:, 1:2], T.PI[:, 0:1], 4, OP.arith_shift_right, ["PI"], ["PI1"])
+    ts(T.PI[:, 2:3], T.PI[:, 0:1], 15, OP.bitwise_and, ["PI"], ["PI2"])
+    cp(T.PF[:, 0:3], T.PI[:, 0:3], ["PI", "PI1", "PI2"], ["PF"])
+    pI, pG, pL = T.PF[:, 0:1], T.PF[:, 1:2], T.PF[:, 2:3]
+    ts(T.BO[:], T.MG[:], pG, OP.is_equal, ["MG", "PF"], ["BO"])
+    ts(T.ID[:], T.MI[:], pI, OP.is_equal, ["MI", "PF"], ["ID"])
+    cp(T.WF[:], T.WI[:], ["WI"], ["WF"])
+    tt(T.MNE[:], T.BO[:], T.ID[:], OP.subtract, ["BO", "ID"], ["MNE"])
+    ts(T.W1[:], T.MNE[:], T.WF[:, 0:1], OP.mult, ["MNE", "WF"], ["W1"])
+    ts(T.W2[:], T.MNE[:], T.WF[:, 1:2], OP.mult, ["MNE", "WF"], ["W2"])
+    act(T.IDH[:], T.ID[:], ["ID"], ["IDH"])
+    act(T.BOH[:], T.BO[:], ["BO"], ["BOH"])
+    for nm, src, f in (("IDN", "ID", -1.0), ("ID2", "ID", 2.0), ("IDN128", "ID", -128.0), ("ID128", "ID", 128.0),
+                       ("ID64", "ID", 64.0), ("ID8192", "ID", 8192.0), ("BO64", "BO", 64.0), ("BO8192", "BO", 8192.0),
+                       ("BN8", "BO", -8.0)):
+        act(T[nm][:], T[src][:], [src], [nm], scale=f)
+
+    def later_constants():
+        ts(T.C2[:], T.ID[:], 16.0, OP.mult, ["ID"], ["C2"])
+        tt(T.BOX[:], T.BO[:], T.C2[:], OP.subtract, ["BO", "C2"], ["BOX"])
+        for e in range(8):
+            cp(T.SK[:, 16 * e:16 * e + 129 * 15 + 1:129], T.BOX[:, 16 * e:16 * e + 16], ["BOX"], ["SK"])
+        ts(T.SL[:], T.MI[:], pI, OP.is_gt, ["MI", "PF"], ["SL"])
+        tt(T.SL[:], T.SL[:], T.BO[:], OP.mult, ["SL", "BO"], ["SL"])
+        tt(T.BASE[:], T.SL[:], T.ID[:], OP.subtract, ["SL", "ID"], ["BASE"])
+        ts(T.C2[:], T.SL[:], 31.0, OP.mult, ["SL"], ["C2"])
+        tt(T.C2[:], T.C2[:], T.BO[:], OP.add, ["C2", "BO"], ["C2"])
+        ts(T.LT1[:], T.ID[:], 17.0, OP.mult, ["ID"], ["LT1"])
+        tt(T.C2[:], T.C2[:], T.LT1[:], OP.subtract, ["C2", "LT1"], ["C2"])
+        for t in range(3):
+            nm = "LT%d" % t
+            cp(T[nm][:], T.BASE[:], ["BASE", "C2"], [nm])
+            cp(T[nm][:, t::16], T.C2[:, t::16], ["C2", nm], [nm])
+            ts(T.THR[:, t:t + 1], pL, float(t), OP.not_equal, ["PF"], ["THR"], -0.5, OP.mult)
+        cp(T.QB[:, 15:128:16], T.BO[:, ::16], ["BO"], ["QB"])
+        ts(T.Q512[:, 15:128:16], T.BO[:, ::16], 512.0, OP.mult, ["BO"], ["Q512"])
+        cp(T.QH[:], T.QB[:], ["QB"], ["QH"])
+        ts(T.Q16[:], T.QB[:], 0.0625, OP.mult, ["QB"], ["Q16"])
+        ts(T.THF[:], T.THI[:], -1.0, OP.mult, ["THI"], ["THF"], 2048.0, OP.add)
+        ts(T.THB[:], T.BO[:], T.THF[:], OP.mult, ["BO", "THF"], ["THB"])
+        ts(T.SQB[:], pL, -4.0, OP.mult, ["PF"], ["SQB"], -1.5, OP.add)
+        ts(T.IDX2[:], T.IDX0[:], pL, OP.add, ["IDX0", "PF"], ["IDX2"])
+        ts(T.RX[:], T.RXI[:], pI, OP.is_equal, ["RXI", "PF"], ["RX"])
+        for c in range(16):
+            ts(T.TRI[:, c, :], T.TRII[:, 16 * c:16 * c + 16], pL, OP.is_gt, ["TRII", "PF"], ["TRI"])
+
+    def qwin(name, p):
+        return T[name][:, 15 - p:143 - p]
+
+    deferred = []
+    for t in range(3):
+        xn, mn = "XN%d" % t, "MN%d" % t
+        X, M = "X%d" % t, "M%d" % t
+        TX, TM = T[X], T[M]
+        for h in range(2):
+            for j, w in ((0, "W1"), (1, "W2")):
+                mm(T.B0[:, 256 * h + 128 * j:256 * h + 128 * j + 128], T[w][:], TX[:, 128 * h:128 * h + 128], True, True,
+                   [w, X], ["B0"])
+        mm(T.B1[:, 0:256], T.ID[:], TX[:], True, True, ["ID", X], ["B1"])
+
+        def hashes(h):
+            a, b = 256 * h, 128 * h
+            ui, pr, hq, hi = ("UI", h), ("PR", h), ("HQ", h), ("HI", h)
+            cp(T.UI[:, a:a + 256], T.B0[:, a:a + 256], ["B0"], [ui])
+            ts(T.UI[:, a:a + 256], T.UI[:, a:a + 256], 4095, OP.bitwise_and, [ui], [ui])
+            tt(T.PR[:, b:b + 128], T.UI[:, a:a + 128], T.UI[:, a + 128:a + 256], OP.mult, [ui], [pr])
+            ts(T.HQ[:, b:b + 128], T.PR[:, b:b + 128], 5, OP.arith_shift_right, [pr], [hq])
+            tt(T.HQ[:, b:b + 128], T.HQ[:, b:b + 128], T.B0[:, a:a + 128], OP.add, [hq, "B0"], [hq])
+            ts(T.HI[:, b:b + 128], T.HQ[:, b:b + 128], 4095, OP.bitwise_and, [hq], [hi])
+            cp(T.HU[:, b:b + 128], T.HI[:, b:b + 128], [hi], [("HU", h)])
+
+        def sgather(w0, w1, key):
+            act(T.CB[:, 16 * w0:16 * w1], T.LX[:, 0:W].indirect(T.HU[:, w0:w1]), ["LX", ("HU", w0 // 128)], [key])
+
+        hashes(0)
+        sgather(0, 64, ("CB", 0))
+        sgather(64, 128, ("CB", 1))
+        hashes(1)
+        sgather(128, 192, ("CB", 2))
+        sgather(192, 224, ("CB", 3))
+        if t == 0:
+            later_constants()
+        cp(T.CB[:, 3584:4096], T.LX[:, 0:W].indirect(T.HU[:, 224:256]), ["LX", ("HU", 1)], [("CB", 4)])
+        for f in deferred:
+            f()
+        deferred = []
+        ts(T.H16[:], T.HI[:], -2048.0, OP.add, [("HI", 0), ("HI", 1)], ["H16"])
+        mm(T.B7[:, 256:512], T.IDH[:], T.H16[:], True, True, ["IDH", "H16"], ["B7"])
+        for c in range(4):
+            for k in range(16):
+                o = 1024 * c
+                tt(T.EB[:, o + 64 * k:o + 64 * k + 64], T.CB[:, o + k:o + 1024:16], T.B1[:, 64 * c:64 * c + 64], OP.not_equal,
+                   [("CB", c), "B1"] + ([("CB", 4)] if c == 3 else []), [("EB", c, k // 4)])
+            for k in range(16):
+                mm(T.B2[:, 64 * c:64 * c + 64], T.SK[:, 128 * k:128 * k + 128], T.EB[:, 1024 * c + 64 * k:1024 * c + 64 * k + 64],
+                   k == 0, k == 15, ["SK", ("EB", c, k // 4)], ["B2"])
+        ts(T.PB[:], T.B2[:, 0:256], -11.5, OP.is_le, ["B2"], ["PB"])
+        lt = "LT%d" % t
+        mm(T.B2[:, 256:512], T[lt][:], T.PB[:], True, True, [lt, "PB"], ["B2"])
+        mm(T.B3[:, 256:512], T.BO[:], T.PB[:], True, True, ["BO", "PB"], ["B3"])
+        ts(T.FB[:], T.B2[:, 256:512], T.THR[:, t:t + 1], OP.is_le, ["B2", "THR"], ["FB"])
+        tt(T.FH[:], T.FB[:], T.B7[:, 256:512], OP.mult, ["FB", "B7"], ["FH"])
+        for p in range(16):
+            mm(T.B4[:, 0:16], qwin("QH", p), T.FH[:, p::16], p == 0, p == 15, ["QH", "FH"], ["B4"])
+        tt(T.FX[:], T.FB[:], T.B1[:, 0:256], OP.mult, ["FB", "B1"], ["FX"])
+        ts(T.NH[:], T.B3[:, 256:512], 0.5, OP.is_le, ["B3"], ["NH"], 64.0, OP.mult)
+        tt(T.XA[:], T.NH[:], T.B1[:, 0:256], OP.add, ["NH", "B1"], ["XA"])
+        for h in range(2):
+            mm(T.B2[:, 8 * h:8 * h + 8], T.FX[:, 128 * h:128 * h + 128], T.BO[:, ::16], True, True, ["FX", "BO"], ["B2"])
+        for p in range(16):
+            mm(T.B2[:, 16:32], qwin("QB", p), T.FX[:, p::16], p == 0, p == 15, ["QB", "FX"], ["B2"])
+        mm(T.B3[:, 256:512], T.BO[:], T.FX[:], True, False, ["BO", "FX"], ["B3"])
+        mm(T.B3[:, 256:512], T.ID2[:], T.NH[:], False, True, ["ID2", "NH"], ["B3"])
+        mm(T.B7[:, 0:256], T.BOH[:], T.FH[:], True, False, ["BOH", "FH"], ["B7"])
+        mm(T.B7[:, 0:256], T.ID128[:], T.NH[:], False, False, ["ID128", "NH"], ["B7"])
+        ts(T.LF[:], T.B4[:, 0:16], 2048.0, OP.add, ["B4"], ["LF"])
+        tt(T.SUB[:], T.LM[:, 0:W].indirect(T.LF[:, 0:16]), TM[:], OP.subtract, ["LM", "LF", M], ["SUB"])
+        act(T.ABS[:], T.SUB[:], ["SUB"], ["ABS"], func=AF.Abs)
+        tt(T.FC[:], T.LX[:, 0:W].indirect(T.LF[:, 0:16]), T.FB[:], OP.mult, ["LX", "LF", "FB"], ["FC"])
+        act(T.SQ[:], T.B3[:, 256:512], ["B3", "SQB"], ["SQ"], func=AF.Square, bias=T.SQB[:])
+        for h in range(2):
+            s = slice(128 * h, 128 * h + 128)
+            o = T.B4[:, 32 + 8 * h:40 + 8 * h]
+            mm(o, T.FB[:, s], T.THB[:, ::16], True, False, ["FB", "THB"], ["B4"])
+            mm(o, T.NH[:, s], T.BN8[:, ::16], False, False, ["NH", "BN8"], ["B4"])
+            mm(o, T.ABS[:, s], T.BO[:, ::16], False, True, ["ABS", "BO"], ["B4"])
+        for h in range(2):
+            mm(T.B4[:, 16 + 8 * h:24 + 8 * h], T.FC[:, 128 * h:128 * h + 128], T.BO[:, ::16], True, True, ["FC", "BO"], ["B4"])
+        cp(T.XTS[:], T.B2[:, 0:16], ["B2"], ["XTS"])
+        cp(T.XL[:], T.B2[:, 16:32], ["B2"], ["XL"])
+        for c in range(16):
+            ts(T.OHX[:, 64 * c:64 * c + 64], T.IO64[:], T.XTS[:, c:c + 1], OP.is_equal, ["IO64", "XTS"], [("OHX", c // 4)])
+        for p in range(16):
+            mm(T.B2[:, 32:48], qwin("QB", p), T.FC[:, p::16], p == 0, p == 15, ["QB", "FC"], ["B2"])
+        cp(T.CTS[:], T.B4[:, 16:32], ["B4"], ["CTS"])
+        ts(T.NTS[:], T.B4[:, 32:48], 2047.5, OP.is_ge, ["B4"], ["NTS"])
+        for c in range(16):
+            s = slice(64 * c, 64 * c + 64)
+            ts(T.OHC[:, s], T.IO64[:], T.CTS[:, c:c + 1], OP.is_equal, ["IO64", "CTS", "NTS"], [("OHC", c // 2)],
+               T.NTS[:, c:c + 1], OP.mult)
+            if c % 2 == 1:
+                for d in (c - 1, c):
+                    s = slice(64 * d, 64 * d + 64)
+                    rd = [("OHX", d // 4), ("OHC", d // 2)]
+                    mm(T.B5[0:64, 0:64], T.OHX[:, s], T.OHC[:, s], d == 0, False, rd, ["B5"])
+                    mm(T.B5[0:64, 0:64], T.OHC[:, s], T.OHX[:, s], False, d == 15, rd, ["B5"])
+        mm(T.B3[:, 0:256], T.THB[:], T.FB[:], True, False, ["THB", "FB"], ["B3"])
+        mm(T.B3[:, 0:256], T.IDN128[:], T.NH[:], False, False, ["IDN128", "NH"], ["B3"])
+        mm(T.B3[:, 0:256], T.BO[:], T.ABS[:], False, True, ["BO", "ABS"], ["B3"])
+        ts(T.XL[:], T.XL[:], 3, OP.bitwise_and, ["XL"], ["XL"])
+        ts(T.MK[:], T.SQ[:], 4.0, OP.is_le, ["SQ"], ["MK"])
+        ts(T.XLF[:], T.XL[:], 64.0, OP.mult, ["XL"], ["XLF"])
+        tt(T.CLF[:], T.XLF[:], T.B2[:, 32:48], OP.add, ["XLF", "B2"], ["CLF"])
+        cp(T.CL[:], T.CLF[:], ["CLF"], ["CL"])
+        ts(T.TB[0:64, :], T.B5[0:64, 0:64], 1.0, OP.min, ["B5"], ["TB"])
+        for r in range(4):
+            mm(T.B5[:, 256 + 64 * r:320 + 64 * r], T.RX[0:64, 128 * r:128 * r + 128], T.TB[0:64, :], True, True, ["RX", "TB"], ["B5"])
+        act(T.TW[:], T.B5[:, 256:512], ["B5"], ["TW"])
+        ts(T.HN[:], T.B3[:, 0:256], 2047.5, OP.is_ge, ["B3"], ["HN"])
+        mm(T.B6[:, 0:256], T.ID[:], TX[:], True, False, ["ID", X], ["B6"])
+        mm(T.B6[:, 0:256], T.IDN[:], T.FX[:], False, False, ["IDN", "FX"], ["B6"])
+        mm(T.B6[:, 0:256], T.ID[:], T.FC[:], False, False, ["ID", "FC"], ["B6"])
+        mm(T.B6[:, 0:256], T.ID64[:], T.HN[:], False, False, ["ID64", "HN"], ["B6"])
+        mm(T.B7[:, 0:256], T.ID8192[:], T.HN[:], False, False, ["ID8192", "HN"], ["B7"])
+        tt(T.GT[:], T.TW[:].indirect(T.CL[:, 0:16]), T.MK[:], OP.mult, ["TW", "CL", "MK"], ["GT"])
+        mm(T.B6[:, 0:256], T.BO64[:], T.GT[:], False, True, ["BO64", "GT"], ["B6"])
+        mm(T.B7[:, 0:256], T.BO8192[:], T.GT[:], False, True, ["BO8192", "GT"], ["B7"])
+        tt(T[xn][:], T.XA[:], T.B6[:, 0:256], OP.min, ["XA", "B6"], [xn])
+        dst = T.cores[(rank + (3 if t < 2 else 2)) % n_ranks]
+        rid, pid, _eng = topo.addr(dst)
+        mask = topo.mask(core, dst)
+        ne = len(topo.engines(core, dst))
+
+        def send(out, src, sem):
+            before("g", [src], [])
+            g.remote_dma(T[out][:], T[src][:], T.sem[sem], T.sem.ls, pid, rid, mask)
+            lastw[out] = (sem, ne, {}, "remote")
+        send("X%d" % (t + 1), xn, "ax%d" % (t + 1))
+        ts(T.DK[:], T.B7[:, 0:256], 6144.0, OP.min, ["B7"], ["DK"])
+        for p in range(16):
+            mm(T.B4[:, 48:64], qwin("Q16", p), T.DK[:, p::16], p == 0, p == 15, ["Q16", "DK"], ["B4"])
+        ts(T.MGR[:], T.B7[:, 0:256], 4000.0, OP.is_lt, ["B7"], ["MGR"])
+        ts(T.DMI[:], T.SUB[:], 0.5, OP.mult, ["SUB"], ["DMI"], -0.25, OP.add)
+        tt(T.DT[:], T.MGR[:], T.DMI[:], OP.mult, ["MGR", "DMI"], ["DT"])
+        mm(T.B0[:, 0:256], T.ID[:], TM[:], True, False, ["ID", M], ["B0"])
+        mm(T.B0[:, 0:256], T.ID[:], T.DT[:], False, True, ["ID", "DT"], ["B0"])
+        act(T[mn][:], T.B0[:, 0:256], ["B0"], [mn])
+        send("M%d" % (t + 1), mn, "am%d" % (t + 1))
+        for p in range(16):
+            mm(T.B5[:, 0:16], qwin("Q16", p), T.DK[:, p::16], p == 0, False, ["Q16", "DK"], ["B5"])
+        cp(T.KLS[:], T.B4[:, 48:64], ["B4"], ["KLS"])
+        for c in range(16):
+            ts(T.EQ[:, c, 0:256 - 16 * c], T.DK[:, 16 * c:256], T.KLS[:, c:c + 1], OP.is_equal, ["DK", "KLS"], ["EQ"])
+        tt(T.EQ[:, :, 0:16], T.EQ[:, :, 0:16], T.TRI[:], OP.mult, ["EQ", "TRI"], ["EQ"])
+        for c in range(16):
+            mm(T.B2[:, 16 * c:256], T.BO[:], T.EQ[:, c, 0:256 - 16 * c], c == 0, c == 15, ["BO", "EQ"], ["B2"])
+        ts(T.LS[:], T.B2[:, 0:256], 0.5, OP.is_ge, ["B2"], ["LS"])
+        for p in range(16):
+            mm(T.B5[:, 0:16], qwin("Q512", p), T.LS[:, p::16], False, p == 15, ["Q512", "LS"], ["B5"])
+        tt(T.OFF[:], T.B5[:, 0:16], T.IDX2[:], OP.min, ["B5", "IDX2"], ["OFF"])
+        ts(T.OFU[:], T.OFF[:], 2048.0, OP.add, ["OFF"], ["OFU"])
+        cp(T.LX[:].indirect(T.OFU[:, 0:16]), T[xn][:], ["OFU", xn, "LX"], ["LX"])
+
+        def scatter_meanings(mn=mn):
+            cp(T.LM[:].indirect(T.OFU[:, 0:16]), T[mn][:], ["OFU", mn, "LM"], ["LM"])
+        deferred = [scatter_meanings]
+
+    dma("s", T.yl[:], T.LX[:, 0:W], ["LX"], ["yl"])
+    for f in deferred:
+        f()
+    act(T.CB[:, 0:1792], T.LM[:, 2304:4096], ["LM"], [("CB", 0), ("CB", 1)], accum_out=T.SUM[:, 1:2])
+    lastw["SUM1"] = lastw[("CB", 0)]
+    do("v", ["LM"], ["SUM0"], "reduce", out=T.SUM[:, 0:1], in_=T.LM[:, 0:2304], axis=AxisListType.X, op=OP.add)
+    tt(T.YM[:], T.SUM[:, 0:1], T.SUM[:, 1:2], OP.add, ["SUM0", "SUM1"], ["YM"])
+    dma("y", T.yx[:], T.X3[:], ["X3"], ["yx"])
+    dma("y", T.yg[:], T.M3[:], ["M3"], ["yg"])
+    dma("y", T.ym[:], T.YM[:], ["YM"], ["ym"])
+    for sem in ("qv", "qs", "qt", "qg"):
+        wait("g", (sem, count[sem], {}, ""))
+    for tok in dmas:
+        wait("g", tok)
+    for s in range(1, 4):
+        wait("g", ("ax%d" % s, ne, {}, ""))
+        wait("g", ("am%d" % s, ne, {}, ""))
+    g.wait_ge(T.sem.ls, 6 * ne)

@@ -11,41 +11,38 @@ def _sb(name, cols, dtype="bfloat16"):
     _S[name] = ("sbuf", [128, cols], dtype)
 
 
-_sb("LX", W + K)
-_sb("LM", W + K)
+_sb("LX", W + 32)
+_sb("LM", W + 32)
 for _n in ("X0", "M0", "X1", "M1", "X2", "M2", "X3", "M3", "XN0", "XN1", "XN2", "MN0", "MN1", "MN2"):
     _sb(_n, K)
-for _n in ("MG", "MI"):
+for _n in ("MG", "MP"):
     _sb(_n, 128, "float32")
 _sb("PI", 4, "int32")
-_sb("PF", 8, "float32")
-_sb("THR", 4, "float32")
-_sb("SQB", 1, "float32")
+_sb("PF", 16, "float32")
+for _n in ("THR", "T3", "VA", "VB", "PC", "PD"):
+    _sb(_n, 4, "float32")
 _sb("WI", 2, "int32")
 _sb("WF", 2, "float32")
 _sb("THI", 1, "int32")
 _sb("THF", 1, "float32")
-_CB = ("BO", "BO64", "BO8192", "ID", "IDN", "ID2", "IDN128", "ID128", "ID64", "ID8192", "SL", "MNE", "BOX", "W1", "W2",
-       "BASE", "C2", "LT0", "LT1", "LT2", "BN8")
-for _n in _CB:
+for _n in ("BO", "BO64", "BO8192", "ID", "IDN", "ID128", "SL", "MNE", "BOX", "W1", "W2", "W32", "LT0", "LT1", "LT2", "CN"):
     _sb(_n, 128)
-for _n in ("BOH", "IDH", "THB"):
-    _sb(_n, 128, "float16")
+_sb("ONES", 512)
+for _n in ("THB", "B15", "BNA"):
+    _sb(_n, 8, "float16")
+for _n in range(4):
+    _sb("PM%d" % _n, 128, "float16")
+    _sb("PN%d" % _n, 128, "float16")
 _sb("SK", 2048)
-_sb("RXI", 512, "float32")
 _sb("RX", 512)
 _sb("IO64", 64)
-_S["TRI"] = ("sbuf", [128, 16, 16], "bfloat16")
-_S["TRII"] = ("sbuf", [128, 256], "float32")
-_sb("IDX0", 16, "float32")
-_sb("IDX2", 16, "float32")
-_sb("QB", 144)
-_sb("Q512", 144)
-_sb("QH", 144, "float16")
-_sb("Q16", 144, "float16")
+for _n in ("JI", "RA", "RB", "RC"):
+    _sb(_n, 32, "float32")
+for _n in ("RR", "EQ", "SC"):
+    _sb(_n, 512)
 _sb("UI", 512, "int32")
 _sb("PR", 256, "int32")
-_sb("HQ", 256, "int32")
+_sb("ZI", 256, "int32")
 _sb("HI", 256, "int32")
 _sb("HU", 256, "uint16")
 _sb("H16", 256, "float16")
@@ -53,43 +50,36 @@ _sb("CB", 4096)
 _sb("EB", 4096)
 _sb("PB", 256)
 _sb("FB", 256, "float16")
-_sb("FH", 256, "float16")
-_sb("FX", 256)
-_sb("FC", 256)
+_S["FH"] = ("sbuf", [128, 8, 32], "float16")
+_sb("FX", 256, "float16")
+_sb("FC", 256, "float16")
 _sb("NH", 256)
 _sb("XA", 256)
+_S["KB"] = ("sbuf", [128, 8, 32], "float32")
+_sb("KC", 256, "float32")
+_sb("KL", 16, "float32")
 _sb("LF", 16, "uint16")
 _sb("SUB", 256)
 _sb("ABS", 256)
-_sb("XTS", 16, "float32")
-_sb("CTS", 16, "float32")
-_sb("NTS", 16, "float32")
 _sb("OHX", 1024)
 _sb("OHC", 1024)
-_sb("XL", 16, "int32")
-_sb("XLF", 16, "float32")
-_sb("CLF", 16, "float32")
+_sb("CI", 16, "int32")
 _sb("CL", 16, "uint16")
-_sb("SQ", 256)
+_sb("AQ", 256)
 _sb("MK", 256)
 _sb("TB", 64)
 _sb("TW", 256)
-_sb("HN", 256)
 _sb("GT", 256)
-_sb("DMI", 256, "int32")
+_sb("D16", 256, "float16")
 _sb("DM", 256)
-_sb("MGR", 256)
-_sb("DT", 256)
-_sb("DK", 256, "float16")
-_sb("KLS", 16, "float32")
-_S["EQ"] = ("sbuf", [128, 16, 256], "bfloat16")
-_sb("LS", 256)
-_sb("OFF", 16, "float32")
+_sb("GD", 256)
+_sb("Z", 16, "float32")
+_sb("Y", 16, "float32")
 _sb("OFU", 16, "uint16")
 _sb("SUM", 4, "float32")
 _sb("YM", 1, "float32")
 for _i in range(8):
-    _S["B%d" % _i] = ("psum", [128, 512], "float32")
+    _S["B%d" % _i] = ("psum", [128, 16, 32] if _i in (0, 4) else [128, 512], "float32")
 SCRATCH = _S
 SEMAPHORES = (["qv", "qs", "qt", "qg", "ls"] + ["d%d" % _i for _i in range(12)]
               + ["ax%d" % _i for _i in range(1, 4)] + ["am%d" % _i for _i in range(1, 4)])
@@ -116,6 +106,10 @@ def rank_program(g, core, T, topo):
                 clock[q][s] = m
         clock[q][sem] = n
 
+    def bank(k):
+        b = k[0] if isinstance(k, tuple) else k
+        return b if b in BANKS else None
+
     def before(q, reads, writes, dma=False):
         toks = {}
 
@@ -132,7 +126,7 @@ def rank_program(g, core, T, topo):
                 if dma or tok[3] != q:
                     need(tok)
         for k in list(reads) + list(writes):
-            for e, tok in touch.get(k, {}).items():
+            for e, tok in touch.get(bank(k), {}).items():
                 if e != q:
                     need(tok)
         for tok in toks.values():
@@ -146,8 +140,8 @@ def rank_program(g, core, T, topo):
             if k not in writes:
                 readers.setdefault(k, {})[tok[0]] = tok
         for k in list(reads) + list(writes):
-            if k in BANKS:
-                touch.setdefault(k, {})[tok[3]] = tok
+            if bank(k):
+                touch.setdefault(bank(k), {})[tok[3]] = tok
 
     BANKS = ["B%d" % i for i in range(8)]
 
@@ -170,8 +164,16 @@ def rank_program(g, core, T, topo):
             ins = g.vector.memset(kw["ap"], kw["c"])
         elif name == "iota":
             ins = g.iota(**kw)
+        elif name == "pick":
+            ins = g.affine_select(**kw)
         elif name == "reduce":
             ins = g.vector.tensor_reduce(**kw)
+        elif name == "turn":
+            ins = g.vector.transpose(**kw)
+        elif name == "inverse":
+            ins = g.vector.reciprocal(**kw)
+        elif name == "scan":
+            ins = g.vector.tensor_tensor_scan(**kw)
         ins.then_inc(T.sem[sem], 1)
         after((sem, count[sem], dict(clock[q]), q), reads, writes)
 
@@ -195,6 +197,12 @@ def rank_program(g, core, T, topo):
         else:
             do("v", r, w, "ts", out=out, in0=a, scalar1=s1, scalar2=s2, op0=op0, op1=op1)
 
+    def tr(out, in_, r, w):
+        do("v", r, w, "turn", out=out, in_=in_)
+
+    def fill(ap, c, w):
+        do("v", [], w, "fill", ap=ap, c=c)
+
     def act(out, in_, r, w, func=AF.Copy, **kw):
         do("s", r, w, "act", out=out, in_=in_, func=func, **kw)
 
@@ -208,6 +216,9 @@ def rank_program(g, core, T, topo):
         else:
             do("g", [], w, "iota", out=out, pattern=pattern, base=base, channel_multiplier=cm)
 
+    def pick(out, in_, pattern, op, other, r, w):
+        do("g", r, w, "pick", out=out, in_=in_, pattern=pattern, compare_op=op, fill=other, base=0, channel_multiplier=-1)
+
     dma("y", T.X0[:], T.xw[:], [], ["X0"])
     dma("s", T.WI[:], T.wts[:], [], ["WI"])
     dma("y", T.LX[:, 0:W], T.lex[:], [], ["LX"])
@@ -215,184 +226,225 @@ def rank_program(g, core, T, topo):
     dma("y", T.M0[:], T.gw[:], [], ["M0"])
     dma("y", T.LM[:, 0:W], T.mng[:], [], ["LM"])
 
+    col = [[1, 128]]
     iota(T.PI[:, 0:1], [[0, 1]], 0, 1, ["PI"], False)
     iota(T.MG[:], [[1, 8], [0, 16]], 0, 0, ["MG"])
-    iota(T.MI[:], [[1, 128]], 0, 0, ["MI"])
-    iota(T.IO64[:], [[1, 64]], 0, 0, ["IO64"])
-    iota(T.IDX0[:], [[16, 16]], 2048, 0, ["IDX0"])
-    iota(T.TRII[:], [[0, 16], [1, 16]], 0, 0, ["TRII"])
-    iota(T.RXI[:], [[1, 4], [0, 8], [4, 16]], 0, 0, ["RXI"])
-    do("v", [], ["SK"], "fill", ap=T.SK[:], c=0.0)
-    for nm in ("QB", "Q512"):
-        do("v", [], [nm], "fill", ap=T[nm][:], c=0.0)
+    fill(T.ONES[:], 1.0, ["ONES"])
     ts(T.PI[:, 1:2], T.PI[:, 0:1], 4, OP.arith_shift_right, ["PI"], ["PI1"])
     ts(T.PI[:, 2:3], T.PI[:, 0:1], 15, OP.bitwise_and, ["PI"], ["PI2"])
-    cp(T.PF[:, 0:3], T.PI[:, 0:3], ["PI", "PI1", "PI2"], ["PF"])
-    pI, pG, pL = T.PF[:, 0:1], T.PF[:, 1:2], T.PF[:, 2:3]
+    fill(T.CN[:], -65536.0, ["CN"])
+    cp(T.PF[:, 0:2], T.PI[:, 1:3], ["PI1", "PI2"], ["PF"])
+    pG, pL = T.PF[:, 0:1], T.PF[:, 1:2]
+    pick(T.ID[:], T.ONES[:, 0:128], col, OP.is_equal, 0.0, ["ONES"], ["ID"])
     ts(T.BO[:], T.MG[:], pG, OP.is_equal, ["MG", "PF"], ["BO"])
-    ts(T.ID[:], T.MI[:], pI, OP.is_equal, ["MI", "PF"], ["ID"])
+    fill(T.SK[:], 0.0, ["SK"])
+    pick(T.MNE[:], T.BO[:], col, OP.not_equal, 0.0, ["BO"], ["MNE"])
+    pick(T.BOX[:], T.BO[:], col, OP.not_equal, -15.0, ["BO"], ["BOX"])
+    iota(T.T3[:], [[1, 4]], 0, 0, ["T3"])
+    iota(T.PC[:], [[-1, 2], [100, 2]], 0, 0, ["PC"])
+    iota(T.MP[:], [[2, 4], [100, 2], [0, 16]], 0, 0, ["MP"])
+    pick(T.SL[:], T.BO[:], col, OP.is_gt, 0.0, ["BO"], ["SL"])
+    pick(T.SL[:], T.SL[:], col, OP.not_equal, -1.0, ["SL"], ["SL"])
+    iota(T.IO64[:], [[1, 64]], 0, 0, ["IO64"])
+    iota(T.JI[:], [[1, 16], [100, 2]], -100, 0, ["JI"])
+    pick(T.RX[:], T.ONES[:], [[1, 4], [0, 8], [4, 16]], OP.is_equal, 0.0, ["ONES"], ["RX"])
     cp(T.WF[:], T.WI[:], ["WI"], ["WF"])
-    tt(T.MNE[:], T.BO[:], T.ID[:], OP.subtract, ["BO", "ID"], ["MNE"])
     ts(T.W1[:], T.MNE[:], T.WF[:, 0:1], OP.mult, ["MNE", "WF"], ["W1"])
     ts(T.W2[:], T.MNE[:], T.WF[:, 1:2], OP.mult, ["MNE", "WF"], ["W2"])
-    act(T.IDH[:], T.ID[:], ["ID"], ["IDH"])
-    act(T.BOH[:], T.BO[:], ["BO"], ["BOH"])
-    for nm, src, f in (("IDN", "ID", -1.0), ("ID2", "ID", 2.0), ("IDN128", "ID", -128.0), ("ID128", "ID", 128.0),
-                       ("ID64", "ID", 64.0), ("ID8192", "ID", 8192.0), ("BO64", "BO", 64.0), ("BO8192", "BO", 8192.0),
-                       ("BN8", "BO", -8.0)):
+    ts(T.W32[:], T.MNE[:], T.WF[:, 0:1], OP.mult, ["MNE", "WF"], ["W32"], 32.0, OP.mult)
+    for nm, src, f in (("IDN", "ID", -1.0), ("ID128", "ID", 128.0), ("BO64", "BO", 64.0), ("BO8192", "BO", 8192.0)):
         act(T[nm][:], T[src][:], [src], [nm], scale=f)
+    act(T.B15[:], T.BO[:, ::16], ["BO"], ["B15"], scale=1.5)
+    act(T.BNA[:], T.BO[:, ::16], ["BO"], ["BNA"], scale=-1.0 / 4096)
 
     def later_constants():
-        ts(T.C2[:], T.ID[:], 16.0, OP.mult, ["ID"], ["C2"])
-        tt(T.BOX[:], T.BO[:], T.C2[:], OP.subtract, ["BO", "C2"], ["BOX"])
         for e in range(8):
-            cp(T.SK[:, 16 * e:16 * e + 129 * 15 + 1:129], T.BOX[:, 16 * e:16 * e + 16], ["BOX"], ["SK"])
-        ts(T.SL[:], T.MI[:], pI, OP.is_gt, ["MI", "PF"], ["SL"])
-        tt(T.SL[:], T.SL[:], T.BO[:], OP.mult, ["SL", "BO"], ["SL"])
-        tt(T.BASE[:], T.SL[:], T.ID[:], OP.subtract, ["SL", "ID"], ["BASE"])
-        ts(T.C2[:], T.SL[:], 31.0, OP.mult, ["SL"], ["C2"])
-        tt(T.C2[:], T.C2[:], T.BO[:], OP.add, ["C2", "BO"], ["C2"])
-        ts(T.LT1[:], T.ID[:], 17.0, OP.mult, ["ID"], ["LT1"])
-        tt(T.C2[:], T.C2[:], T.LT1[:], OP.subtract, ["C2", "LT1"], ["C2"])
+            cp(T.SK[:, 16 * e:16 * e + 129 * 15 + 1:129], T.BOX[:, 16 * e:16 * e + 16], ["BOX", "SK"], [("SK", e)])
+        lastw["SK"] = lastw[("SK", 7)]
+        ts(T.VA[:], T.T3[:], pL, OP.is_gt, ["T3", "PF"], ["VA"], 31.0, OP.mult)
+        ts(T.VB[:], T.T3[:], pL, OP.is_equal, ["T3", "PF"], ["VB"], -17.0, OP.mult)
+        ts(T.PD[:], T.PC[:], pG, OP.add, ["PC", "PF"], ["PD"])
+        ts(T.THR[:], T.T3[:], pL, OP.not_equal, ["T3", "PF"], ["THR"], -0.5, OP.mult)
+        tt(T.VA[:], T.VA[:], T.VB[:], OP.add, ["VA", "VB"], ["VA"])
+        ts(T.THF[:], T.THI[:], -2048.0, OP.add, ["THI"], ["THF"], 1.0 / 4096, OP.mult)
+        ts(T.PF[:, 8:9], pL, -4.0, OP.mult, ["PF"], ["SQB"], -1.5, OP.add)
+        ts(T.VA[:], T.VA[:], 1.0, OP.add, ["VA"], ["VA"])
+        for i in range(4):
+            ts(T["PM%d" % i][:], T.MP[:], T.PD[:, i:i + 1], OP.is_equal, ["MP", "PD"], ["PM%d" % i])
         for t in range(3):
             nm = "LT%d" % t
-            cp(T[nm][:], T.BASE[:], ["BASE", "C2"], [nm])
-            cp(T[nm][:, t::16], T.C2[:, t::16], ["C2", nm], [nm])
-            ts(T.THR[:, t:t + 1], pL, float(t), OP.not_equal, ["PF"], ["THR"], -0.5, OP.mult)
-        cp(T.QB[:, 15:128:16], T.BO[:, ::16], ["BO"], ["QB"])
-        ts(T.Q512[:, 15:128:16], T.BO[:, ::16], 512.0, OP.mult, ["BO"], ["Q512"])
-        cp(T.QH[:], T.QB[:], ["QB"], ["QH"])
-        ts(T.Q16[:], T.QB[:], 0.0625, OP.mult, ["QB"], ["Q16"])
-        ts(T.THF[:], T.THI[:], -1.0, OP.mult, ["THI"], ["THF"], 2048.0, OP.add)
-        ts(T.THB[:], T.BO[:], T.THF[:], OP.mult, ["BO", "THF"], ["THB"])
-        ts(T.SQB[:], pL, -4.0, OP.mult, ["PF"], ["SQB"], -1.5, OP.add)
-        ts(T.IDX2[:], T.IDX0[:], pL, OP.add, ["IDX0", "PF"], ["IDX2"])
-        ts(T.RX[:], T.RXI[:], pI, OP.is_equal, ["RXI", "PF"], ["RX"])
-        for c in range(16):
-            ts(T.TRI[:, c, :], T.TRII[:, 16 * c:16 * c + 16], pL, OP.is_gt, ["TRII", "PF"], ["TRI"])
+            act(T[nm][:], T.SL[:], ["SL"], [nm])
+        for t in range(3):
+            nm = "LT%d" % t
+            act(T[nm][:, t::16], T.BO[:, ::16], ["BO", "VA", nm], [nm], func=AF.Identity, scale=T.VA[:, t:t + 1])
+        for i in range(4):
+            ts(T["PN%d" % i][:], T["PM%d" % i][:], 64.0, OP.mult, ["PM%d" % i], ["PN%d" % i])
+        ts(T.THB[:], T.BO[:, ::16], T.THF[:], OP.mult, ["BO", "THF"], ["THB"])
 
-    def qwin(name, p):
-        return T[name][:, 15 - p:143 - p]
+    def scan_constants():
+        yield ts(T.PF[:, 9:10], pL, 15.0, OP.is_lt, ["PF"], ["PF9"], 255.0, OP.mult)
+        yield ts(T.RA[:], T.JI[:], pL, OP.is_ge, ["JI", "PF"], ["RA"], 257.0, OP.mult)
+        yield ts(T.PF[:, 11:12], pL, float(W), OP.add, ["PF"], ["SPARE"])
+        yield ts(T.RC[:], T.JI[:], pL, OP.is_equal, ["JI", "PF", "PF9"], ["RC"], T.PF[:, 9:10], OP.mult)
+        yield ts(T.PF[:, 12:13], pL, float(W + 16), OP.add, ["PF"], ["SPARE"])
+        yield fill(T.RR[:, 0:1], 0.0, ["RR0"])
+        yield tt(T.RA[:], T.RA[:], T.RC[:], OP.add, ["RA", "RC"], ["RA"])
+        yield fill(T.EQ[:, 0:256:2], 0.0, ["EQ0"])
+        yield ts(T.RA[:], T.RA[:], -256.0, OP.add, ["RA"], ["RA"])
+        yield ts(T.PF[:, 10:11], T.PF[:, 9:10], 0.5, OP.mult, ["PF9"], ["WIN"], 0.5, OP.add)
+        yield do("v", ["RA"], ["RB"], "inverse", out=T.RB[:], in_=T.RA[:])
+        yield tt(T.RR[:, 1:32], T.RA[:, 0:31], T.RB[:, 1:32], OP.mult, ["RA", "RB"], ["RR"])
+        for n in (32, 64, 128, 256):
+            yield cp(T.RR[:, n:2 * n], T.RR[:, 0:n], ["RR", "RR0"], ["RR"])
 
-    deferred = []
+    chores = scan_constants()
+
+    def chore(n):
+        for _ in range(n):
+            next(chores, None)
+
+    def turned(slot, parts):
+        for s in range(2):
+            n = 0
+            for pm, src in parts:
+                for c in range(2):
+                    n += 1
+                    nm = "%s%d" % (pm, 2 * s + c)
+                    rhs = T[src][:, :, 16 * c:16 * c + 16] if slot == 0 else T[src][:, 128 * c:128 * c + 128]
+                    mm(T.B4[:, 8 * slot:8 * slot + 8, 16 * s:16 * s + 16], T[nm][:], rhs,
+                       n == 1, n == 2 * len(parts), [nm, src], [("B4", slot)])
+
+    def scatter(pairs):
+        for c in range(7, -1, -1):
+            for lex, src in pairs:
+                cp(T[lex][:].indirect(T.OFU[:, 2 * c:2 * c + 2]), T[src][:, 32 * c:32 * c + 32], ["OFU", src, lex], [lex])
+
     for t in range(3):
         xn, mn = "XN%d" % t, "MN%d" % t
         X, M = "X%d" % t, "M%d" % t
         TX, TM = T[X], T[M]
-        for h in range(2):
+        mm(T.B6[:, 0:256], T.CN[:], T.ONES[:, 0:256], True, False, ["CN", "ONES"], [("B6", "Z")])
+
+        def sums(c):
+            b = ("B7", "B5")[c // 2]
             for j, w in ((0, "W1"), (1, "W2")):
-                mm(T.B0[:, 256 * h + 128 * j:256 * h + 128 * j + 128], T[w][:], TX[:, 128 * h:128 * h + 128], True, True,
-                   [w, X], ["B0"])
+                o = 128 * (c % 2) + 64 * j
+                mm(T[b][:, o:o + 64], T[w][:], TX[:, 64 * c:64 * c + 64], True, True, [w, X], [(b, c)])
+        sums(0)
+        sums(1)
+        mm(T.B6[:, 0:256], T.W32[:], TX[:], False, True, ["W32", X], [("B6", "Z")])
+        sums(2)
+        sums(3)
         mm(T.B1[:, 0:256], T.ID[:], TX[:], True, True, ["ID", X], ["B1"])
 
-        def hashes(h):
-            a, b = 256 * h, 128 * h
-            ui, pr, hq, hi = ("UI", h), ("PR", h), ("HQ", h), ("HI", h)
-            cp(T.UI[:, a:a + 256], T.B0[:, a:a + 256], ["B0"], [ui])
-            ts(T.UI[:, a:a + 256], T.UI[:, a:a + 256], 4095, OP.bitwise_and, [ui], [ui])
-            tt(T.PR[:, b:b + 128], T.UI[:, a:a + 128], T.UI[:, a + 128:a + 256], OP.mult, [ui], [pr])
-            ts(T.HQ[:, b:b + 128], T.PR[:, b:b + 128], 5, OP.arith_shift_right, [pr], [hq])
-            tt(T.HQ[:, b:b + 128], T.HQ[:, b:b + 128], T.B0[:, a:a + 128], OP.add, [hq, "B0"], [hq])
-            ts(T.HI[:, b:b + 128], T.HQ[:, b:b + 128], 4095, OP.bitwise_and, [hq], [hi])
-            cp(T.HU[:, b:b + 128], T.HI[:, b:b + 128], [hi], [("HU", h)])
+        def hashes(c):
+            b = ("B7", "B5")[c // 2]
+            s, u = slice(64 * c, 64 * c + 64), slice(128 * c, 128 * c + 128)
+            yield cp(T.UI[:, u], T[b][:, 128 * (c % 2):128 * (c % 2) + 128], [(b, c)], [("UI", c)])
+            yield ts(T.UI[:, u], T.UI[:, u], 4095, OP.bitwise_and, [("UI", c)], [("UI", c)])
+            yield tt(T.PR[:, s], T.UI[:, 128 * c:128 * c + 64], T.UI[:, 128 * c + 64:128 * c + 128], OP.mult, [("UI", c)], [("PR", c)])
+            yield tt(T.ZI[:, s], T.PR[:, s], T.B6[:, s], OP.add, [("PR", c), ("B6", "Z")], [("ZI", c)])
+            yield ts(T.HI[:, s], T.ZI[:, s], 5, OP.arith_shift_right, [("ZI", c)], [("HI", c)], 4095, OP.bitwise_and)
+            yield cp(T.HU[:, s], T.HI[:, s], [("HI", c)], [("HU", c)])
 
-        def sgather(w0, w1, key):
-            act(T.CB[:, 16 * w0:16 * w1], T.LX[:, 0:W].indirect(T.HU[:, w0:w1]), ["LX", ("HU", w0 // 128)], [key])
+        def sgather(c):
+            act(T.CB[:, 1024 * c:1024 * c + 1024], T.LX[:, 0:W].indirect(T.HU[:, 64 * c:64 * c + 64]), ["LX", ("HU", c)], [("CB", c)])
 
-        hashes(0)
-        sgather(0, 64, ("CB", 0))
-        sgather(64, 128, ("CB", 1))
-        hashes(1)
-        sgather(128, 192, ("CB", 2))
-        sgather(192, 224, ("CB", 3))
+        def compare(c):
+            o = 1024 * c
+            for k in range(16):
+                tt(T.EB[:, o + 64 * k:o + 64 * k + 64], T.CB[:, o + k:o + 1024:16], T.B1[:, 64 * c:64 * c + 64], OP.not_equal,
+                   [("CB", c), "B1"], [("EB", c, k // 2)])
+                if k % 2 == 1:
+                    for j in (k - 1, k):
+                        mm(T.B2[:, 64 * c:64 * c + 64], T.SK[:, 128 * j:128 * j + 128], T.EB[:, o + 64 * j:o + 64 * j + 64],
+                           j == 0, j == 15, ["SK", ("EB", c, j // 2)], ["B2"])
+
+        for c in (0, 2):
+            for _ in zip(hashes(c), hashes(c + 1)):
+                pass
         if t == 0:
             later_constants()
-        cp(T.CB[:, 3584:4096], T.LX[:, 0:W].indirect(T.HU[:, 224:256]), ["LX", ("HU", 1)], [("CB", 4)])
-        for f in deferred:
-            f()
-        deferred = []
-        ts(T.H16[:], T.HI[:], -2048.0, OP.add, [("HI", 0), ("HI", 1)], ["H16"])
-        mm(T.B7[:, 256:512], T.IDH[:], T.H16[:], True, True, ["IDH", "H16"], ["B7"])
         for c in range(4):
-            for k in range(16):
-                o = 1024 * c
-                tt(T.EB[:, o + 64 * k:o + 64 * k + 64], T.CB[:, o + k:o + 1024:16], T.B1[:, 64 * c:64 * c + 64], OP.not_equal,
-                   [("CB", c), "B1"] + ([("CB", 4)] if c == 3 else []), [("EB", c, k // 4)])
-            for k in range(16):
-                mm(T.B2[:, 64 * c:64 * c + 64], T.SK[:, 128 * k:128 * k + 128], T.EB[:, 1024 * c + 64 * k:1024 * c + 64 * k + 64],
-                   k == 0, k == 15, ["SK", ("EB", c, k // 4)], ["B2"])
+            sgather(c)
+        ts(T.H16[:], T.HU[:], -2048.0, OP.add, [("HU", c) for c in range(4)], ["H16"])
+        mm(T.B6[:, 256:512], T.ID[:], T.H16[:], True, True, ["ID", "H16"], [("B6", "H")])
+        for c in range(4):
+            compare(c)
+            chore(6 if c < 3 else 0)
         ts(T.PB[:], T.B2[:, 0:256], -11.5, OP.is_le, ["B2"], ["PB"])
         lt = "LT%d" % t
         mm(T.B2[:, 256:512], T[lt][:], T.PB[:], True, True, [lt, "PB"], ["B2"])
-        mm(T.B3[:, 256:512], T.BO[:], T.PB[:], True, True, ["BO", "PB"], ["B3"])
+        mm(T.B3[:, 0:256], T.BO[:], T.PB[:], True, True, ["BO", "PB"], ["B3"])
         ts(T.FB[:], T.B2[:, 256:512], T.THR[:, t:t + 1], OP.is_le, ["B2", "THR"], ["FB"])
-        tt(T.FH[:], T.FB[:], T.B7[:, 256:512], OP.mult, ["FB", "B7"], ["FH"])
-        for p in range(16):
-            mm(T.B4[:, 0:16], qwin("QH", p), T.FH[:, p::16], p == 0, p == 15, ["QH", "FH"], ["B4"])
+        act(T.NH[:], T.B3[:, 0:256], ["B3"], ["NH"], func=AF.Relu, scale=-128.0, bias=64.0)
+        tt(T.FH[:], T.FB[:], T.B6[:, 256:512], OP.mult, ["FB", ("B6", "H")], ["FH"])
+        turned(0, [("PM", "FH")])
         tt(T.FX[:], T.FB[:], T.B1[:, 0:256], OP.mult, ["FB", "B1"], ["FX"])
-        ts(T.NH[:], T.B3[:, 256:512], 0.5, OP.is_le, ["B3"], ["NH"], 64.0, OP.mult)
-        tt(T.XA[:], T.NH[:], T.B1[:, 0:256], OP.add, ["NH", "B1"], ["XA"])
-        for h in range(2):
-            mm(T.B2[:, 8 * h:8 * h + 8], T.FX[:, 128 * h:128 * h + 128], T.BO[:, ::16], True, True, ["FX", "BO"], ["B2"])
-        for p in range(16):
-            mm(T.B2[:, 16:32], qwin("QB", p), T.FX[:, p::16], p == 0, p == 15, ["QB", "FX"], ["B2"])
-        mm(T.B3[:, 256:512], T.BO[:], T.FX[:], True, False, ["BO", "FX"], ["B3"])
-        mm(T.B3[:, 256:512], T.ID2[:], T.NH[:], False, True, ["ID2", "NH"], ["B3"])
-        mm(T.B7[:, 0:256], T.BOH[:], T.FH[:], True, False, ["BOH", "FH"], ["B7"])
-        mm(T.B7[:, 0:256], T.ID128[:], T.NH[:], False, False, ["ID128", "NH"], ["B7"])
-        ts(T.LF[:], T.B4[:, 0:16], 2048.0, OP.add, ["B4"], ["LF"])
-        tt(T.SUB[:], T.LM[:, 0:W].indirect(T.LF[:, 0:16]), TM[:], OP.subtract, ["LM", "LF", M], ["SUB"])
-        act(T.ABS[:], T.SUB[:], ["SUB"], ["ABS"], func=AF.Abs)
-        tt(T.FC[:], T.LX[:, 0:W].indirect(T.LF[:, 0:16]), T.FB[:], OP.mult, ["LX", "LF", "FB"], ["FC"])
-        act(T.SQ[:], T.B3[:, 256:512], ["B3", "SQB"], ["SQ"], func=AF.Square, bias=T.SQB[:])
         for h in range(2):
             s = slice(128 * h, 128 * h + 128)
-            o = T.B4[:, 32 + 8 * h:40 + 8 * h]
-            mm(o, T.FB[:, s], T.THB[:, ::16], True, False, ["FB", "THB"], ["B4"])
-            mm(o, T.NH[:, s], T.BN8[:, ::16], False, False, ["NH", "BN8"], ["B4"])
-            mm(o, T.ABS[:, s], T.BO[:, ::16], False, True, ["ABS", "BO"], ["B4"])
+            mm(T.B3[:, 256 + 8 * h:264 + 8 * h], T.FX[:, s], T.BO[:, ::16], True, False, ["FX", "BO"], ["B3"])
+            mm(T.B3[:, 256 + 8 * h:264 + 8 * h], T.NH[:, s], T.BO[:, ::16], False, True, ["NH", "BO"], ["B3"])
+        tr(T.KB[:], T.B4[:, 0:8, :], [("B4", 0)], ["KB"])
+        mm(T.B7[:, 256:512], T.BO[:], T.FX[:], True, False, ["BO", "FX"], ["B7"])
+        mm(T.B7[:, 256:512], T.ID[:], T.NH[:], False, True, ["ID", "NH"], ["B7"])
+        mm(T.B0[:, 8:16, :], T.ID[:], TX[:], True, False, ["ID", X], ["B0"])
+        mm(T.B0[:, 8:16, :], T.ID[:], T.NH[:], False, True, ["ID", "NH"], ["B0"])
+
+        def hot_x(c0, c1):
+            for c in range(c0, c1):
+                ts(T.OHX[:, 64 * c:64 * c + 64], T.IO64[:], T.B3[:, 256 + c:257 + c], OP.is_equal, ["IO64", "B3"], [("OHX", c)])
+        hot_x(0, 2)
+        ts(T.LF[:], T.KB[:, :, ::16], 2048.0, OP.add, ["KB"], ["LF"])
+        hot_x(2, 4)
+        tt(T.SUB[:], T.LM[:, 0:W].indirect(T.LF[:, 0:16]), TM[:], OP.subtract, ["LM", "LF", M], ["SUB"])
+        act(T.AQ[:], T.B7[:, 256:512], ["B7", "SQB"], ["AQ"], func=AF.Abs, bias=T.PF[:, 8:9])
+        act(T.ABS[:], T.SUB[:], ["SUB"], ["ABS"], func=AF.Abs)
+        tt(T.FC[:], T.LX[:, 0:W].indirect(T.LF[:, 0:16]), T.FB[:], OP.mult, ["LX", "LF", "FB"], ["FC"])
+        hot_x(4, 16)
         for h in range(2):
-            mm(T.B4[:, 16 + 8 * h:24 + 8 * h], T.FC[:, 128 * h:128 * h + 128], T.BO[:, ::16], True, True, ["FC", "BO"], ["B4"])
-        cp(T.XTS[:], T.B2[:, 0:16], ["B2"], ["XTS"])
-        cp(T.XL[:], T.B2[:, 16:32], ["B2"], ["XL"])
-        for c in range(16):
-            ts(T.OHX[:, 64 * c:64 * c + 64], T.IO64[:], T.XTS[:, c:c + 1], OP.is_equal, ["IO64", "XTS"], [("OHX", c // 4)])
-        for p in range(16):
-            mm(T.B2[:, 32:48], qwin("QB", p), T.FC[:, p::16], p == 0, p == 15, ["QB", "FC"], ["B2"])
-        cp(T.CTS[:], T.B4[:, 16:32], ["B4"], ["CTS"])
-        ts(T.NTS[:], T.B4[:, 32:48], 2047.5, OP.is_ge, ["B4"], ["NTS"])
+            s = slice(128 * h, 128 * h + 128)
+            o = T.B5[:, 16 + 8 * h:24 + 8 * h]
+            mm(o, T.FB[:, s], T.THB[:], True, False, ["FB", "THB"], ["B5"])
+            mm(o, T.FB[:, s], T.B15[:], False, False, ["FB", "B15"], ["B5"])
+            mm(o, T.ABS[:, s], T.BNA[:], False, True, ["ABS", "BNA"], ["B5"])
+        for h in range(2):
+            mm(T.B5[:, 8 * h:8 * h + 8], T.FC[:, 128 * h:128 * h + 128], T.BO[:, ::16], True, True, ["FC", "BO"], ["B5"])
+        turned(1, [("PN", "FX"), ("PM", "FC")])
+        act(T.MK[:], T.AQ[:], ["AQ"], ["MK"], func=AF.Relu, scale=-2.0, bias=4.0)
+        act(T.XA[:], T.B0[:, 8:16, :], ["B0"], ["XA"])
+        act(T.D16[:], T.SUB[:], ["SUB"], ["D16"], func=AF.Identity, scale=0.5, bias=1535.75)
+        act(T.DM[:], T.D16[:], ["D16"], ["DM"], func=AF.Identity, bias=-1536.0)
+        for o in range(2):
+            act(T.KL[:, 8 * o:8 * o + 8], T.KB[:, :, 16 * o], ["KB"], ["KL"])
         for c in range(16):
             s = slice(64 * c, 64 * c + 64)
-            ts(T.OHC[:, s], T.IO64[:], T.CTS[:, c:c + 1], OP.is_equal, ["IO64", "CTS", "NTS"], [("OHC", c // 2)],
-               T.NTS[:, c:c + 1], OP.mult)
-            if c % 2 == 1:
-                for d in (c - 1, c):
-                    s = slice(64 * d, 64 * d + 64)
-                    rd = [("OHX", d // 4), ("OHC", d // 2)]
-                    mm(T.B5[0:64, 0:64], T.OHX[:, s], T.OHC[:, s], d == 0, False, rd, ["B5"])
-                    mm(T.B5[0:64, 0:64], T.OHC[:, s], T.OHX[:, s], False, d == 15, rd, ["B5"])
-        mm(T.B3[:, 0:256], T.THB[:], T.FB[:], True, False, ["THB", "FB"], ["B3"])
-        mm(T.B3[:, 0:256], T.IDN128[:], T.NH[:], False, False, ["IDN128", "NH"], ["B3"])
-        mm(T.B3[:, 0:256], T.BO[:], T.ABS[:], False, True, ["BO", "ABS"], ["B3"])
-        ts(T.XL[:], T.XL[:], 3, OP.bitwise_and, ["XL"], ["XL"])
-        ts(T.MK[:], T.SQ[:], 4.0, OP.is_le, ["SQ"], ["MK"])
-        ts(T.XLF[:], T.XL[:], 64.0, OP.mult, ["XL"], ["XLF"])
-        tt(T.CLF[:], T.XLF[:], T.B2[:, 32:48], OP.add, ["XLF", "B2"], ["CLF"])
-        cp(T.CL[:], T.CLF[:], ["CLF"], ["CL"])
-        ts(T.TB[0:64, :], T.B5[0:64, 0:64], 1.0, OP.min, ["B5"], ["TB"])
+            ts(T.OHC[:, s], T.IO64[:], T.B5[:, c:c + 1], OP.is_equal, ["IO64", "B5"], [("OHC", c)],
+               T.B5[:, 16 + c:17 + c], OP.is_ge)
+            rd = [("OHX", c), ("OHC", c)]
+            mm(T.B6[0:64, 0:64], T.OHX[:, s], T.OHC[:, s], c == 0, False, rd, ["B6"])
+            mm(T.B6[0:64, 0:64], T.OHC[:, s], T.OHX[:, s], False, c == 15, rd, ["B6"])
+        tr(T.KC[:], T.B4[:, 8:16, :], [("B4", 1)], ["KC"])
+        cp(T.TB[0:64, :], T.B6[0:64, 0:64], ["B6"], ["TB"])
         for r in range(4):
-            mm(T.B5[:, 256 + 64 * r:320 + 64 * r], T.RX[0:64, 128 * r:128 * r + 128], T.TB[0:64, :], True, True, ["RX", "TB"], ["B5"])
-        act(T.TW[:], T.B5[:, 256:512], ["B5"], ["TW"])
-        ts(T.HN[:], T.B3[:, 0:256], 2047.5, OP.is_ge, ["B3"], ["HN"])
-        mm(T.B6[:, 0:256], T.ID[:], TX[:], True, False, ["ID", X], ["B6"])
-        mm(T.B6[:, 0:256], T.IDN[:], T.FX[:], False, False, ["IDN", "FX"], ["B6"])
-        mm(T.B6[:, 0:256], T.ID[:], T.FC[:], False, False, ["ID", "FC"], ["B6"])
-        mm(T.B6[:, 0:256], T.ID64[:], T.HN[:], False, False, ["ID64", "HN"], ["B6"])
-        mm(T.B7[:, 0:256], T.ID8192[:], T.HN[:], False, False, ["ID8192", "HN"], ["B7"])
+            mm(T.B6[:, 256 + 64 * r:320 + 64 * r], T.RX[0:64, 128 * r:128 * r + 128], T.TB[0:64, :], True, True, ["RX", "TB"], ["B6"])
+        for h in range(2):
+            cp(T.CI[:, 8 * h:8 * h + 8], T.KC[:, 16 * h::32], ["KC"], [("CI", h)])
+        mm(T.B7[:, 0:256], T.ID[:], TX[:], True, False, ["ID", X], ["B7"])
+        mm(T.B7[:, 0:256], T.IDN[:], T.FX[:], False, False, ["IDN", "FX"], ["B7"])
+        mm(T.B7[:, 0:256], T.ID[:], T.FC[:], False, False, ["ID", "FC"], ["B7"])
+        mm(T.B0[:, 0:8, :], T.BO[:], T.FH[:], True, False, ["BO", "FH"], ["B0"])
+        mm(T.B0[:, 0:8, :], T.ID128[:], T.NH[:], False, False, ["ID128", "NH"], ["B0"])
+        mm(T.B3[:, 0:256], T.ID[:], T.NH[:], True, False, ["ID", "NH"], ["B3"])
+        ts(T.CI[:], T.CI[:], 255, OP.bitwise_and, [("CI", 0), ("CI", 1)], ["CI"])
+        cp(T.TW[:], T.B6[:, 256:512], ["B6"], ["TW"])
+        cp(T.CL[:], T.CI[:], ["CI"], ["CL"])
         tt(T.GT[:], T.TW[:].indirect(T.CL[:, 0:16]), T.MK[:], OP.mult, ["TW", "CL", "MK"], ["GT"])
-        mm(T.B6[:, 0:256], T.BO64[:], T.GT[:], False, True, ["BO64", "GT"], ["B6"])
-        mm(T.B7[:, 0:256], T.BO8192[:], T.GT[:], False, True, ["BO8192", "GT"], ["B7"])
-        tt(T[xn][:], T.XA[:], T.B6[:, 0:256], OP.min, ["XA", "B6"], [xn])
+        mm(T.B7[:, 0:256], T.BO64[:], T.GT[:], False, True, ["BO64", "GT"], ["B7"])
+        mm(T.B3[:, 0:256], T.BO[:], T.GT[:], False, True, ["BO", "GT"], ["B3"])
+        mm(T.B0[:, 0:8, :], T.BO8192[:], T.GT[:], False, True, ["BO8192", "GT"], ["B0"])
+        tt(T[xn][:], T.XA[:], T.B7[:, 0:256], OP.min, ["XA", "B7"], [xn])
+        act(T.B5[:, 256:512], T.B3[:, 0:256], ["B3"], ["B5"], func=AF.Relu, scale=-1.0, bias=1.0)
         dst = T.cores[(rank + (3 if t < 2 else 2)) % n_ranks]
         rid, pid, _eng = topo.addr(dst)
         mask = topo.mask(core, dst)
@@ -403,45 +455,28 @@ def rank_program(g, core, T, topo):
             g.remote_dma(T[out][:], T[src][:], T.sem[sem], T.sem.ls, pid, rid, mask)
             lastw[out] = (sem, ne, {}, "remote")
         send("X%d" % (t + 1), xn, "ax%d" % (t + 1))
-        ts(T.DK[:], T.B7[:, 0:256], 6144.0, OP.min, ["B7"], ["DK"])
-        for p in range(16):
-            mm(T.B4[:, 48:64], qwin("Q16", p), T.DK[:, p::16], p == 0, p == 15, ["Q16", "DK"], ["B4"])
-        ts(T.MGR[:], T.B7[:, 0:256], 4000.0, OP.is_lt, ["B7"], ["MGR"])
-        ts(T.DMI[:], T.SUB[:], 0.5, OP.mult, ["SUB"], ["DMI"], -0.25, OP.add)
-        tt(T.DT[:], T.MGR[:], T.DMI[:], OP.mult, ["MGR", "DMI"], ["DT"])
-        mm(T.B0[:, 0:256], T.ID[:], TM[:], True, False, ["ID", M], ["B0"])
-        mm(T.B0[:, 0:256], T.ID[:], T.DT[:], False, True, ["ID", "DT"], ["B0"])
-        act(T[mn][:], T.B0[:, 0:256], ["B0"], [mn])
+        for o, a, b in ((1, 0, 0), (256, 16, 0), (257, 16, 16)):
+            tt(T.EQ[:, o:o + 255:2], T.KB[:, :, a:a + 16], T.B0[:, 0:8, b:b + 16], OP.is_equal, ["KB", "B0"], ["EQ"])
+        mm(T.B2[:, 0:256], T.ID[:], TM[:], True, False, ["ID", M], ["B2"])
+        tt(T.GD[:], T.DM[:], T.B5[:, 256:512], OP.mult, ["DM", "B5"], ["GD"])
+        mm(T.B2[:, 0:256], T.ID[:], T.GD[:], False, True, ["ID", "GD"], ["B2"])
+        act(T[mn][:], T.B2[:, 0:256], ["B2"], [mn])
         send("M%d" % (t + 1), mn, "am%d" % (t + 1))
-        for p in range(16):
-            mm(T.B5[:, 0:16], qwin("Q16", p), T.DK[:, p::16], p == 0, False, ["Q16", "DK"], ["B5"])
-        cp(T.KLS[:], T.B4[:, 48:64], ["B4"], ["KLS"])
-        for c in range(16):
-            ts(T.EQ[:, c, 0:256 - 16 * c], T.DK[:, 16 * c:256], T.KLS[:, c:c + 1], OP.is_equal, ["DK", "KLS"], ["EQ"])
-        tt(T.EQ[:, :, 0:16], T.EQ[:, :, 0:16], T.TRI[:], OP.mult, ["EQ", "TRI"], ["EQ"])
-        for c in range(16):
-            mm(T.B2[:, 16 * c:256], T.BO[:], T.EQ[:, c, 0:256 - 16 * c], c == 0, c == 15, ["BO", "EQ"], ["B2"])
-        ts(T.LS[:], T.B2[:, 0:256], 0.5, OP.is_ge, ["B2"], ["LS"])
-        for p in range(16):
-            mm(T.B5[:, 0:16], qwin("Q512", p), T.LS[:, p::16], False, p == 15, ["Q512", "LS"], ["B5"])
-        tt(T.OFF[:], T.B5[:, 0:16], T.IDX2[:], OP.min, ["B5", "IDX2"], ["OFF"])
-        ts(T.OFU[:], T.OFF[:], 2048.0, OP.add, ["OFF"], ["OFU"])
-        cp(T.LX[:].indirect(T.OFU[:, 0:16]), T[xn][:], ["OFU", xn, "LX"], ["LX"])
+        do("v", ["RR", "EQ", "EQ0"], ["SC"], "scan", out=T.SC[:], data0=T.RR[:], data1=T.EQ[:], initial=0.0, op0=OP.mult, op1=OP.add)
+        ts(T.Z[:], T.SC[:, 31::32], T.PF[:, 10:11], OP.is_lt, ["SC", "WIN"], ["Z"], 8192.0, OP.mult)
+        tt(T.Y[:], T.Z[:], T.KL[:], OP.add, ["Z", "KL"], ["Y"])
+        for o in range(2):
+            ts(T.OFU[:, o::2], T.Y[:, 8 * o:8 * o + 8], 2048.0, OP.add, ["Y", "SPARE"], ["OFU"], T.PF[:, 11 + o:12 + o], OP.min)
+        scatter([("LX", xn), ("LM", mn)])
 
-        def scatter_meanings(mn=mn):
-            cp(T.LM[:].indirect(T.OFU[:, 0:16]), T[mn][:], ["OFU", mn, "LM"], ["LM"])
-        deferred = [scatter_meanings]
-
-    dma("s", T.yl[:], T.LX[:, 0:W], ["LX"], ["yl"])
-    for f in deferred:
-        f()
-    act(T.CB[:, 0:1792], T.LM[:, 2304:4096], ["LM"], [("CB", 0), ("CB", 1)], accum_out=T.SUM[:, 1:2])
+    dma("y", T.yl[:], T.LX[:, 0:W], ["LX"], ["yl"])
+    act(T.CB[:, 0:2048], T.LM[:, 2048:4096], ["LM"], [("CB", 0), ("CB", 1)], accum_out=T.SUM[:, 1:2])
     lastw["SUM1"] = lastw[("CB", 0)]
-    do("v", ["LM"], ["SUM0"], "reduce", out=T.SUM[:, 0:1], in_=T.LM[:, 0:2304], axis=AxisListType.X, op=OP.add)
+    do("v", ["LM"], ["SUM0"], "reduce", out=T.SUM[:, 0:1], in_=T.LM[:, 0:2048], axis=AxisListType.X, op=OP.add)
     tt(T.YM[:], T.SUM[:, 0:1], T.SUM[:, 1:2], OP.add, ["SUM0", "SUM1"], ["YM"])
     dma("y", T.yx[:], T.X3[:], ["X3"], ["yx"])
     dma("y", T.yg[:], T.M3[:], ["M3"], ["yg"])
-    dma("y", T.ym[:], T.YM[:], ["YM"], ["ym"])
+    dma("s", T.ym[:], T.YM[:], ["YM"], ["ym"])
     for sem in ("qv", "qs", "qt", "qg"):
         wait("g", (sem, count[sem], {}, ""))
     for tok in dmas:

@@ -3,6 +3,7 @@ from concourse.mybir import AluOpType, AxisListType, ActivationFunctionType
 OP = AluOpType
 AF = ActivationFunctionType
 W, K = 4096, 256
+SHARE = (80, 64, 64)
 
 _S = {}
 
@@ -25,14 +26,14 @@ _sb("WI", 2, "int32")
 _sb("WF", 2, "float32")
 _sb("THI", 1, "int32")
 _sb("THF", 1, "float32")
-for _n in ("BO", "BO64", "BO8192", "ID", "IDN", "ID128", "SL", "MNE", "BOX", "W1", "W2", "W32", "LT0", "LT1", "LT2", "CN"):
+for _n in ("BO", "BO64", "BO8192", "ID", "IDN", "ID128", "SL", "MNE", "BOX", "W1", "W2", "W32", "LT0", "LT1", "LT2", "CN",
+           "C5120", "IDN4096"):
     _sb(_n, 128)
 _sb("ONES", 512)
 for _n in ("THB", "B15", "BNA"):
     _sb(_n, 8, "float16")
 for _n in range(4):
     _sb("PM%d" % _n, 128, "float16")
-    _sb("PN%d" % _n, 128, "float16")
 _sb("SK", 2048)
 _sb("RX", 512)
 _sb("IO64", 64)
@@ -40,7 +41,11 @@ for _n in ("JI", "RA", "RB", "RC"):
     _sb(_n, 32, "float32")
 for _n in ("RR", "EQ", "SC"):
     _sb(_n, 512)
-_sb("UI", 512, "int32")
+_sb("UI", 256, "int32")
+_sb("Q", 256)
+_sb("UP", 128, "float32")
+_sb("QB", 144, "float16")
+_sb("Q64", 144, "float16")
 _sb("PR", 256, "int32")
 _sb("ZI", 256, "int32")
 _sb("HI", 256, "int32")
@@ -56,7 +61,6 @@ _sb("FC", 256, "float16")
 _sb("NH", 256)
 _sb("XA", 256)
 _S["KB"] = ("sbuf", [128, 8, 32], "float32")
-_sb("KC", 256, "float32")
 _sb("KL", 16, "float32")
 _sb("LF", 16, "uint16")
 _sb("SUB", 256)
@@ -223,8 +227,8 @@ def rank_program(g, core, T, topo):
     dma("s", T.WI[:], T.wts[:], [], ["WI"])
     dma("y", T.LX[:, 0:W], T.lex[:], [], ["LX"])
     dma("s", T.THI[:], T.th[:], [], ["THI"])
+    dma("y", T.LM[:, 0:W], T.mng[:], ["LX"], ["LM"])
     dma("y", T.M0[:], T.gw[:], [], ["M0"])
-    dma("y", T.LM[:, 0:W], T.mng[:], [], ["LM"])
 
     col = [[1, 128]]
     iota(T.PI[:, 0:1], [[0, 1]], 0, 1, ["PI"], False)
@@ -233,7 +237,10 @@ def rank_program(g, core, T, topo):
     ts(T.PI[:, 1:2], T.PI[:, 0:1], 4, OP.arith_shift_right, ["PI"], ["PI1"])
     ts(T.PI[:, 2:3], T.PI[:, 0:1], 15, OP.bitwise_and, ["PI"], ["PI2"])
     fill(T.CN[:], -65536.0, ["CN"])
+    fill(T.C5120[:], 5120.0, ["C5120"])
     cp(T.PF[:, 0:2], T.PI[:, 1:3], ["PI1", "PI2"], ["PF"])
+    fill(T.QB[:], 0.0, ["QB"])
+    fill(T.Q64[:], 0.0, ["Q64"])
     pG, pL = T.PF[:, 0:1], T.PF[:, 1:2]
     pick(T.ID[:], T.ONES[:, 0:128], col, OP.is_equal, 0.0, ["ONES"], ["ID"])
     ts(T.BO[:], T.MG[:], pG, OP.is_equal, ["MG", "PF"], ["BO"])
@@ -252,12 +259,14 @@ def rank_program(g, core, T, topo):
     ts(T.W1[:], T.MNE[:], T.WF[:, 0:1], OP.mult, ["MNE", "WF"], ["W1"])
     ts(T.W2[:], T.MNE[:], T.WF[:, 1:2], OP.mult, ["MNE", "WF"], ["W2"])
     ts(T.W32[:], T.MNE[:], T.WF[:, 0:1], OP.mult, ["MNE", "WF"], ["W32"], 32.0, OP.mult)
-    for nm, src, f in (("IDN", "ID", -1.0), ("ID128", "ID", 128.0), ("BO64", "BO", 64.0), ("BO8192", "BO", 8192.0)):
+    for nm, src, f in (("IDN4096", "ID", -4096.0), ("IDN", "ID", -1.0), ("ID128", "ID", 128.0)):
         act(T[nm][:], T[src][:], [src], [nm], scale=f)
-    act(T.B15[:], T.BO[:, ::16], ["BO"], ["B15"], scale=1.5)
-    act(T.BNA[:], T.BO[:, ::16], ["BO"], ["BNA"], scale=-1.0 / 4096)
 
     def later_constants():
+        for nm, src, f in (("BO64", "BO", 64.0), ("BO8192", "BO", 8192.0)):
+            act(T[nm][:], T[src][:], [src], [nm], scale=f)
+        act(T.B15[:], T.BO[:, ::16], ["BO"], ["B15"], scale=1.5)
+        act(T.BNA[:], T.BO[:, ::16], ["BO"], ["BNA"], scale=-1.0 / 4096)
         for e in range(8):
             cp(T.SK[:, 16 * e:16 * e + 129 * 15 + 1:129], T.BOX[:, 16 * e:16 * e + 16], ["BOX", "SK"], [("SK", e)])
         lastw["SK"] = lastw[("SK", 7)]
@@ -269,19 +278,18 @@ def rank_program(g, core, T, topo):
         ts(T.THF[:], T.THI[:], -2048.0, OP.add, ["THI"], ["THF"], 1.0 / 4096, OP.mult)
         ts(T.PF[:, 8:9], pL, -4.0, OP.mult, ["PF"], ["SQB"], -1.5, OP.add)
         ts(T.VA[:], T.VA[:], 1.0, OP.add, ["VA"], ["VA"])
-        for i in range(4):
-            ts(T["PM%d" % i][:], T.MP[:], T.PD[:, i:i + 1], OP.is_equal, ["MP", "PD"], ["PM%d" % i])
         for t in range(3):
-            nm = "LT%d" % t
-            act(T[nm][:], T.SL[:], ["SL"], [nm])
-        for t in range(3):
-            nm = "LT%d" % t
-            act(T[nm][:, t::16], T.BO[:, ::16], ["BO", "VA", nm], [nm], func=AF.Identity, scale=T.VA[:, t:t + 1])
-        for i in range(4):
-            ts(T["PN%d" % i][:], T["PM%d" % i][:], 64.0, OP.mult, ["PM%d" % i], ["PN%d" % i])
+            act(T["LT%d" % t][:], T.SL[:], ["SL"], ["LT%d" % t])
+        cp(T.QB[:, 15:128:16], T.BO[:, ::16], ["BO", "QB"], ["QB"])
+        ts(T.Q64[:, 15:128:16], T.BO[:, ::16], 64.0, OP.mult, ["BO", "Q64"], ["Q64"])
         ts(T.THB[:], T.BO[:, ::16], T.THF[:], OP.mult, ["BO", "THF"], ["THB"])
+        for t in range(3):
+            nm = "LT%d" % t
+            ts(T[nm][:, t::16], T.BO[:, ::16], T.VA[:, t:t + 1], OP.mult, ["BO", "VA", nm], [nm])
 
     def scan_constants():
+        for i in range(4):
+            yield ts(T["PM%d" % i][:], T.MP[:], T.PD[:, i:i + 1], OP.is_equal, ["MP", "PD"], ["PM%d" % i])
         yield ts(T.PF[:, 9:10], pL, 15.0, OP.is_lt, ["PF"], ["PF9"], 255.0, OP.mult)
         yield ts(T.RA[:], T.JI[:], pL, OP.is_ge, ["JI", "PF"], ["RA"], 257.0, OP.mult)
         yield ts(T.PF[:, 11:12], pL, float(W), OP.add, ["PF"], ["SPARE"])
@@ -303,16 +311,15 @@ def rank_program(g, core, T, topo):
         for _ in range(n):
             next(chores, None)
 
-    def turned(slot, parts):
+    def turned():
         for s in range(2):
-            n = 0
-            for pm, src in parts:
-                for c in range(2):
-                    n += 1
-                    nm = "%s%d" % (pm, 2 * s + c)
-                    rhs = T[src][:, :, 16 * c:16 * c + 16] if slot == 0 else T[src][:, 128 * c:128 * c + 128]
-                    mm(T.B4[:, 8 * slot:8 * slot + 8, 16 * s:16 * s + 16], T[nm][:], rhs,
-                       n == 1, n == 2 * len(parts), [nm, src], [("B4", slot)])
+            for c in range(2):
+                nm = "PM%d" % (2 * s + c)
+                mm(T.B4[:, 0:8, 16 * s:16 * s + 16], T[nm][:], T.FH[:, :, 16 * c:16 * c + 16], c == 0, c == 1, [nm, "FH"], ["B4"])
+
+    def listed(q, src, first):
+        for p in range(16):
+            mm(T.B2[:, 0:16], T[q][:, 15 - p:143 - p], T[src][:, p::16], first and p == 0, p == 15 and not first, [q, src], ["B2"])
 
     def scatter(pairs):
         for c in range(7, -1, -1):
@@ -324,37 +331,42 @@ def rank_program(g, core, T, topo):
         X, M = "X%d" % t, "M%d" % t
         TX, TM = T[X], T[M]
         mm(T.B6[:, 0:256], T.CN[:], T.ONES[:, 0:256], True, False, ["CN", "ONES"], [("B6", "Z")])
+        mm(T.B3[:, 0:256], T.C5120[:], T.ONES[:, 0:256], True, False, ["C5120", "ONES"], ["B3"])
 
-        def sums(c):
-            b = ("B7", "B5")[c // 2]
+        def sums(b, o, w0, n, alone):
             for j, w in ((0, "W1"), (1, "W2")):
-                o = 128 * (c % 2) + 64 * j
-                mm(T[b][:, o:o + 64], T[w][:], TX[:, 64 * c:64 * c + 64], True, True, [w, X], [(b, c)])
-        sums(0)
-        sums(1)
+                mm(T[b][:, o + n * j:o + n * j + n], T[w][:], TX[:, w0:w0 + n], alone, alone, [w, X], [b])
+        sums("B7", 0, 0, 64, True)
+        sums("B7", 128, 64, 64, True)
+        sums("B5", 0, 128, 128, True)
         mm(T.B6[:, 0:256], T.W32[:], TX[:], False, True, ["W32", X], [("B6", "Z")])
-        sums(2)
-        sums(3)
+        sums("B3", 0, 128, 128, False)
+        act(T.Q[:], T.B5[:, 0:256], ["B5"], ["Q"], func=AF.Identity, scale=1.0 / 4096, bias=159.5 + 1.0 / 8192)
         mm(T.B1[:, 0:256], T.ID[:], TX[:], True, True, ["ID", X], ["B1"])
+        mm(T.B3[:, 0:256], T.IDN4096[:], T.Q[:], False, True, ["IDN4096", "Q"], ["B3"])
+        act(T.UP[:], T.B3[:, 128:256], ["B3"], ["UP"])
 
         def hashes(c):
-            b = ("B7", "B5")[c // 2]
             s, u = slice(64 * c, 64 * c + 64), slice(128 * c, 128 * c + 128)
-            yield cp(T.UI[:, u], T[b][:, 128 * (c % 2):128 * (c % 2) + 128], [(b, c)], [("UI", c)])
-            yield ts(T.UI[:, u], T.UI[:, u], 4095, OP.bitwise_and, [("UI", c)], [("UI", c)])
-            yield tt(T.PR[:, s], T.UI[:, 128 * c:128 * c + 64], T.UI[:, 128 * c + 64:128 * c + 128], OP.mult, [("UI", c)], [("PR", c)])
+            if c < 2:
+                yield cp(T.UI[:, u], T.B7[:, u], ["B7"], [("UI", c)])
+                yield ts(T.UI[:, u], T.UI[:, u], 4095, OP.bitwise_and, [("UI", c)], [("UI", c)])
+                yield tt(T.PR[:, s], T.UI[:, 128 * c:128 * c + 64], T.UI[:, 128 * c + 64:128 * c + 128], OP.mult, [("UI", c)], [("PR", c)])
+            else:
+                u = slice(64 * c - 128, 64 * c - 64)
+                yield tt(T.PR[:, s], T.UP[:, u], T.B3[:, u], OP.mult, ["UP", "B3"], [("PR", c)])
             yield tt(T.ZI[:, s], T.PR[:, s], T.B6[:, s], OP.add, [("PR", c), ("B6", "Z")], [("ZI", c)])
             yield ts(T.HI[:, s], T.ZI[:, s], 5, OP.arith_shift_right, [("ZI", c)], [("HI", c)], 4095, OP.bitwise_and)
             yield cp(T.HU[:, s], T.HI[:, s], [("HI", c)], [("HU", c)])
 
-        def sgather(c):
-            act(T.CB[:, 1024 * c:1024 * c + 1024], T.LX[:, 0:W].indirect(T.HU[:, 64 * c:64 * c + 64]), ["LX", ("HU", c)], [("CB", c)])
+        def gather(how, w0, w1, key):
+            how(T.CB[:, 16 * w0:16 * w1], T.LX[:, 0:W].indirect(T.HU[:, w0:w1]), ["LX", ("HU", w0 // 64)], [key])
 
         def compare(c):
             o = 1024 * c
             for k in range(16):
                 tt(T.EB[:, o + 64 * k:o + 64 * k + 64], T.CB[:, o + k:o + 1024:16], T.B1[:, 64 * c:64 * c + 64], OP.not_equal,
-                   [("CB", c), "B1"], [("EB", c, k // 2)])
+                   [("CB", c), ("CB", c, "v"), "B1"], [("EB", c, k // 2)])
                 if k % 2 == 1:
                     for j in (k - 1, k):
                         mm(T.B2[:, 64 * c:64 * c + 64], T.SK[:, 128 * j:128 * j + 128], T.EB[:, o + 64 * j:o + 64 * j + 64],
@@ -365,43 +377,50 @@ def rank_program(g, core, T, topo):
                 pass
         if t == 0:
             later_constants()
-        for c in range(4):
-            sgather(c)
+        share = SHARE[t]
+        for c in range(3):
+            gather(act, 64 * c, min(64 * c + 64, 256 - share), ("CB", c))
+        gather(cp, 192, 256, ("CB", 3))
+        if share > 64:
+            gather(cp, 256 - share, 192, ("CB", 2, "v"))
         ts(T.H16[:], T.HU[:], -2048.0, OP.add, [("HU", c) for c in range(4)], ["H16"])
         mm(T.B6[:, 256:512], T.ID[:], T.H16[:], True, True, ["ID", "H16"], [("B6", "H")])
-        for c in range(4):
+        for c in (0, 3, 1, 2):
             compare(c)
-            chore(6 if c < 3 else 0)
         ts(T.PB[:], T.B2[:, 0:256], -11.5, OP.is_le, ["B2"], ["PB"])
         lt = "LT%d" % t
         mm(T.B2[:, 256:512], T[lt][:], T.PB[:], True, True, [lt, "PB"], ["B2"])
         mm(T.B3[:, 0:256], T.BO[:], T.PB[:], True, True, ["BO", "PB"], ["B3"])
+        chore(4)
         ts(T.FB[:], T.B2[:, 256:512], T.THR[:, t:t + 1], OP.is_le, ["B2", "THR"], ["FB"])
         act(T.NH[:], T.B3[:, 0:256], ["B3"], ["NH"], func=AF.Relu, scale=-128.0, bias=64.0)
+        chore(2)
         tt(T.FH[:], T.FB[:], T.B6[:, 256:512], OP.mult, ["FB", ("B6", "H")], ["FH"])
-        turned(0, [("PM", "FH")])
+        for p in range(16):
+            mm(T.B5[:, 0:16], T.QB[:, 15 - p:143 - p], T.FH[:, :, p::16], p == 0, p == 15, ["QB", "FH"], ["B5"])
         tt(T.FX[:], T.FB[:], T.B1[:, 0:256], OP.mult, ["FB", "B1"], ["FX"])
         for h in range(2):
             s = slice(128 * h, 128 * h + 128)
             mm(T.B3[:, 256 + 8 * h:264 + 8 * h], T.FX[:, s], T.BO[:, ::16], True, False, ["FX", "BO"], ["B3"])
             mm(T.B3[:, 256 + 8 * h:264 + 8 * h], T.NH[:, s], T.BO[:, ::16], False, True, ["NH", "BO"], ["B3"])
-        tr(T.KB[:], T.B4[:, 0:8, :], [("B4", 0)], ["KB"])
+        chore(6)
+        ts(T.LF[:], T.B5[:, 0:16], 2048.0, OP.add, ["B5"], ["LF"])
         mm(T.B7[:, 256:512], T.BO[:], T.FX[:], True, False, ["BO", "FX"], ["B7"])
         mm(T.B7[:, 256:512], T.ID[:], T.NH[:], False, True, ["ID", "NH"], ["B7"])
         mm(T.B0[:, 8:16, :], T.ID[:], TX[:], True, False, ["ID", X], ["B0"])
         mm(T.B0[:, 8:16, :], T.ID[:], T.NH[:], False, True, ["ID", "NH"], ["B0"])
+        listed("Q64", "FX", True)
+        turned()
 
         def hot_x(c0, c1):
             for c in range(c0, c1):
                 ts(T.OHX[:, 64 * c:64 * c + 64], T.IO64[:], T.B3[:, 256 + c:257 + c], OP.is_equal, ["IO64", "B3"], [("OHX", c)])
         hot_x(0, 2)
-        ts(T.LF[:], T.KB[:, :, ::16], 2048.0, OP.add, ["KB"], ["LF"])
-        hot_x(2, 4)
         tt(T.SUB[:], T.LM[:, 0:W].indirect(T.LF[:, 0:16]), TM[:], OP.subtract, ["LM", "LF", M], ["SUB"])
         act(T.AQ[:], T.B7[:, 256:512], ["B7", "SQB"], ["AQ"], func=AF.Abs, bias=T.PF[:, 8:9])
         act(T.ABS[:], T.SUB[:], ["SUB"], ["ABS"], func=AF.Abs)
         tt(T.FC[:], T.LX[:, 0:W].indirect(T.LF[:, 0:16]), T.FB[:], OP.mult, ["LX", "LF", "FB"], ["FC"])
-        hot_x(4, 16)
+        hot_x(2, 16)
         for h in range(2):
             s = slice(128 * h, 128 * h + 128)
             o = T.B5[:, 16 + 8 * h:24 + 8 * h]
@@ -410,13 +429,11 @@ def rank_program(g, core, T, topo):
             mm(o, T.ABS[:, s], T.BNA[:], False, True, ["ABS", "BNA"], ["B5"])
         for h in range(2):
             mm(T.B5[:, 8 * h:8 * h + 8], T.FC[:, 128 * h:128 * h + 128], T.BO[:, ::16], True, True, ["FC", "BO"], ["B5"])
-        turned(1, [("PN", "FX"), ("PM", "FC")])
+        listed("QB", "FC", False)
         act(T.MK[:], T.AQ[:], ["AQ"], ["MK"], func=AF.Relu, scale=-2.0, bias=4.0)
         act(T.XA[:], T.B0[:, 8:16, :], ["B0"], ["XA"])
         act(T.D16[:], T.SUB[:], ["SUB"], ["D16"], func=AF.Identity, scale=0.5, bias=1535.75)
         act(T.DM[:], T.D16[:], ["D16"], ["DM"], func=AF.Identity, bias=-1536.0)
-        for o in range(2):
-            act(T.KL[:, 8 * o:8 * o + 8], T.KB[:, :, 16 * o], ["KB"], ["KL"])
         for c in range(16):
             s = slice(64 * c, 64 * c + 64)
             ts(T.OHC[:, s], T.IO64[:], T.B5[:, c:c + 1], OP.is_equal, ["IO64", "B5"], [("OHC", c)],
@@ -424,22 +441,27 @@ def rank_program(g, core, T, topo):
             rd = [("OHX", c), ("OHC", c)]
             mm(T.B6[0:64, 0:64], T.OHX[:, s], T.OHC[:, s], c == 0, False, rd, ["B6"])
             mm(T.B6[0:64, 0:64], T.OHC[:, s], T.OHX[:, s], False, c == 15, rd, ["B6"])
-        tr(T.KC[:], T.B4[:, 8:16, :], [("B4", 1)], ["KC"])
+        cp(T.CI[:], T.B2[:, 0:16], ["B2"], ["CI"])
+        tr(T.KB[:], T.B4[:, 0:8, :], ["B4"], ["KB"])
         cp(T.TB[0:64, :], T.B6[0:64, 0:64], ["B6"], ["TB"])
+        for o in range(2):
+            act(T.KL[:, 8 * o:8 * o + 8], T.KB[:, :, 16 * o], ["KB"], ["KL"])
         for r in range(4):
             mm(T.B6[:, 256 + 64 * r:320 + 64 * r], T.RX[0:64, 128 * r:128 * r + 128], T.TB[0:64, :], True, True, ["RX", "TB"], ["B6"])
-        for h in range(2):
-            cp(T.CI[:, 8 * h:8 * h + 8], T.KC[:, 16 * h::32], ["KC"], [("CI", h)])
         mm(T.B7[:, 0:256], T.ID[:], TX[:], True, False, ["ID", X], ["B7"])
         mm(T.B7[:, 0:256], T.IDN[:], T.FX[:], False, False, ["IDN", "FX"], ["B7"])
         mm(T.B7[:, 0:256], T.ID[:], T.FC[:], False, False, ["ID", "FC"], ["B7"])
         mm(T.B0[:, 0:8, :], T.BO[:], T.FH[:], True, False, ["BO", "FH"], ["B0"])
         mm(T.B0[:, 0:8, :], T.ID128[:], T.NH[:], False, False, ["ID128", "NH"], ["B0"])
         mm(T.B3[:, 0:256], T.ID[:], T.NH[:], True, False, ["ID", "NH"], ["B3"])
-        ts(T.CI[:], T.CI[:], 255, OP.bitwise_and, [("CI", 0), ("CI", 1)], ["CI"])
-        cp(T.TW[:], T.B6[:, 256:512], ["B6"], ["TW"])
+        ts(T.CI[:], T.CI[:], 255, OP.bitwise_and, ["CI"], ["CI"])
+        chore(2)
         cp(T.CL[:], T.CI[:], ["CI"], ["CL"])
+        chore(1)
+        cp(T.TW[:], T.B6[:, 256:512], ["B6"], ["TW"])
+        chore(1)
         tt(T.GT[:], T.TW[:].indirect(T.CL[:, 0:16]), T.MK[:], OP.mult, ["TW", "CL", "MK"], ["GT"])
+        chore(2)
         mm(T.B7[:, 0:256], T.BO64[:], T.GT[:], False, True, ["BO64", "GT"], ["B7"])
         mm(T.B3[:, 0:256], T.BO[:], T.GT[:], False, True, ["BO", "GT"], ["B3"])
         mm(T.B0[:, 0:8, :], T.BO8192[:], T.GT[:], False, True, ["BO8192", "GT"], ["B0"])
@@ -458,6 +480,7 @@ def rank_program(g, core, T, topo):
         for o, a, b in ((1, 0, 0), (256, 16, 0), (257, 16, 16)):
             tt(T.EQ[:, o:o + 255:2], T.KB[:, :, a:a + 16], T.B0[:, 0:8, b:b + 16], OP.is_equal, ["KB", "B0"], ["EQ"])
         mm(T.B2[:, 0:256], T.ID[:], TM[:], True, False, ["ID", M], ["B2"])
+        chore(2)
         tt(T.GD[:], T.DM[:], T.B5[:, 256:512], OP.mult, ["DM", "B5"], ["GD"])
         mm(T.B2[:, 0:256], T.ID[:], T.GD[:], False, True, ["ID", "GD"], ["B2"])
         act(T[mn][:], T.B2[:, 0:256], ["B2"], [mn])

@@ -3,7 +3,11 @@ from concourse.mybir import AluOpType, AxisListType, ActivationFunctionType
 OP = AluOpType
 AF = ActivationFunctionType
 W, K = 4096, 256
-SHARE = (80, 64, 64)
+BOTH = (6, 4)
+HALVES = True
+ONE = False
+SHARE = (64, 64, 64)
+ORDER = (0, 3, 1, 2)
 
 _S = {}
 
@@ -20,73 +24,60 @@ for _n in ("MG", "MP"):
     _sb(_n, 128, "float32")
 _sb("PI", 4, "int32")
 _sb("PF", 16, "float32")
-for _n in ("THR", "T3", "VA", "VB", "PC", "PD"):
+for _n in ("THR", "T3", "PC", "PD"):
     _sb(_n, 4, "float32")
 _sb("WI", 2, "int32")
 _sb("WF", 2, "float32")
 _sb("THI", 1, "int32")
 _sb("THF", 1, "float32")
 for _n in ("BO", "BO64", "BO8192", "ID", "IDN", "ID128", "SL", "MNE", "BOX", "W1", "W2", "W32", "LT0", "LT1", "LT2", "CN",
-           "C5120", "IDN4096"):
+           "C5120", "IDN4096", "ZERO"):
     _sb(_n, 128)
 _sb("ONES", 512)
 for _n in ("THB", "B15", "BNA"):
     _sb(_n, 8, "float16")
 for _n in range(4):
     _sb("PM%d" % _n, 128, "float16")
+    _sb("PN%d" % _n, 128, "float16")
 _sb("SK", 2048)
 _sb("RX", 512)
 _sb("IO64", 64)
+_sb("NUM", 256)
 for _n in ("JI", "RA", "RB", "RC"):
     _sb(_n, 32, "float32")
 for _n in ("RR", "EQ", "SC"):
     _sb(_n, 512)
-_sb("UI", 256, "int32")
-_sb("Q", 256)
+_sb("UI", 512, "int32")
+for _n in ("PR", "ZI", "HI"):
+    _sb(_n, 256, "int32")
 _sb("UP", 128, "float32")
-_sb("QB", 144, "float16")
-_sb("Q64", 144, "float16")
-_sb("PR", 256, "int32")
-_sb("ZI", 256, "int32")
-_sb("HI", 256, "int32")
+_sb("Q", 256)
 _sb("HU", 256, "uint16")
-_sb("H16", 256, "float16")
-_sb("CB", 4096)
-_sb("EB", 4096)
-_sb("PB", 256)
-_sb("FB", 256, "float16")
+for _n in ("H16", "FB", "FX", "FC", "D16"):
+    _sb(_n, 256, "float16")
+for _n in ("PB", "NH", "XA", "SUB", "ABS", "AQ", "MK", "TW", "GT", "DM", "GD"):
+    _sb(_n, 256)
+_sb("CB", W)
+_sb("EB", W + 32)
 _S["FH"] = ("sbuf", [128, 8, 32], "float16")
-_sb("FX", 256, "float16")
-_sb("FC", 256, "float16")
-_sb("NH", 256)
-_sb("XA", 256)
 _S["KB"] = ("sbuf", [128, 8, 32], "float32")
-_sb("KL", 16, "float32")
-_sb("LF", 16, "uint16")
-_sb("SUB", 256)
-_sb("ABS", 256)
+_sb("KC", 256, "float32")
+_sb("WD", 257, "float32")
+for _n in ("KL", "Y"):
+    _sb(_n, 16, "float32")
+for _n in ("LF", "CL", "OFU"):
+    _sb(_n, 16, "uint16")
+_sb("CI", 16, "int32")
 _sb("OHX", 1024)
 _sb("OHC", 1024)
-_sb("CI", 16, "int32")
-_sb("CL", 16, "uint16")
-_sb("AQ", 256)
-_sb("MK", 256)
+_sb("TA", 64)
 _sb("TB", 64)
-_sb("TW", 256)
-_sb("GT", 256)
-_sb("D16", 256, "float16")
-_sb("DM", 256)
-_sb("GD", 256)
-_sb("Z", 16, "float32")
-_sb("Y", 16, "float32")
-_sb("OFU", 16, "uint16")
-_sb("SUM", 4, "float32")
 _sb("YM", 1, "float32")
 for _i in range(8):
     _S["B%d" % _i] = ("psum", [128, 16, 32] if _i in (0, 4) else [128, 512], "float32")
 SCRATCH = _S
-SEMAPHORES = (["qv", "qs", "qt", "qg", "ls"] + ["d%d" % _i for _i in range(12)]
-              + ["ax%d" % _i for _i in range(1, 4)] + ["am%d" % _i for _i in range(1, 4)])
+SEMAPHORES = (["qv", "qs", "qt", "qg", "ls"] + ["d%d" % _i for _i in range(10)]
+              + [_n + str(_i) for _n in ("ax", "ay", "am") for _i in range(1, 4)])
 
 
 def rank_program(g, core, T, topo):
@@ -98,7 +89,7 @@ def rank_program(g, core, T, topo):
     clock = {q: {} for q in que}
     count = {"qv": 0, "qs": 0, "qt": 0, "qg": 0}
     lastw, readers, touch = {}, {}, {}
-    dmas = []
+    dmas, sent = [], []
 
     def wait(q, tok):
         sem, n, snap = tok[0], tok[1], tok[2]
@@ -174,8 +165,6 @@ def rank_program(g, core, T, topo):
             ins = g.vector.tensor_reduce(**kw)
         elif name == "turn":
             ins = g.vector.transpose(**kw)
-        elif name == "inverse":
-            ins = g.vector.reciprocal(**kw)
         elif name == "scan":
             ins = g.vector.tensor_tensor_scan(**kw)
         ins.then_inc(T.sem[sem], 1)
@@ -188,6 +177,13 @@ def rank_program(g, core, T, topo):
         tok = (sem, 16, dict(clock[q]), "dma")
         dmas.append(tok)
         after(tok, reads, writes)
+
+    def send(dst, out, src, read, write, sem):
+        rid, pid, _eng = topo.addr(dst)
+        before("g", [read], [])
+        g.remote_dma(out, src, T.sem[sem], T.sem.ls, pid, rid, topo.mask(core, dst))
+        lastw[write] = (sem, len(topo.engines(core, dst)), {}, "remote")
+        sent.append(lastw[write])
 
     def cp(out, in_, r, w):
         do("v", r, w, "copy", out=out, in_=in_)
@@ -220,10 +216,17 @@ def rank_program(g, core, T, topo):
         else:
             do("g", [], w, "iota", out=out, pattern=pattern, base=base, channel_multiplier=cm)
 
-    def pick(out, in_, pattern, op, other, r, w):
-        do("g", r, w, "pick", out=out, in_=in_, pattern=pattern, compare_op=op, fill=other, base=0, channel_multiplier=-1)
+    def pick(out, in_, pattern, op, other, r, w, base=0):
+        do("g", r, w, "pick", out=out, in_=in_, pattern=pattern, compare_op=op, fill=other, base=base, channel_multiplier=-1)
 
-    dma("y", T.X0[:], T.xw[:], [], ["X0"])
+    def some(steps, n):
+        for _ in range(n):
+            next(steps, None)
+
+    def half(h):
+        return slice(128 * h, 128 * h + 128)
+
+    dma("y", T.X0[:], T.xw[:], [], [("X0", 0), ("X0", 1)])
     dma("s", T.WI[:], T.wts[:], [], ["WI"])
     dma("y", T.LX[:, 0:W], T.lex[:], [], ["LX"])
     dma("s", T.THI[:], T.th[:], [], ["THI"])
@@ -239,272 +242,297 @@ def rank_program(g, core, T, topo):
     fill(T.CN[:], -65536.0, ["CN"])
     fill(T.C5120[:], 5120.0, ["C5120"])
     cp(T.PF[:, 0:2], T.PI[:, 1:3], ["PI1", "PI2"], ["PF"])
-    fill(T.QB[:], 0.0, ["QB"])
-    fill(T.Q64[:], 0.0, ["Q64"])
+    fill(T.ZERO[:], 0.0, ["ZERO"])
     pG, pL = T.PF[:, 0:1], T.PF[:, 1:2]
     pick(T.ID[:], T.ONES[:, 0:128], col, OP.is_equal, 0.0, ["ONES"], ["ID"])
     ts(T.BO[:], T.MG[:], pG, OP.is_equal, ["MG", "PF"], ["BO"])
-    fill(T.SK[:], 0.0, ["SK"])
+    fill(T.SK[:, 0:1024], 0.0, ["SK"])
+    for e in (2, 3):
+        act(T.SK[:, 512 * e:512 * e + 512], T.ONES[:], ["ONES"], ["SK1"], scale=0.0)
     pick(T.MNE[:], T.BO[:], col, OP.not_equal, 0.0, ["BO"], ["MNE"])
     pick(T.BOX[:], T.BO[:], col, OP.not_equal, -15.0, ["BO"], ["BOX"])
+    ts(T.BO64[:], T.BO[:], 64.0, OP.mult, ["BO"], ["BO64"])
+    ts(T.IDN4096[:], T.ID[:], -4096.0, OP.mult, ["ID"], ["IDN4096"])
     iota(T.T3[:], [[1, 4]], 0, 0, ["T3"])
     iota(T.PC[:], [[-1, 2], [100, 2]], 0, 0, ["PC"])
-    iota(T.MP[:], [[2, 4], [100, 2], [0, 16]], 0, 0, ["MP"])
+    iota(T.JI[:], [[1, 16], [-100, 2]], 0, 0, ["JI"])
+    for e in range(8):
+        pick(T.SK[:, 16 * e:16 * e + 129 * 15 + 1:129], T.BOX[:, 16 * e:16 * e + 16], [[0, 16]], OP.is_ge, 0.0, ["BOX", "SK", "SK1"],
+             [("SK", e)], 127)
+    lastw["SK"] = lastw[("SK", 7)]
     pick(T.SL[:], T.BO[:], col, OP.is_gt, 0.0, ["BO"], ["SL"])
-    pick(T.SL[:], T.SL[:], col, OP.not_equal, -1.0, ["SL"], ["SL"])
+
+    def lowest(t):
+        nm = "LT%d" % t
+        pick(T[nm][:], T.SL[:], col, OP.not_equal, -1.0, ["SL"], [nm])
+        for src, op, other, base in (("BO64", OP.is_gt, 1.0, t), (None, OP.is_ge, 0.0, 15), (None, OP.not_equal, -16.0, t)):
+            pick(T[nm][:, t::16], T[src][:, ::16] if src else T[nm][:, t::16], [[16, 8]], op, other, [nm, "BO64"], [nm], base)
+    lowest(0)
+    iota(T.MP[:], [[2, 4], [100, 2], [0, 16]], 0, 0, ["MP"])
     iota(T.IO64[:], [[1, 64]], 0, 0, ["IO64"])
-    iota(T.JI[:], [[1, 16], [100, 2]], -100, 0, ["JI"])
     pick(T.RX[:], T.ONES[:], [[1, 4], [0, 8], [4, 16]], OP.is_equal, 0.0, ["ONES"], ["RX"])
+    lowest(1)
+    lowest(2)
+    iota(T.NUM[:], [[-1, 256]], -1, 0, ["NUM"])
     cp(T.WF[:], T.WI[:], ["WI"], ["WF"])
+    ts(T.ID128[:], T.ID[:], 128.0, OP.mult, ["ID"], ["ID128"])
     ts(T.W1[:], T.MNE[:], T.WF[:, 0:1], OP.mult, ["MNE", "WF"], ["W1"])
     ts(T.W2[:], T.MNE[:], T.WF[:, 1:2], OP.mult, ["MNE", "WF"], ["W2"])
     ts(T.W32[:], T.MNE[:], T.WF[:, 0:1], OP.mult, ["MNE", "WF"], ["W32"], 32.0, OP.mult)
-    for nm, src, f in (("IDN4096", "ID", -4096.0), ("IDN", "ID", -1.0), ("ID128", "ID", 128.0)):
-        act(T[nm][:], T[src][:], [src], [nm], scale=f)
+    ts(T.IDN[:], T.ID[:], -1.0, OP.mult, ["ID"], ["IDN"])
+    ts(T.BO8192[:], T.BO[:], 8192.0, OP.mult, ["BO"], ["BO8192"])
+    ts(T.B15[:], T.BO[:, ::16], 1.5, OP.mult, ["BO"], ["B15"])
+    ts(T.BNA[:], T.BO[:, ::16], -1.0 / 4096, OP.mult, ["BO"], ["BNA"])
+    ts(T.PF[:, 8:9], pL, -4.0, OP.mult, ["PF"], ["SQB"], -1.5, OP.add)
 
-    def later_constants():
-        for nm, src, f in (("BO64", "BO", 64.0), ("BO8192", "BO", 8192.0)):
-            act(T[nm][:], T[src][:], [src], [nm], scale=f)
-        act(T.B15[:], T.BO[:, ::16], ["BO"], ["B15"], scale=1.5)
-        act(T.BNA[:], T.BO[:, ::16], ["BO"], ["BNA"], scale=-1.0 / 4096)
-        for e in range(8):
-            cp(T.SK[:, 16 * e:16 * e + 129 * 15 + 1:129], T.BOX[:, 16 * e:16 * e + 16], ["BOX", "SK"], [("SK", e)])
-        lastw["SK"] = lastw[("SK", 7)]
-        ts(T.VA[:], T.T3[:], pL, OP.is_gt, ["T3", "PF"], ["VA"], 31.0, OP.mult)
-        ts(T.VB[:], T.T3[:], pL, OP.is_equal, ["T3", "PF"], ["VB"], -17.0, OP.mult)
-        ts(T.PD[:], T.PC[:], pG, OP.add, ["PC", "PF"], ["PD"])
-        ts(T.THR[:], T.T3[:], pL, OP.not_equal, ["T3", "PF"], ["THR"], -0.5, OP.mult)
-        tt(T.VA[:], T.VA[:], T.VB[:], OP.add, ["VA", "VB"], ["VA"])
-        ts(T.THF[:], T.THI[:], -2048.0, OP.add, ["THI"], ["THF"], 1.0 / 4096, OP.mult)
-        ts(T.PF[:, 8:9], pL, -4.0, OP.mult, ["PF"], ["SQB"], -1.5, OP.add)
-        ts(T.VA[:], T.VA[:], 1.0, OP.add, ["VA"], ["VA"])
-        for t in range(3):
-            act(T["LT%d" % t][:], T.SL[:], ["SL"], ["LT%d" % t])
-        cp(T.QB[:, 15:128:16], T.BO[:, ::16], ["BO", "QB"], ["QB"])
-        ts(T.Q64[:, 15:128:16], T.BO[:, ::16], 64.0, OP.mult, ["BO", "Q64"], ["Q64"])
-        ts(T.THB[:], T.BO[:, ::16], T.THF[:], OP.mult, ["BO", "THF"], ["THB"])
-        for t in range(3):
-            nm = "LT%d" % t
-            ts(T[nm][:, t::16], T.BO[:, ::16], T.VA[:, t:t + 1], OP.mult, ["BO", "VA", nm], [nm])
-
-    def scan_constants():
-        for i in range(4):
-            yield ts(T["PM%d" % i][:], T.MP[:], T.PD[:, i:i + 1], OP.is_equal, ["MP", "PD"], ["PM%d" % i])
-        yield ts(T.PF[:, 9:10], pL, 15.0, OP.is_lt, ["PF"], ["PF9"], 255.0, OP.mult)
-        yield ts(T.RA[:], T.JI[:], pL, OP.is_ge, ["JI", "PF"], ["RA"], 257.0, OP.mult)
-        yield ts(T.PF[:, 11:12], pL, float(W), OP.add, ["PF"], ["SPARE"])
-        yield ts(T.RC[:], T.JI[:], pL, OP.is_equal, ["JI", "PF", "PF9"], ["RC"], T.PF[:, 9:10], OP.mult)
-        yield ts(T.PF[:, 12:13], pL, float(W + 16), OP.add, ["PF"], ["SPARE"])
+    def last_constants():
+        yield ts(T.RC[:], T.JI[:], pL, OP.is_equal, ["JI", "PF"], ["RC"], -2.0, OP.mult)
+        yield ts(T.RA[:], T.JI[:], pL, OP.is_gt, ["JI", "PF"], ["RA"], 2.0 ** -16 - 1, OP.mult)
+        yield ts(T.RB[:], T.JI[:], pL, OP.is_gt, ["JI", "PF"], ["RB"], 2.0 ** 16 - 1, OP.mult)
+        yield ts(T.RC[:], T.RC[:], 1.0, OP.add, ["RC"], ["RC"])
+        yield ts(T.PD[:], T.PC[:], pG, OP.add, ["PC", "PF"], ["PD"])
         yield fill(T.RR[:, 0:1], 0.0, ["RR0"])
         yield tt(T.RA[:], T.RA[:], T.RC[:], OP.add, ["RA", "RC"], ["RA"])
-        yield fill(T.EQ[:, 0:256:2], 0.0, ["EQ0"])
-        yield ts(T.RA[:], T.RA[:], -256.0, OP.add, ["RA"], ["RA"])
-        yield ts(T.PF[:, 10:11], T.PF[:, 9:10], 0.5, OP.mult, ["PF9"], ["WIN"], 0.5, OP.add)
-        yield do("v", ["RA"], ["RB"], "inverse", out=T.RB[:], in_=T.RA[:])
-        yield tt(T.RR[:, 1:32], T.RA[:, 0:31], T.RB[:, 1:32], OP.mult, ["RA", "RB"], ["RR"])
+        yield tt(T.RB[:], T.RB[:], T.RC[:], OP.add, ["RB", "RC"], ["RB"])
+        yield ts(T.THR[:], T.T3[:], pL, OP.not_equal, ["T3", "PF"], ["THR"], -0.5, OP.mult)
+        yield ts(T.THF[:], T.THI[:], -2048.0, OP.add, ["THI"], ["THF"], 1.0 / 4096, OP.mult)
+        tt(T.RR[:, 1:32], T.RA[:, 0:31], T.RB[:, 1:32], OP.mult, ["RA", "RB"], ["RR"])
         for n in (32, 64, 128, 256):
-            yield cp(T.RR[:, n:2 * n], T.RR[:, 0:n], ["RR", "RR0"], ["RR"])
+            pick(T.RR[:, n:2 * n], T.RR[:, 0:n], [[0, n]], OP.is_ge, 0.0, ["RR", "RR0"], ["RR"], 127)
+        yield
+        for i in range(4):
+            yield ts(T["PM%d" % i][:], T.MP[:], T.PD[:, i:i + 1], OP.is_equal, ["MP", "PD"], ["PM%d" % i])
+        yield ts(T.THB[:], T.BO[:, ::16], T.THF[:], OP.mult, ["BO", "THF"], ["THB"])
+        for i in range(4):
+            yield ts(T["PN%d" % i][:], T["PM%d" % i][:], 64.0, OP.mult, ["PM%d" % i], ["PN%d" % i])
+        yield ts(T.PF[:, 11:12], pL, float(W), OP.add, ["PF"], ["SPARE"])
+        yield ts(T.PF[:, 12:13], pL, float(W + 16), OP.add, ["PF"], ["SPARE"])
+        yield fill(T.EQ[:, 1:256:2], 0.0, ["EQ0"])
 
-    chores = scan_constants()
+    chores = last_constants()
 
-    def chore(n):
-        for _ in range(n):
-            next(chores, None)
-
-    def turned():
-        for s in range(2):
-            for c in range(2):
-                nm = "PM%d" % (2 * s + c)
-                mm(T.B4[:, 0:8, 16 * s:16 * s + 16], T[nm][:], T.FH[:, :, 16 * c:16 * c + 16], c == 0, c == 1, [nm, "FH"], ["B4"])
-
-    def listed(q, src, first):
-        for p in range(16):
-            mm(T.B2[:, 0:16], T[q][:, 15 - p:143 - p], T[src][:, p::16], first and p == 0, p == 15 and not first, [q, src], ["B2"])
-
-    def scatter(pairs):
+    def scatter(lex, src):
         for c in range(7, -1, -1):
-            for lex, src in pairs:
-                cp(T[lex][:].indirect(T.OFU[:, 2 * c:2 * c + 2]), T[src][:, 32 * c:32 * c + 32], ["OFU", src, lex], [lex])
+            yield cp(T[lex][:].indirect(T.OFU[:, 2 * c:2 * c + 2]), T[src][:, 32 * c:32 * c + 32], ["OFU", lex, src], [lex])
 
-    for t in range(3):
-        xn, mn = "XN%d" % t, "MN%d" % t
-        X, M = "X%d" % t, "M%d" % t
-        TX, TM = T[X], T[M]
-        mm(T.B6[:, 0:256], T.CN[:], T.ONES[:, 0:256], True, False, ["CN", "ONES"], [("B6", "Z")])
+    ZB = ("B4", "B0")
+
+    def hash_sums(X):
+        TX = T[X]
+        for b in ZB:
+            mm(T[b][:, 0:4, :], T.CN[:], T.ONES[:, 0:128], True, False, ["CN", "ONES"], [b])
         mm(T.B3[:, 0:256], T.C5120[:], T.ONES[:, 0:256], True, False, ["C5120", "ONES"], ["B3"])
 
         def sums(b, o, w0, n, alone):
             for j, w in ((0, "W1"), (1, "W2")):
-                mm(T[b][:, o + n * j:o + n * j + n], T[w][:], TX[:, w0:w0 + n], alone, alone, [w, X], [b])
+                mm(T[b][:, o + n * j:o + n * j + n], T[w][:], TX[:, w0:w0 + n], alone, alone, [w, (X, w0 // 128)], [b])
+
+        def times32(h):
+            mm(T[ZB[h]][:, 0:4, :], T.W32[:], TX[:, half(h)], False, True, ["W32", (X, h)], [ZB[h]])
         sums("B7", 0, 0, 64, True)
         sums("B7", 128, 64, 64, True)
+        times32(0)
         sums("B5", 0, 128, 128, True)
-        mm(T.B6[:, 0:256], T.W32[:], TX[:], False, True, ["W32", X], [("B6", "Z")])
         sums("B3", 0, 128, 128, False)
         act(T.Q[:], T.B5[:, 0:256], ["B5"], ["Q"], func=AF.Identity, scale=1.0 / 4096, bias=159.5 + 1.0 / 8192)
-        mm(T.B1[:, 0:256], T.ID[:], TX[:], True, True, ["ID", X], ["B1"])
+        times32(1)
+        mm(T.B1[:, 0:256], T.ID[:], TX[:], True, True, ["ID", (X, 0), (X, 1)], ["B1"])
         mm(T.B3[:, 0:256], T.IDN4096[:], T.Q[:], False, True, ["IDN4096", "Q"], ["B3"])
         act(T.UP[:], T.B3[:, 128:256], ["B3"], ["UP"])
 
-        def hashes(c):
-            s, u = slice(64 * c, 64 * c + 64), slice(128 * c, 128 * c + 128)
-            if c < 2:
-                yield cp(T.UI[:, u], T.B7[:, u], ["B7"], [("UI", c)])
-                yield ts(T.UI[:, u], T.UI[:, u], 4095, OP.bitwise_and, [("UI", c)], [("UI", c)])
-                yield tt(T.PR[:, s], T.UI[:, 128 * c:128 * c + 64], T.UI[:, 128 * c + 64:128 * c + 128], OP.mult, [("UI", c)], [("PR", c)])
-            else:
-                u = slice(64 * c - 128, 64 * c - 64)
-                yield tt(T.PR[:, s], T.UP[:, u], T.B3[:, u], OP.mult, ["UP", "B3"], [("PR", c)])
-            yield tt(T.ZI[:, s], T.PR[:, s], T.B6[:, s], OP.add, [("PR", c), ("B6", "Z")], [("ZI", c)])
-            yield ts(T.HI[:, s], T.ZI[:, s], 5, OP.arith_shift_right, [("ZI", c)], [("HI", c)], 4095, OP.bitwise_and)
-            yield cp(T.HU[:, s], T.HI[:, s], [("HI", c)], [("HU", c)])
+    def hashes(c):
+        s, u, z = slice(64 * c, 64 * c + 64), slice(128 * c, 128 * c + 128), slice(2 * (c % 2), 2 * (c % 2) + 2)
+        if c < 2:
+            yield cp(T.UI[:, u], T.B7[:, u], ["B7"], [("UI", c)])
+            yield ts(T.UI[:, u], T.UI[:, u], 4095, OP.bitwise_and, [("UI", c)], [("UI", c)])
+            yield tt(T.PR[:, s], T.UI[:, 128 * c:128 * c + 64], T.UI[:, 128 * c + 64:128 * c + 128], OP.mult, [("UI", c)], [("PR", c)])
+        else:
+            u = slice(64 * c - 128, 64 * c - 64)
+            yield tt(T.PR[:, s], T.UP[:, u], T.B3[:, u], OP.mult, ["UP", "B3"], [("PR", c)])
+        yield tt(T.ZI[:, s], T.PR[:, s], T[ZB[c // 2]][:, z, :], OP.add, [("PR", c), ZB[c // 2]], [("ZI", c)])
+        yield ts(T.HI[:, s], T.ZI[:, s], 5, OP.arith_shift_right, [("ZI", c)], [("HI", c)], 4095, OP.bitwise_and)
+        yield cp(T.HU[:, s], T.HI[:, s], [("HI", c)], [("HU", c)])
 
-        def gather(how, w0, w1, key):
-            how(T.CB[:, 16 * w0:16 * w1], T.LX[:, 0:W].indirect(T.HU[:, w0:w1]), ["LX", ("HU", w0 // 64)], [key])
+    hash_sums("X0")
+    some(zip(hashes(0), hashes(1)), 6)
+    some(chores, 8)
+    late = iter(())
+
+    for t in range(3):
+        xn, mn = "XN%d" % t, "MN%d" % t
+        X, M, X1, M1 = "X%d" % t, "M%d" % t, "X%d" % (t + 1), "M%d" % (t + 1)
+        TX, TM = T[X], T[M]
+        dst = T.cores[(rank + (3 if t < 2 else 2)) % n_ranks]
 
         def compare(c):
             o = 1024 * c
             for k in range(16):
                 tt(T.EB[:, o + 64 * k:o + 64 * k + 64], T.CB[:, o + k:o + 1024:16], T.B1[:, 64 * c:64 * c + 64], OP.not_equal,
-                   [("CB", c), ("CB", c, "v"), "B1"], [("EB", c, k // 2)])
+                   [("CB", c), "CBV", "B1"], [("EB", c, k // 2)])
                 if k % 2 == 1:
                     for j in (k - 1, k):
-                        mm(T.B2[:, 64 * c:64 * c + 64], T.SK[:, 128 * j:128 * j + 128], T.EB[:, o + 64 * j:o + 64 * j + 64],
-                           j == 0, j == 15, ["SK", ("EB", c, j // 2)], ["B2"])
+                        mm(T.B2[:, 64 * c:64 * c + 64], T.SK[:, 128 * j:128 * j + 128],
+                           T.EB[:, o + 64 * j:o + 64 * j + 64], j == 0, j == 15, ["SK", ("EB", c, j // 2)], ["B2"])
 
-        for c in (0, 2):
-            for _ in zip(hashes(c), hashes(c + 1)):
-                pass
-        if t == 0:
-            later_constants()
-        share = SHARE[t]
+        for i, _ in enumerate(zip(hashes(2), hashes(3))):
+            some(chores, i < 3)
+        def gather(how, w0, w1, key):
+            how(T.CB[:, 16 * w0:16 * w1], T.LX[:, 0:W].indirect(T.HU[:, w0:w1]), ["LX", ("HU", w0 // 64)], [key])
         for c in range(3):
-            gather(act, 64 * c, min(64 * c + 64, 256 - share), ("CB", c))
+            gather(act, 64 * c, min(64 * c + 64, 256 - SHARE[t]), ("CB", c))
         gather(cp, 192, 256, ("CB", 3))
-        if share > 64:
-            gather(cp, 256 - share, 192, ("CB", 2, "v"))
+        if SHARE[t] > 64:
+            gather(cp, 256 - SHARE[t], 192, "CBV")
         ts(T.H16[:], T.HU[:], -2048.0, OP.add, [("HU", c) for c in range(4)], ["H16"])
         mm(T.B6[:, 256:512], T.ID[:], T.H16[:], True, True, ["ID", "H16"], [("B6", "H")])
-        for c in (0, 3, 1, 2):
+        for c in ORDER:
             compare(c)
         ts(T.PB[:], T.B2[:, 0:256], -11.5, OP.is_le, ["B2"], ["PB"])
         lt = "LT%d" % t
         mm(T.B2[:, 256:512], T[lt][:], T.PB[:], True, True, [lt, "PB"], ["B2"])
         mm(T.B3[:, 0:256], T.BO[:], T.PB[:], True, True, ["BO", "PB"], ["B3"])
-        chore(4)
+        some(late, 2)
+        some(chores, 4)
         ts(T.FB[:], T.B2[:, 256:512], T.THR[:, t:t + 1], OP.is_le, ["B2", "THR"], ["FB"])
         act(T.NH[:], T.B3[:, 0:256], ["B3"], ["NH"], func=AF.Relu, scale=-128.0, bias=64.0)
-        chore(2)
+        some(late, 1)
+        some(chores, 2)
         tt(T.FH[:], T.FB[:], T.B6[:, 256:512], OP.mult, ["FB", ("B6", "H")], ["FH"])
-        for p in range(16):
-            mm(T.B5[:, 0:16], T.QB[:, 15 - p:143 - p], T.FH[:, :, p::16], p == 0, p == 15, ["QB", "FH"], ["B5"])
+        for i in range(4):
+            s, c = i // 2, i % 2
+            mm(T.B4[:, 0:8, 16 * s:16 * s + 16], T["PM%d" % i][:], T.FH[:, :, 16 * c:16 * c + 16], c == 0, c == 1,
+               ["PM%d" % i, "FH"], ["B4"])
         tt(T.FX[:], T.FB[:], T.B1[:, 0:256], OP.mult, ["FB", "B1"], ["FX"])
         for h in range(2):
-            s = slice(128 * h, 128 * h + 128)
-            mm(T.B3[:, 256 + 8 * h:264 + 8 * h], T.FX[:, s], T.BO[:, ::16], True, False, ["FX", "BO"], ["B3"])
-            mm(T.B3[:, 256 + 8 * h:264 + 8 * h], T.NH[:, s], T.BO[:, ::16], False, True, ["NH", "BO"], ["B3"])
-        chore(6)
-        ts(T.LF[:], T.B5[:, 0:16], 2048.0, OP.add, ["B5"], ["LF"])
+            mm(T.B3[:, 256 + 8 * h:264 + 8 * h], T.FX[:, half(h)], T.BO[:, ::16], True, False, ["FX", "BO"], ["B3"])
+            mm(T.B3[:, 256 + 8 * h:264 + 8 * h], T.NH[:, half(h)], T.BO[:, ::16], False, True, ["NH", "BO"], ["B3"])
+        some(late, 8)
+        some(chores, 5)
+        tr(T.KB[:], T.B4[:, 0:8, :], ["B4"], ["KB"])
         mm(T.B7[:, 256:512], T.BO[:], T.FX[:], True, False, ["BO", "FX"], ["B7"])
         mm(T.B7[:, 256:512], T.ID[:], T.NH[:], False, True, ["ID", "NH"], ["B7"])
-        mm(T.B0[:, 8:16, :], T.ID[:], TX[:], True, False, ["ID", X], ["B0"])
-        mm(T.B0[:, 8:16, :], T.ID[:], T.NH[:], False, True, ["ID", "NH"], ["B0"])
-        listed("Q64", "FX", True)
-        turned()
+        mm(T.B2[:, 0:256], T.ID[:], TX[:], True, False, ["ID", X], ["B2"])
+        mm(T.B2[:, 0:256], T.ID[:], T.NH[:], False, True, ["ID", "NH"], ["B2"])
+        mm(T.B4[:, 8:16, :], T.ZERO[:], T.ONES[:, 0:256], True, False, ["ZERO", "ONES"], [("B4", 1)])
+
+        def coded(pm, src):
+            for i in range(4):
+                s, c = i // 2, i % 2
+                mm(T.B4[:, 8:16, 16 * s:16 * s + 16], T[pm + str(i)][:], T[src][:, half(c)], False, src == "FC" and i == 3,
+                   [pm + str(i), src], [("B4", 1)])
 
         def hot_x(c0, c1):
             for c in range(c0, c1):
                 ts(T.OHX[:, 64 * c:64 * c + 64], T.IO64[:], T.B3[:, 256 + c:257 + c], OP.is_equal, ["IO64", "B3"], [("OHX", c)])
+        coded("PN", "FX")
+        mm(T.B0[:, 0:8, :], T.BO[:], T.FH[:], True, False, ["BO", "FH"], ["B0"])
+        mm(T.B0[:, 0:8, :], T.ID128[:], T.NH[:], False, False, ["ID128", "NH"], ["B0"])
         hot_x(0, 2)
-        tt(T.SUB[:], T.LM[:, 0:W].indirect(T.LF[:, 0:16]), TM[:], OP.subtract, ["LM", "LF", M], ["SUB"])
-        act(T.AQ[:], T.B7[:, 256:512], ["B7", "SQB"], ["AQ"], func=AF.Abs, bias=T.PF[:, 8:9])
+        ts(T.LF[:], T.KB[:, :, ::16], 2048.0, OP.add, ["KB"], ["LF"])
+        hot_x(2, 4)
+        tt(T.SUB[:], T.LM[:, 0:W].indirect(T.LF[:, 0:16]), TM[:], OP.subtract, ["LM", M, "LF"], ["SUB"])
         act(T.ABS[:], T.SUB[:], ["SUB"], ["ABS"], func=AF.Abs)
+        act(T.AQ[:], T.B7[:, 256:512], ["B7", "SQB"], ["AQ"], func=AF.Abs, bias=T.PF[:, 8:9])
         tt(T.FC[:], T.LX[:, 0:W].indirect(T.LF[:, 0:16]), T.FB[:], OP.mult, ["LX", "LF", "FB"], ["FC"])
-        hot_x(2, 16)
+        hot_x(4, 16)
         for h in range(2):
-            s = slice(128 * h, 128 * h + 128)
+            mm(T.B5[:, 8 * h:8 * h + 8], T.FC[:, half(h)], T.BO[:, ::16], True, True, ["FC", "BO"], ["B5"])
+        for h in range(2):
             o = T.B5[:, 16 + 8 * h:24 + 8 * h]
-            mm(o, T.FB[:, s], T.THB[:], True, False, ["FB", "THB"], ["B5"])
-            mm(o, T.FB[:, s], T.B15[:], False, False, ["FB", "B15"], ["B5"])
-            mm(o, T.ABS[:, s], T.BNA[:], False, True, ["ABS", "BNA"], ["B5"])
-        for h in range(2):
-            mm(T.B5[:, 8 * h:8 * h + 8], T.FC[:, 128 * h:128 * h + 128], T.BO[:, ::16], True, True, ["FC", "BO"], ["B5"])
-        listed("QB", "FC", False)
+            for i, (src, w) in enumerate((("FB", "THB"), ("FB", "B15"), ("ABS", "BNA"))):
+                mm(o, T[src][:, half(h)], T[w][:], i == 0, i == 2, [src, w], ["B5"])
+        coded("PM", "FC")
+        act(T.XA[:], T.B2[:, 0:256], ["B2"], ["XA"])
         act(T.MK[:], T.AQ[:], ["AQ"], ["MK"], func=AF.Relu, scale=-2.0, bias=4.0)
-        act(T.XA[:], T.B0[:, 8:16, :], ["B0"], ["XA"])
         act(T.D16[:], T.SUB[:], ["SUB"], ["D16"], func=AF.Identity, scale=0.5, bias=1535.75)
         act(T.DM[:], T.D16[:], ["D16"], ["DM"], func=AF.Identity, bias=-1536.0)
         for c in range(16):
             s = slice(64 * c, 64 * c + 64)
-            ts(T.OHC[:, s], T.IO64[:], T.B5[:, c:c + 1], OP.is_equal, ["IO64", "B5"], [("OHC", c)],
-               T.B5[:, 16 + c:17 + c], OP.is_ge)
+            ts(T.OHC[:, s], T.IO64[:], T.B5[:, c:c + 1], OP.is_equal, ["IO64", "B5"], [("OHC", c)], T.B5[:, 16 + c:17 + c], OP.is_ge)
             rd = [("OHX", c), ("OHC", c)]
+            if ONE:
+                mm(T.B7[0:64, 0:64], T.OHX[:, s], T.OHC[:, s], c == 0, c == 15, rd, ["B7"])
+                continue
             mm(T.B6[0:64, 0:64], T.OHX[:, s], T.OHC[:, s], c == 0, False, rd, ["B6"])
             mm(T.B6[0:64, 0:64], T.OHC[:, s], T.OHX[:, s], False, c == 15, rd, ["B6"])
-        cp(T.CI[:], T.B2[:, 0:16], ["B2"], ["CI"])
-        tr(T.KB[:], T.B4[:, 0:8, :], ["B4"], ["KB"])
-        cp(T.TB[0:64, :], T.B6[0:64, 0:64], ["B6"], ["TB"])
+        tr(T.KC[:], T.B4[:, 8:16, :], [("B4", 1)], ["KC"])
+        if ONE:
+            cp(T.TA[0:64, :], T.B7[0:64, 0:64], ["B7"], ["TA"])
+            mm(T.B6[0:64, 0:64], T.TA[0:64, :], T.ID[0:64, 0:64], True, False, ["TA", "ID"], ["B6"])
+            mm(T.B6[0:64, 0:64], T.ID[0:64, 0:64], T.TA[0:64, :], False, True, ["TA", "ID"], ["B6"])
         for o in range(2):
-            act(T.KL[:, 8 * o:8 * o + 8], T.KB[:, :, 16 * o], ["KB"], ["KL"])
+            act(T.KL[:, 8 * o:8 * o + 8], T.KB[:, :, 16 * o], ["KB"], ["KL"], func=AF.Identity, scale=1.0 / 8192, bias=1.25)
+        some(chores, 2)
+        for h in range(2):
+            cp(T.CI[:, 8 * h:8 * h + 8], T.KC[:, 16 * h::32], ["KC"], ["CI"])
+        cp(T.TB[0:64, :], T.B6[0:64, 0:64], ["B6"], ["TB"])
         for r in range(4):
             mm(T.B6[:, 256 + 64 * r:320 + 64 * r], T.RX[0:64, 128 * r:128 * r + 128], T.TB[0:64, :], True, True, ["RX", "TB"], ["B6"])
-        mm(T.B7[:, 0:256], T.ID[:], TX[:], True, False, ["ID", X], ["B7"])
-        mm(T.B7[:, 0:256], T.IDN[:], T.FX[:], False, False, ["IDN", "FX"], ["B7"])
-        mm(T.B7[:, 0:256], T.ID[:], T.FC[:], False, False, ["ID", "FC"], ["B7"])
-        mm(T.B0[:, 0:8, :], T.BO[:], T.FH[:], True, False, ["BO", "FH"], ["B0"])
-        mm(T.B0[:, 0:8, :], T.ID128[:], T.NH[:], False, False, ["ID128", "NH"], ["B0"])
+        for i, (l, src) in enumerate((("ID", X), ("IDN", "FX"), ("ID", "FC"))):
+            mm(T.B1[:, 256:512], T[l][:], T[src][:], i == 0, False, [l, src], ["B1"])
         mm(T.B3[:, 0:256], T.ID[:], T.NH[:], True, False, ["ID", "NH"], ["B3"])
         ts(T.CI[:], T.CI[:], 255, OP.bitwise_and, ["CI"], ["CI"])
-        chore(2)
+        some(chores, 3)
         cp(T.CL[:], T.CI[:], ["CI"], ["CL"])
-        chore(1)
         cp(T.TW[:], T.B6[:, 256:512], ["B6"], ["TW"])
-        chore(1)
         tt(T.GT[:], T.TW[:].indirect(T.CL[:, 0:16]), T.MK[:], OP.mult, ["TW", "CL", "MK"], ["GT"])
-        chore(2)
-        mm(T.B7[:, 0:256], T.BO64[:], T.GT[:], False, True, ["BO64", "GT"], ["B7"])
-        mm(T.B3[:, 0:256], T.BO[:], T.GT[:], False, True, ["BO", "GT"], ["B3"])
-        mm(T.B0[:, 0:8, :], T.BO8192[:], T.GT[:], False, True, ["BO8192", "GT"], ["B0"])
-        tt(T[xn][:], T.XA[:], T.B7[:, 0:256], OP.min, ["XA", "B7"], [xn])
-        act(T.B5[:, 256:512], T.B3[:, 0:256], ["B3"], ["B5"], func=AF.Relu, scale=-1.0, bias=1.0)
-        dst = T.cores[(rank + (3 if t < 2 else 2)) % n_ranks]
-        rid, pid, _eng = topo.addr(dst)
-        mask = topo.mask(core, dst)
-        ne = len(topo.engines(core, dst))
+        ends = [(T.B1[:, 256:512], "BO64", "B1"), (T.B0[:, 0:8, :], "BO8192", "B0"), (T.B3[:, 0:256], "BO", "B3")]
+        for o, l, b in ends if t < 2 else [ends[1], ends[0], ends[2]]:
+            mm(o, T[l][:], T.GT[:], False, True, [l, "GT"], [b])
 
-        def send(out, src, sem):
-            before("g", [src], [])
-            g.remote_dma(T[out][:], T[src][:], T.sem[sem], T.sem.ls, pid, rid, mask)
-            lastw[out] = (sem, ne, {}, "remote")
-        send("X%d" % (t + 1), xn, "ax%d" % (t + 1))
-        for o, a, b in ((1, 0, 0), (256, 16, 0), (257, 16, 16)):
-            tt(T.EQ[:, o:o + 255:2], T.KB[:, :, a:a + 16], T.B0[:, 0:8, b:b + 16], OP.is_equal, ["KB", "B0"], ["EQ"])
+        def equal():
+            for o, a, b in ((0, 0, 0), (256, 16, 16), (257, 16, 0)):
+                tt(T.EQ[:, o:o + 255:2], T.KB[:, :, a:a + 16], T.B0[:, 0:8, b:b + 16], OP.is_equal, ["KB", "B0"], ["EQ"])
+        if t == 2:
+            equal()
+        tt(T[xn][:], T.XA[:], T.B1[:, 256:512], OP.min, ["XA", "B1"], [xn])
+        if HALVES and t < 2:
+            for h in range(2):
+                send(dst, T[X1][:, half(h)], T[xn][:, half(h)], xn, (X1, h), ("ax", "ay")[h] + str(t + 1))
+        else:
+            send(dst, T[X1][:], T[xn][:], xn, (X1, 0), "ax" + str(t + 1))
+            lastw[(X1, 1)] = lastw[(X1, 0)]
+        act(T.B5[:, 256:512], T.B3[:, 0:256], ["B3"], ["B5"], func=AF.Relu, scale=-1.0, bias=1.0)
+        if t < 2:
+            equal()
+        do("v", ["RR", "EQ", "EQ0"], ["SC"], "scan", out=T.SC[:], data0=T.RR[:], data1=T.EQ[:], initial=0.0, op0=OP.mult, op1=OP.add)
         mm(T.B2[:, 0:256], T.ID[:], TM[:], True, False, ["ID", M], ["B2"])
-        chore(2)
+        for j in range(3 if t == 2 else 0):
+            mm(T.B6[:], T.ID[:], T.LM[:, 512 * j:512 * j + 512], j == 0, False, ["ID", "LM"], ["B6"])
         tt(T.GD[:], T.DM[:], T.B5[:, 256:512], OP.mult, ["DM", "B5"], ["GD"])
         mm(T.B2[:, 0:256], T.ID[:], T.GD[:], False, True, ["ID", "GD"], ["B2"])
         act(T[mn][:], T.B2[:, 0:256], ["B2"], [mn])
-        send("M%d" % (t + 1), mn, "am%d" % (t + 1))
-        do("v", ["RR", "EQ", "EQ0"], ["SC"], "scan", out=T.SC[:], data0=T.RR[:], data1=T.EQ[:], initial=0.0, op0=OP.mult, op1=OP.add)
-        ts(T.Z[:], T.SC[:, 31::32], T.PF[:, 10:11], OP.is_lt, ["SC", "WIN"], ["Z"], 8192.0, OP.mult)
-        tt(T.Y[:], T.Z[:], T.KL[:], OP.add, ["Z", "KL"], ["Y"])
+        tt(T.Y[:], T.SC[:, 31::32], T.KL[:], OP.add, ["SC", "KL"], ["Y"])
         for o in range(2):
-            ts(T.OFU[:, o::2], T.Y[:, 8 * o:8 * o + 8], 2048.0, OP.add, ["Y", "SPARE"], ["OFU"], T.PF[:, 11 + o:12 + o], OP.min)
-        scatter([("LX", xn), ("LM", mn)])
+            ts(T.OFU[:, o::2], T.Y[:, 8 * o:8 * o + 8], 8192.0, OP.mult, ["Y", "SPARE"], ["OFU"], T.PF[:, 11 + o:12 + o], OP.min)
+        letters, late = scatter("LX", xn), scatter("LM", mn)
+        if t < 2:
+            hash_sums(X1)
+            before("g", [(X1, 0), (X1, 1)], [])
+            send(dst, T[M1][:], T[mn][:], mn, M1, "am" + str(t + 1))
+            some(letters, 2)
+            some(zip(late, letters), BOTH[t])
+            for _ in zip(hashes(0), hashes(1)):
+                next(letters, None)
 
+    numbers = scatter("EB", "NUM")
+    send(dst, T[M1][:], T[mn][:], mn, M1, "am3")
+    for j in range(3, 8):
+        mm(T.B6[:], T.ID[:], T.LM[:, 512 * j:512 * j + 512], False, j == 7, ["ID", "LM"], ["B6"])
+    for i, (l, src) in enumerate((("IDN", "SUB"), ("ID", "DM"))):
+        mm(T.B7[:, 0:256], T[l][:], T[src][:], i == 0, i == 1, [l, src], ["B7"])
+    act(T.B6[:], T.B6[:], ["B6"], ["B6", "B3"], accum_out=T.B3[:, 256:257])
+    dma("s", T.yx[:], T.X3[:], [("X3", 0), ("X3", 1)], ["yx"])
+    some(zip(numbers, letters), 8)
     dma("y", T.yl[:], T.LX[:, 0:W], ["LX"], ["yl"])
-    act(T.CB[:, 0:2048], T.LM[:, 2048:4096], ["LM"], [("CB", 0), ("CB", 1)], accum_out=T.SUM[:, 1:2])
-    lastw["SUM1"] = lastw[("CB", 0)]
-    do("v", ["LM"], ["SUM0"], "reduce", out=T.SUM[:, 0:1], in_=T.LM[:, 0:2048], axis=AxisListType.X, op=OP.add)
-    tt(T.YM[:], T.SUM[:, 0:1], T.SUM[:, 1:2], OP.add, ["SUM0", "SUM1"], ["YM"])
-    dma("y", T.yx[:], T.X3[:], ["X3"], ["yx"])
-    dma("y", T.yg[:], T.M3[:], ["M3"], ["yg"])
+    tt(T.PB[:], T.EB[:, 0:W].indirect(T.LF[:, 0:16]), T.NUM[:], OP.is_equal, ["EB", "NUM", "LF"], ["PB"])
+    cp(T.WD[:, 256:257], T.B3[:, 256:257], ["B3"], ["WD1"])
+    tt(T.WD[:, 0:256], T.PB[:], T.B7[:, 0:256], OP.mult, ["PB", "B7"], ["WD"])
+    do("v", ["WD", "WD1"], ["YM"], "reduce", out=T.YM[:], in_=T.WD[:], axis=AxisListType.X, op=OP.add)
     dma("s", T.ym[:], T.YM[:], ["YM"], ["ym"])
+    dma("s", T.yg[:], T.M3[:], ["M3"], ["yg"])
     for sem in ("qv", "qs", "qt", "qg"):
         wait("g", (sem, count[sem], {}, ""))
-    for tok in dmas:
+    for tok in dmas + sent:
         wait("g", tok)
-    for s in range(1, 4):
-        wait("g", ("ax%d" % s, ne, {}, ""))
-        wait("g", ("am%d" % s, ne, {}, ""))
-    g.wait_ge(T.sem.ls, 6 * ne)
+    g.wait_ge(T.sem.ls, sum(tok[1] for tok in sent))

@@ -1,15 +1,40 @@
+from concourse.bass import DstId, RemoteDMATransfer
 from concourse.mybir import AluOpType, AxisListType, ActivationFunctionType
 
 OP = AluOpType
 AF = ActivationFunctionType
 W, K = 4096, 256
-BOTH = (6, 4)
-HALVES = True
-ONE = False
-SHARE = (64, 64, 64)
-ORDER = (0, 3, 1, 2)
+SHARE = (32, 32, 32)
+CODE_FIRST = True
+CYCLE, GATHER, SCATTER = 0.83, 1.56, 3.8
+COLUMN = 0.5
+CALL = 120
+FAR = 2600
+FARM = 5000
+FARX = 2600
+FARE = 3000
+RELAY = ("am1", "am2")
+FUSED = False
+AHEAD = (1,)
+ISSUE = 200
+LOADM = 7500
+SLOWG = 1.5
+ONV = ()
+WHOLE = ()
+LOADX = 5000
+ZERO = 4
+IDLE = 2
+EARLY = (0, 0)
+LAST = 2600
+ROUNDS = 2
+TRIES = 0
+SOON = (0, 2500, 500)
+STEPS = (1, 0, 3, -2, 8, -6)
+CASES = ((1, 0.85, -50, 250, 0.8, 1), (1, 1.1, 10, 150, 1.1, 1.2), (1.4, 1.3, 0, 250, 1, 1))
+PLANS = ((1, 1, 0, 180, 1, 1, 0.7),)
+_NOTE = []
 
-_S = {}
+_S, _ORDER = {}, []
 
 
 def _sb(name, cols, dtype="bfloat16"):
@@ -24,75 +49,650 @@ for _n in ("MG", "MP"):
     _sb(_n, 128, "float32")
 _sb("PI", 4, "int32")
 _sb("PF", 16, "float32")
-for _n in ("THR", "T3", "PC", "PD"):
+for _n in ("THR", "T3", "PC", "LE", "LL", "QS"):
     _sb(_n, 4, "float32")
 _sb("WI", 2, "int32")
 _sb("WF", 2, "float32")
 _sb("THI", 1, "int32")
-_sb("THF", 1, "float32")
-for _n in ("BO", "BO64", "BO8192", "ID", "IDN", "ID128", "SL", "MNE", "BOX", "W1", "W2", "W32", "LT0", "LT1", "LT2", "CN",
-           "C5120", "IDN4096", "ZERO"):
+for _n in ("BO", "BO64", "BO8192", "BON", "ID", "IDN", "ID128", "IDN64", "SL", "MNE", "BOX", "W1", "W2", "W132", "W232", "LT0", "LT1", "LT2",
+           "IDN4096"):
     _sb(_n, 128)
-_sb("ONES", 512)
-for _n in ("THB", "B15", "BNA"):
+_sb("ONES", 256)
+_sb("CT", 640)
+_sb("BO12288", 128)
+_sb("UN", 256)
+for _n in ("THB", "B15", "BNA", "BPA"):
     _sb(_n, 8, "float16")
 for _n in range(4):
     _sb("PM%d" % _n, 128, "float16")
     _sb("PN%d" % _n, 128, "float16")
 _sb("SK", 2048)
 _sb("RX", 512)
+_sb("QX", 512, "float16")
 _sb("IO64", 64)
+_sb("QB", 8, "float32")
+_sb("QQ", 192, "float32")
 _sb("NUM", 256)
 for _n in ("JI", "RA", "RB", "RC"):
     _sb(_n, 32, "float32")
-for _n in ("RR", "EQ", "SC"):
+_sb("RR", 256)
+for _n in ("EQ", "SC"):
     _sb(_n, 512)
-_sb("UI", 512, "int32")
 for _n in ("PR", "ZI", "HI"):
     _sb(_n, 256, "int32")
-_sb("UP", 128, "float32")
-_sb("Q", 256)
-_sb("HU", 256, "uint16")
-for _n in ("H16", "FB", "FX", "FC", "D16"):
+_sb("UP", 256, "float32")
+_sb("Q", 512)
+for _n in ("H0", "H1", "H2", "HN0", "HN1"):
+    _sb(_n, 256, "uint16")
+for _n in ("H16", "FB", "FX", "FC", "D16", "FQ"):
     _sb(_n, 256, "float16")
-for _n in ("PB", "NH", "XA", "SUB", "ABS", "AQ", "MK", "TW", "GT", "DM", "GD"):
+for _n in ("PB", "NH", "XA", "SUB", "RL", "AQ", "MK", "TW", "GT", "DM"):
     _sb(_n, 256)
+_sb("GD", 256)
 _sb("CB", W)
 _sb("EB", W + 32)
 _S["FH"] = ("sbuf", [128, 8, 32], "float16")
 _S["KB"] = ("sbuf", [128, 8, 32], "float32")
-_sb("KC", 256, "float32")
+_S["KC"] = ("sbuf", [128, 8, 32], "float32")
+_S["CI"] = ("sbuf", [128, 2, 8], "int32")
 _sb("WD", 257, "float32")
-for _n in ("KL", "Y"):
-    _sb(_n, 16, "float32")
+_S["KL"] = ("sbuf", [128, 2, 8], "float32")
+_S["Y"] = ("sbuf", [128, 2, 8], "float32")
 for _n in ("LF", "CL", "OFU"):
     _sb(_n, 16, "uint16")
-_sb("CI", 16, "int32")
 _sb("OHX", 1024)
 _sb("OHC", 1024)
-_sb("TA", 64)
 _sb("TB", 64)
-_sb("YM", 1, "float32")
-for _i in range(8):
-    _S["B%d" % _i] = ("psum", [128, 16, 32] if _i in (0, 4) else [128, 512], "float32")
+BANKS = ["B%d" % _i for _i in range(8)]
+for _n in BANKS:
+    _S[_n] = ("psum", [128, 16, 32], "float32")
 SCRATCH = _S
-SEMAPHORES = (["qv", "qs", "qt", "qg", "ls"] + ["d%d" % _i for _i in range(10)]
-              + [_n + str(_i) for _n in ("ax", "ay", "am") for _i in range(1, 4)])
+SEMAPHORES = (["qv", "qs", "qt", "qg", "ls"] + ["d%d" % _i for _i in range(11)]
+              + [_n + str(_i) for _n in ("aw", "ax", "ay", "az", "am") for _i in range(1, 4)])
+HANDED = ([(_t, _n + str(_t + 1), _a, _b, _s + str(_t + 1)) for _t in range(2)
+           for _n, _a, _b, _s in (("X", 128, 256, "ax"), ("X", 0, 128, "aw"), ("M", 0, 256, "am")) if _s + str(_t + 1) in RELAY]
+          + [(2, "X3", 0, 256, "ax3")] * ("end" in RELAY))
+
+
+def in_order(calls):
+    n = len(calls)
+    queue, banks, needs = [c["q"] for c in calls], [c["banks"] for c in calls], [c["after"] | set(c["behind"]) for c in calls]
+
+    def priced(slow, column, call, hop, far, load):
+        cost = [c["cost"] * (column if c["q"] == "t" else slow) + (call if c["name"] == "act" else 0) for c in calls]
+        late = [c["late"] * {"send": far, "dma": load}.get(c["name"], 1) for c in calls]
+        before, later = [[] for _ in calls], [[] for _ in calls]
+        for i, c in enumerate(calls):
+            for p, gap in ([(p, 0 if c["q"] == calls[p]["q"] == "t" else late[p] + hop) for p in c["after"]] + [(p, 0) for p in c["behind"]]):
+                before[i].append((p, gap))
+                later[p].append((i, gap))
+        return cost, late, before, later, hop
+
+    def length(order, cost, late, before, later, hop):
+        end, held, last, bank = [0] * n, [None] * n, {}, {b: {} for b in BANKS}
+        for i in order:
+            q, at, by = queue[i], 0, None
+            for p, gap in before[i]:
+                if end[p] + gap > at:
+                    at, by = end[p] + gap, p
+            if q in last and end[last[q]] > at:
+                at, by = end[last[q]], last[q]
+            for b in banks[i]:
+                for e, p in bank[b].items():
+                    if e != q and end[p] + hop > at:
+                        at, by = end[p] + hop, p
+                bank[b][q] = i
+            end[i], held[i], last[q] = at + cost[i], by, i
+        i = max(range(n), key=lambda i: end[i] + late[i])
+        total, chain = end[i] + late[i], []
+        while held[i] is not None:
+            if held[i] not in needs[i]:
+                chain.append((held[i], i))
+            i = held[i]
+        return total, chain
+
+    def mended(order):
+        def total(order):
+            found = [length(order, *case) for case in cases]
+            return sum(x[0] / case[0] for x, case in zip(found, CASES)), [pair for x in found for pair in x[1]]
+        best, chain = total(order)
+        tried, left = set(), TRIES
+        while left:
+            move = next(((u, v, k) for u, v in chain for k in STEPS if (u, v, k) not in tried), None)
+            if move is None:
+                break
+            tried.add(move)
+            u, v, k = move
+            a, b = order.index(u), order.index(v)
+            if k > 0:
+                ahead = [x for x in range(a, max(a - 150, -1), -1) if queue[order[x]] == queue[u]][:k]
+                a, moved = ahead[-1], {v}
+                for i in reversed(order[a:b]):
+                    if any(i in needs[j] for j in moved):
+                        moved.add(i)
+                first, then = moved, set(order[a:b + 1]) - moved
+            else:
+                b, moved = [x for x in range(b, min(b + 150, n)) if queue[order[x]] == queue[v]][:1 - k][-1], {u}
+                for i in order[a + 1:b + 1]:
+                    if needs[i] & moved:
+                        moved.add(i)
+                first, then = set(order[a:b + 1]) - moved, moved
+            if u in first or v in then:
+                continue
+            left -= 1
+            other = order[:a] + [i for i in order[a:b + 1] if i in first] + [i for i in order[a:b + 1] if i in then] + order[b + 1:]
+            found = total(other)
+            if found[0] < best:
+                order, (best, chain) = other, found
+        _NOTE.append(("mended", TRIES - left, [round(length(order, *case)[0] / c[0] / 1000, 2) for c, case in zip(CASES, cases)]))
+        return order
+
+    def lay_out(way, waits, frees, first, cost, hop, yields):
+        end, left, free, bank = [None] * n, [len(w) for w in waits], {}, {}
+        open_ = {i for i in range(n) if not left[i]}
+
+        def ready(i, guess):
+            c = calls[i]
+            return max([(guess[p] + cost[p] if end[p] is None else end[p]) + gap for p, gap in waits[i]]
+                       + [e + hop for b in c["banks"] for q, e in bank.get(b, {}).items() if q != c["q"]] + [first[i]])
+
+        while open_:
+            at = {i: max(ready(i, None), free.get(calls[i]["q"], 0)) for i in open_}
+            now = min(at.values())
+            q = calls[min(open_, key=lambda i: (at[i], i))]["q"]
+            soon, front = dict(at), set(open_)
+            for _ in range(3):
+                front = {j for i in front for j, gap in frees[i] if all(end[p] is not None or p in soon for p, gap in waits[j])}
+                soon.update({j: ready(j, soon) for j in front})
+            mine = sorted((i for i in soon if calls[i]["q"] == q), key=lambda i: (-way[i], i))
+            for k, i in enumerate(mine):
+                if i in at and at[i] == now and all(now + cost[i] - soon[p] <= yields * (soon[p] - now) for p in mine[:k]):
+                    break
+            else:
+                free[q] = min(soon[p] for p in mine if soon[p] > now)
+                continue
+            end[i] = free[q] = now + cost[i]
+            for b in calls[i]["banks"]:
+                bank.setdefault(b, {})[q] = end[i]
+            open_.remove(i)
+            for j, gap in frees[i]:
+                left[j] -= 1
+                if not left[j]:
+                    open_.add(j)
+        return end
+
+    cases, best = [priced(*case) for case in CASES], None
+    for plan in PLANS:
+        cost, late, before, later, hop = priced(*plan[:6])
+        way = [0] * n
+        for i in range(n - 1, -1, -1):
+            way[i] = cost[i] + calls[i].get("soon", 0) + max([way[j] + gap for j, gap in later[i]] + [late[i]])
+        for r in range(ROUNDS):
+            if r:
+                way = lay_out(end, later, before, late, cost, hop, plan[6])
+            end = lay_out(way, before, later, [0] * n, cost, hop, plan[6])
+            order = sorted(range(n), key=lambda i: (end[i] - cost[i], i))
+            total = [length(order, *case)[0] / CASES[k][0] for k, case in enumerate(cases)]
+            _NOTE.append((plan, r, [round(x / 1000, 2) for x in total]))
+            if best is None or sum(total) < best[0]:
+                best = (sum(total), order)
+    return mended(best[1])
 
 
 def rank_program(g, core, T, topo):
-    rank = T.rank_of(core)
-    if rank is None:
-        return
     n_ranks = len(T.cores)
+
+    def target(c, t):
+        return T.cores[(T.rank_of(c) + (3 if t < 2 else 2)) % n_ranks]
+
+    def helper(c):
+        ranks = [r for r in topo.cores_of(c) if T.rank_of(r) is not None]
+        able = [h for h in topo.cores_of(c) if topo.die(h) != topo.die(c) and all(topo.may_write(h, target(r, t)) for r in ranks for t in range(3))]
+        return able[ranks.index(c)]
+
+    def write(dst, out, src, sem, mask):
+        rid, pid, _eng = topo.addr(dst)
+        g.remote_dma(out, src, T.sem[sem], T.sem.ls, pid, rid, mask)
+
+    if T.rank_of(core) is None:
+        for c in topo.cores_of(core):
+            if T.rank_of(c) is not None and helper(c) == core:
+                n = 0
+                for t, name, c0, c1, sem in HANDED:
+                    dst = target(c, t)
+                    g.wait_ge(T.sem[sem], len(topo.engines(c, dst)))
+                    write(dst, T[name][:, c0:c1], T[name][:, c0:c1], sem, topo.mask(core, dst))
+                    n += len(topo.engines(core, dst))
+                g.wait_ge(T.sem.ls, n)
+        return
+    calls, known, lines = [], {}, {}
+
+    def do(q, reads, writes, cost, name, kw, late=0):
+        after = set()
+        reads, writes = [[k if isinstance(k, tuple) else (k,) for k in keys] for keys in (reads, writes)]
+        for keys, overwrites in ((reads, False), (writes, True)):
+            for k in keys:
+                for other, (writer, readers) in known.setdefault(k[0], {}).items():
+                    if other[:len(k)] == k[:len(other)]:
+                        after.update(writer + (readers if overwrites else []))
+        for k in reads:
+            known[k[0]].setdefault(k, ([], []))[1].append(len(calls))
+        for k in writes:
+            for other in [o for o in known[k[0]] if o[:len(k)] == k]:
+                del known[k[0]][other]
+            known[k[0]][k] = ([len(calls)], [])
+        calls.append({"q": q, "name": name, "kw": kw, "cost": cost, "late": late, "after": after, "behind": [],
+                      "banks": {k[0] for k in reads + writes if k[0] in BANKS}})
+
+    def in_line(name):
+        calls[-1]["behind"] = lines.get(name, [])
+        lines[name] = [len(calls) - 1]
+
+    def dma(q, out, in_, reads, writes, late):
+        do(q, reads, writes, 50, "dma", (out, in_), late)
+        if q == "y":
+            in_line(q)
+
+    def send(dst, out, src, reads, writes, sem, late=FAR, also=None):
+        do("g", reads, writes, ISSUE, "send", (dst, out, src, sem, also), late)
+
+    def cycles(n):
+        return max(64, n) * CYCLE
+
+    def cp(out, in_, r, w, n=0):
+        do("v", r, w, cycles(n), "copy", dict(out=out, in_=in_))
+
+    def tt(out, a, b, op, r, w, n=0):
+        do("v", r, w, cycles(n), "tt", dict(out=out, in0=a, in1=b, op=op))
+
+    def ts(out, a, s1, op0, r, w, s2=None, op1=None, n=0):
+        kw = dict(out=out, in0=a, scalar1=s1, scalar2=s2, op0=op0)
+        if op1 is not None:
+            kw["op1"] = op1
+        do("v", r, w, cycles(n), "ts", kw)
+
+    def tr(out, in_, r, w):
+        do("v", r, w, cycles(128), "turn", dict(out=out, in_=in_))
+
+    def fill(ap, c, w, n=0):
+        do("v", [], w, cycles(n), "fill", (ap, c))
+
+    def act(out, in_, r, w, n, func=AF.Copy, **kw):
+        do("s", r, w, CALL + n * CYCLE, "act", dict(out=out, in_=in_, func=func, **kw))
+
+    def mm(out, l, r, start, stop, rd, b, n):
+        do("t", rd, [b], max(64, n) * COLUMN, "mm", (out, l, r, start, stop), 60)
+
+    def iota(out, pattern, base, cm, w, n, small=True):
+        kw = dict(out=out, pattern=pattern, base=base, channel_multiplier=cm)
+        if small:
+            kw["allow_small_or_imprecise_dtypes"] = True
+        do("g", [], w, SLOWG * (130 + 2 * n * CYCLE), "iota", kw)
+
+    def pick(out, in_, pattern, op, other, r, w, n, base=0, cm=-1):
+        do("g", r, w, SLOWG * (170 + 2 * n * CYCLE), "pick", dict(out=out, in_=in_, pattern=pattern, compare_op=op, fill=other, base=base,
+                                                       channel_multiplier=cm))
+
+    def gathered(n):
+        return 60 + GATHER * n
+
+    def half(h):
+        return slice(128 * h, 128 * h + 128)
+
+    def ps(b, c0, c1, p=slice(None)):
+        if c0 % 32 == 0 and c1 % 32 == 0:
+            return T[b][p, c0 // 32:c1 // 32, :]
+        return T[b][p, c0 // 32, c0 % 32:c0 % 32 + c1 - c0]
+
+    dma("y", T.X0[:], T.xw[:], [], ["X0"], 1500)
+    dma("s", T.WI[:], T.wts[:], [], ["WI"], 1400)
+    dma("y", T.LX[:, 0:W], T.lex[:], [], ["LX"], LOADX)
+    dma("s", T.THI[:], T.th[:], [], ["THI"], 1400)
+    dma("y", T.M0[:], T.gw[:], ["LX"], ["M0"], 1500)
+    dma("y", T.LM[:, 0:W], T.mng[:], ["LX"], ["LM"], LOADM)
+
+    col = [[1, 128]]
+    iota(T.PI[:, 0:1], [[0, 1]], 0, 1, [("PI", 0)], 1, False)
+    iota(T.MG[:], [[1, 8], [0, 16]], 0, 0, ["MG"], 128)
+    fill(T.ONES[:], 1.0, ["ONES"], 128)
+    ts(T.PI[:, 1:2], T.PI[:, 0:1], 4, OP.arith_shift_right, [("PI", 0)], [("PI", 1)])
+    ts(T.PI[:, 2:3], T.PI[:, 0:1], 15, OP.bitwise_and, [("PI", 0)], [("PI", 2)])
+    for a, b, c in ((0, 256, -65536.0), (256, 512, 5120.0), (512, 640, -48.0)):
+        fill(T.CT[:, a:b], c, [("CT", a)], (b - a) // 2)
+    cp(T.PF[:, 0:2], T.PI[:, 1:3], ["PI"], [("PF", 0)])
+    pG, pL, P0 = T.PF[:, 0:1], T.PF[:, 1:2], ("PF", 0)
+    pick(T.ID[:], T.ONES[:, 0:128], col, OP.is_equal, 0.0, ["ONES"], ["ID"], 128)
+    ts(T.BO[:], T.MG[:], pG, OP.is_equal, ["MG", P0], ["BO"], n=128)
+    tt(T.MNE[:], T.BO[:], T.ID[:], OP.subtract, ["BO", "ID"], ["MNE"], 256)
+    ts(T.BOX[:], T.ID[:], -16.0, OP.mult, ["ID"], ["BOX"])
+    tt(T.BOX[:], T.BOX[:], T.BO[:], OP.add, ["BO", "BOX"], ["BOX"], 256)
+    cp(T.WF[:], T.WI[:], ["WI"], ["WF"])
+    ts(T.W1[:], T.MNE[:], T.WF[:, 0:1], OP.mult, ["MNE", "WF"], ["W1"])
+    ts(T.W2[:], T.MNE[:], T.WF[:, 1:2], OP.mult, ["MNE", "WF"], ["W2"])
+    ts(T.W132[:], T.MNE[:], T.WF[:, 0:1], OP.mult, ["MNE", "WF"], ["W132"], 32.0, OP.mult)
+    ts(T.W232[:], T.MNE[:], T.WF[:, 1:2], OP.mult, ["MNE", "WF"], ["W232"], 32.0, OP.mult)
+    for nm, src, c in (("BO64", "BO", 64.0), ("IDN4096", "ID", -4096.0), ("ID128", "ID", 128.0), ("IDN", "ID", -1.0), ("IDN64", "ID", -1.0 / 64),
+                       ("BO8192", "BO", 8192.0), ("BON", "BO", -1.0), ("BO12288", "BO", 12288.0)):
+        ts(T[nm][:], T[src][:], c, OP.mult, [src], [nm])
+    for nm, c in (("B15", 1.5), ("BNA", -2.0 / 4096), ("BPA", 1.0 / 4096)):
+        ts(T[nm][:], T.BO[:, ::16], c, OP.mult, ["BO"], [nm])
+    for e in range(8):
+        if e < ZERO:
+            fill(T.SK[:, 256 * e:256 * e + 256], 0.0, [("SK", "zero", e)], 128)
+        else:
+            act(T.SK[:, 256 * e:256 * e + 256], T.ONES[:], ["ONES"], [("SK", "zero", e)], 256, scale=0.0)
+    for e in range(8):
+        pick(T.SK[:, 16 * e:16 * e + 129 * 15 + 1:129], T.BOX[:, 16 * e:16 * e + 16], [[0, 16]], OP.is_ge, 0.0, ["BOX", ("SK", "zero")],
+             [("SK", e)], 16, 127)
+    pick(T.SL[:], T.BO[:], col, OP.is_gt, 0.0, ["BO"], ["SL"], 128)
+
+    def lowest(t):
+        nm = "LT%d" % t
+        pick(T[nm][:], T.SL[:], col, OP.not_equal, -1.0, ["SL"], [nm], 128)
+        if t == 2:
+            in_line("sent")
+        for src, op, other, base in (("BO64", OP.is_gt, 1.0, t), (None, OP.is_ge, 0.0, 15), (None, OP.not_equal, -16.0, t)):
+            pick(T[nm][:, t::16], T[src][:, ::16] if src else T[nm][:, t::16], [[16, 8]], op, other, [nm, "BO64"], [nm], 8, base)
+    lowest(0)
+    lowest(1)
+    iota(T.T3[:], [[1, 4]], 0, 0, ["T3"], 4)
+    ts(T.THR[:], T.T3[:], pL, OP.not_equal, ["T3", P0], ["THR"], -0.5, OP.mult)
+    ts(T.PF[:, 10:11], T.THI[:], -2048.0, OP.add, ["THI"], [("PF", 10)], 1.0 / 4096, OP.mult)
+    ts(T.THB[:], T.BO[:, ::16], T.PF[:, 10:11], OP.mult, ["BO", ("PF", 10)], ["THB"])
+    iota(T.PC[:], [[-1, 2], [100, 2]], 0, 0, ["PC"], 4)
+    iota(T.MP[:], [[2, 4], [100, 2], [0, 16]], 0, 0, ["MP"], 128)
+    ts(T.PF[:, 2:6], T.PC[:], pG, OP.add, ["PC", P0], [("PF", 2)])
+    for i in range(4):
+        ts(T["PM%d" % i][:], T.MP[:], T.PF[:, 2 + i:3 + i], OP.is_equal, ["MP", ("PF", 2)], ["PM%d" % i], n=128)
+        ts(T["PN%d" % i][:], T["PM%d" % i][:], 64.0, OP.mult, ["PM%d" % i], ["PN%d" % i])
+        calls[-1]["soon"] = EARLY[0]
+    ts(T.LE[:], T.T3[:], pL, OP.is_equal, ["T3", P0], ["LE"])
+    ts(T.LL[:], T.T3[:], pL, OP.is_gt, ["T3", P0], ["LL"])
+    iota(T.QQ[:, 0:64], [[-1, 64]], 31, 0, [("QQ", 0)], 64)
+    act(T.PF[:, 8:9], pL, [P0], [("PF", 8)], 1, func=AF.Identity, scale=-4.0, bias=-1.5)
+    act(T.PF[:, 9:10], T.LL[:, 2:3], ["LL", P0], [("PF", 9)], 1, func=AF.Identity, scale=-32.0, bias=pL)
+    for i, (e, a, b) in enumerate(((1, -2.0, T.LL[:, 3:4]), (1, -1.0, 0.0), (2, -0.25, 0.0), (2, -1.25, 1.0))):
+        act(T.QS[:, i:i + 1], T.LE[:, e:e + 1], ["LE", "LL"], [("QS", i)], 1, func=AF.Identity, scale=a, bias=b)
+    for i in range(2):
+        act(T.QQ[:, 64 * i + 64:64 * i + 128], T.QQ[:, 0:64], [("QQ", 0), "QS"], [("QQ", i + 1)], 64, func=AF.Identity,
+            scale=T.QS[:, 2 * i:2 * i + 1], bias=T.QS[:, 2 * i + 1:2 * i + 2])
+    tt(T.QQ[:, 0:64], T.QQ[:, 64:128], T.QQ[:, 128:192], OP.mult, ["QQ"], [("QQ", 0)], 128)
+    cp(T.QB[:], T.BO[:, ::16], ["BO"], ["QB"])
+    for e in range(8):
+        act(T.QX[:, 64 * e:64 * e + 64], T.QQ[:, 0:64], [("QQ", 0), "QB"], [("QX", e)], 64, func=AF.Identity, scale=T.QB[:, e:e + 1])
+    iota(T.IO64[:], [[1, 64]], 0, 0, ["IO64"], 64)
+    for e in range(2):
+        pick(T.RX[:, 256 * e:256 * e + 256], T.ONES[:], [[1, 2], [0, 8], [4, 16]], OP.is_equal, 0.0, ["ONES"], [("RX", e)], 256, 2 * e)
+    ts(T.RX[:, 128:384], T.RX[:, 128:384], 0.5, OP.mult, ["RX"], ["RX"], n=128)
+    iota(T.JI[:], [[1, 16], [-100, 2]], 0, 0, ["JI"], 32)
+    ts(T.RC[:], T.JI[:], pL, OP.is_equal, ["JI", P0], ["RC"], -2.0, OP.mult)
+    ts(T.RA[:], T.JI[:], pL, OP.is_gt, ["JI", P0], ["RA"], 2.0 ** -16 - 1, OP.mult)
+    ts(T.RB[:], T.JI[:], pL, OP.is_gt, ["JI", P0], ["RB"], 2.0 ** 16 - 1, OP.mult)
+    ts(T.RC[:], T.RC[:], 1.0, OP.add, ["RC"], ["RC"])
+    tt(T.RA[:], T.RA[:], T.RC[:], OP.add, ["RA", "RC"], ["RA"])
+    tt(T.RB[:], T.RB[:], T.RC[:], OP.add, ["RB", "RC"], ["RB"])
+    fill(T.RR[:, 0:1], 0.0, [("RR", 0)])
+    tt(T.RR[:, 1:32], T.RA[:, 0:31], T.RB[:, 1:32], OP.mult, ["RA", "RB"], [("RR", 1)])
+    calls[-1]["soon"] = EARLY[1]
+    for n in (32, 64, 128):
+        pick(T.RR[:, n:2 * n], T.RR[:, 0:n], [[0, n]], OP.is_ge, 0.0, ["RR"], [("RR", n)], n, 127)
+    for h in range(2):
+        ts(T.PF[:, 11 + h:12 + h], pL, float(W + 16 * h), OP.add, [P0], [("PF", 11 + h)])
+        fill(T.EQ[:, 256 * h + 1:256 * h + 128:2], 0.0, [("EQ", h, "zero")])
+
+    def scatter(lex, src):
+        for c in range(7, -1, -1):
+            cp(T[lex][:].indirect(T.OFU[:, 2 * c:2 * c + 2]), T[src][:, 32 * c:32 * c + 32], [("OFU", c // 4), (src, c // 4)], [lex],
+               60 + 32 * SCATTER)
+
+    XP, SCORE, COLS, ENDS, HASH = ("B7", "B1"), ("B2", "B0"), ("B2", "B5"), ("B7", "B1"), ("B5", "B0")
+
+    def hashed(parts, h, idle=False):
+        s, b, q = half(h), HASH[h], T.Q[:, 256 * h:256 * h + 256]
+        for o, ws in ((0, ("W132", "W232")), (256, ("W1", "W2"))):
+            mm(ps(b, o, o + 256), T.ONES[:, 0:128], T.CT[:, o:o + 256], True, False, ["ONES", "CT"], b, 256)
+            for X in parts:
+                for j, w in enumerate(ws):
+                    mm(ps(b, o + 128 * j, o + 128 * j + 128), T[w][:], T[X][:, s], False, (X, j) == (parts[-1], 1) and (idle or o == 0),
+                       [w, (X, h)], b, 128)
+        if idle:
+            cp(T.ZI[:], ps(b, 256, 512), [b], ["ZI"], 256)
+            ts(T.ZI[:], T.ZI[:], 4095, OP.bitwise_and, ["ZI"], ["ZI"], n=256)
+            tt(T.PR[:, s], T.ZI[:, 0:128], T.ZI[:, 128:256], OP.mult, ["ZI"], [("PR", h)], 256)
+        else:
+            act(q, ps(b, 0, 256), [b], [("Q", h)], 256, func=AF.Identity, scale=2.0 ** -17, bias=223.5 + 1.0 / 8192)
+            mm(ps(b, 256, 512), T.IDN4096[:], q, False, True, ["IDN4096", ("Q", h)], b, 256)
+            act(T.UP[:, s], ps(b, 384, 512), [b], [("UP", h)], 128)
+            tt(T.PR[:, s], T.UP[:, s], ps(b, 256, 384), OP.mult, [("UP", h), b], [("PR", h)], 128)
+        tt(T.ZI[:, s], T.PR[:, s], ps(b, 0, 128), OP.add, [("PR", h), b], [("ZI", h)], 128)
+        ts(T.HI[:, s], T.ZI[:, s], 5, OP.arith_shift_right, [("ZI", h)], [("HI", h)], 4095, OP.bitwise_and, 128)
+        calls[-1]["soon"] = SOON[h]
+
+    for h in (1, 0):
+        hashed(["X0"], h, h == IDLE)
+        cp(T.H0[:, half(h)], T.HI[:, half(h)], [("HI", h)], [("H0", h)], 128)
+
+    for t in range(3):
+        xn, mn = "XN%d" % t, "MN%d" % t
+        X, M, X1, M1 = "X%d" % t, "M%d" % t, "X%d" % (t + 1), "M%d" % (t + 1)
+        H, H1, hn = "H%d" % t, "H%d" % (t + 1), "HN%d" % t
+        TX, TM = T[X], T[M]
+        dst = target(core, t)
+        lt, top = "LT%d" % t, slice(0, 64)
+
+        cut = 256 - SHARE[t]
+        for w0, w1 in ((224, 256), (192, 224), (128, 192), (0, 64), (64, 96), (96, 128)):
+            args = (T.CB[:, 16 * w0:16 * w1], T.LX[:, 0:W].indirect(T[H][:, w0:w1]), ["LX", (H, w0 // 128)], [("CB", w0 // 64, w0)])
+            if w0 >= cut:
+                cp(*args, gathered(16 * (w1 - w0)))
+            else:
+                act(*args, GATHER * 16 * (w1 - w0))
+                in_line("gather")
+        for h in (1, 0):
+            ts(T.H16[:, half(h)], T[H][:, half(h)], -2048.0, OP.add, [(H, h)], [("H16", h)])
+            mm(ps(XP[h], 128 * h, 128 * h + 128), T.ID[:], TX[:, half(h)], True, True, ["ID", (X, h)], XP[h], 128)
+            mm(ps(XP[h], 256, 384), T.ID[:], T.H16[:, half(h)], True, True, ["ID", ("H16", h)], XP[h], 128)
+            for j in range(2):
+                mm(T[XP[h]][:, 4 - 4 * h:8 - 4 * h, j::2], T.ID[:], TX[:, 128 * h + 64:128 * h + 128], True, True, ["ID", (X, h)], XP[h], 64)
+
+        def lane(h):
+            b, s = SCORE[h], half(h)
+            for w0, n in ((224, 32), (192, 32), (128, 64)) if h else ((0, 64), (64, 32), (96, 32)):
+                m = 64 // n
+                x0 = w0 if m == 1 else 2 * w0 - 384 * h
+                for k in range(16 // m):
+                    o, part = 16 * w0 + 64 * k, ("CB", w0 // 64) + ((w0,) if m > 1 else ())
+                    tt(T.EB[:, o:o + 64], T.CB[:, 16 * w0 + k:16 * (w0 + n):16 // m], ps(XP[h], x0, x0 + 64), OP.not_equal, [part, XP[h]],
+                       [("EB", o)])
+                    for j in range(m):
+                        mm(ps(b, w0 % 128, w0 % 128 + n), T.SK[:, 128 * (k + 8 * j):128 * (k + 8 * j + 1)], T.EB[:, o + j:o + 64:m],
+                           k + 8 * j == 0, k + 8 * j == 15, ["SK", ("EB", o)], b, n)
+            ts(T.PB[:, s], ps(b, 0, 128), -11.5, OP.is_le, [b], [("PB", h)], n=128)
+            mm(ps(b, 128, 256), T[lt][:], T.PB[:, s], True, True, [lt, ("PB", h)], b, 128)
+            mm(ps(b, 256, 384), T.BO[:], T.PB[:, s], True, True, ["BO", ("PB", h)], b, 128)
+            ts(T.FB[:, s], ps(b, 128, 256), T.THR[:, t:t + 1], OP.is_le, [b, "THR"], [("FB", h)], n=128)
+            act(T.NH[:, s], ps(b, 256, 384), [b], [("NH", h)], 128, func=AF.Relu, scale=-128.0, bias=64.0)
+            tt(T.FH[:, 4 * h:4 * h + 4, :], T.FB[:, s], ps(XP[h], 256, 384), OP.mult, [("FB", h), XP[h]], [("FH", h)], 128)
+            tt(T.FX[:, s], T.FB[:, s], ps(XP[h], 128 * h, 128 * h + 128), OP.mult, [("FB", h), XP[h]], [("FX", h)], 128)
+
+        def place_f(h):
+            c4 = slice(4 * h, 4 * h + 4)
+            for i in range(4):
+                s, c = i // 2, i % 2
+                mm(T.B3[:, c4, 16 * s:16 * s + 16], T["PM%d" % i][:], T.FH[:, c4, 16 * c:16 * c + 16], c == 0, c == 1,
+                   ["PM%d" % i, ("FH", h)], "B3", 64)
+            tr(T.KB[:, c4, :], T.B3[:, c4, :], ["B3"], [("KB", h)])
+            ts(T.LF[:, 8 * h:8 * h + 8], T.KB[:, c4, ::16], 2048.0, OP.add, [("KB", h)], [("LF", h)])
+
+        def lookup_f(h):
+            s, places = half(h), T.LF[:, 8 * h:8 * h + 8]
+            tt(T.SUB[:, s], T.LM[:, 0:W].indirect(places), TM[:, s], OP.subtract, ["LM", M, ("LF", h)], [("SUB", h)], gathered(128))
+            tt(T.FC[:, s], T.LX[:, 0:W].indirect(places), T.FB[:, s], OP.mult, ["LX", ("LF", h), ("FB", h)], [("FC", h)], gathered(128))
+            ts(T.RL[:, s], T.SUB[:, s], 0.0, OP.max, [("SUB", h)], [("RL", h)])
+            for o, src, w in ((8, "FB", "THB"), (8, "FB", "B15"), (8, "NH", "B15"), (8, "SUB", "BPA"), (0, "FC", "BO"), (8, "RL", "BNA")):
+                mm(ps(COLS[h], o, o + 8), T[src][:, s], T[w][:, ::16] if w == "BO" else T[w][:], w == "THB", w == "BNA", [(src, h), w],
+                   COLS[h], 8)
+
+        def hot_x(h):
+            o, b = ps("B4", 128 * h, 128 * h + 128), ("B1", "B6")[h]
+            mm(o, T.BO[:], T.FX[:, half(h)], True, True, ["BO", ("FX", h)], "B4", 128)
+            act(T.FQ[:, half(h)], o, ["B4", ("PF", 9), "LL"], [("FQ", h)], 128, func=AF.Square, scale=T.LL[:, 2:3], bias=T.PF[:, 9:10])
+            mm(ps(b, 0, 512), T.FQ[:, half(h)], T.QX[:], True, True, [("FQ", h), "QX"], b, 512)
+            for c0, c1 in ((0, 512),) if h or "one" in ONV else ((0, 256), (256, 512)):
+                act(T.OHX[:, 512 * h + c0:512 * h + c1], ps(b, c0, c1), [b], [("OHX", h, e) for e in range(c0 // 256, c1 // 256)], c1 - c0,
+                    func=AF.Relu, bias=1.0)
+
+        def coded(h):
+            for pm, src in (("PN", "FX"), ("PM", "FC")):
+                for i in range(4):
+                    s, w0 = i // 2, 128 * h + 64 * (i % 2)
+                    mm(T.B3[:, 8 + 4 * h:12 + 4 * h, 16 * s:16 * s + 16], T[pm + str(i)][:], T[src][:, w0:w0 + 64], src == "FX" and i == 0,
+                       src == "FC" and i == 3, [pm + str(i), (src, h)], "B3", 64)
+            tr(T.KC[:, 4 * h:4 * h + 4, :], T.B3[:, 8 + 4 * h:12 + 4 * h, :], ["B3"], [("KC", h)])
+
+        def table(h):
+            for e in range(8):
+                s, b = slice(512 * h + 64 * e, 512 * h + 64 * e + 64), COLS[h]
+                ts(T.OHC[:, s], T.IO64[:], ps(b, e, e + 1), OP.is_equal, ["IO64", b], [("OHC", h, e)], ps(b, 8 + e, 9 + e), OP.is_ge)
+                rd = [("OHX", h, e // 4), ("OHC", h, e)]
+                mm(ps("B6", 0, 64, top), T.OHX[:, s], T.OHC[:, s], (h, e) == (1, 0), False, rd, "B6", 64)
+                mm(ps("B6", 0, 64, top), T.OHC[:, s], T.OHX[:, s], False, (h, e) == (0, 7), rd, "B6", 64)
+
+        def ahead(h):
+            s, b = half(h), HASH[h]
+            for i, (l, src) in enumerate((("ID", X), ("IDN", "FX"), ("IDN", "NH"), ("ID", "FC"))):
+                mm(ps(b, 384, 512), T[l][:], T[src][:, s], i == 0, i == 3, [l, (src, h)], b, 128)
+            tt(T.UN[:, s], TX[:, s], ps(b, 384, 512), OP.min, [(X, h), b], [("UN", h)], 128)
+            hashed(["NH", "UN"], h)
+
+        lane(1)
+        lane(0)
+        place_f(1)
+        lookup_f(1)
+        if t < 2:
+            ahead(1)
+        if CODE_FIRST:
+            coded(1)
+        place_f(0)
+        lookup_f(0)
+        if not CODE_FIRST:
+            coded(1)
+        coded(0)
+        for h in (1, 0):
+            hot_x(h)
+        for h in (1, 0):
+            table(h)
+        if t < 2 and 0 in AHEAD:
+            ahead(0)
+        mm(ps("B4", 256, 512), T.BO[:], T.FX[:], True, False, ["BO", "FX"], "B4", 256)
+        mm(ps("B4", 256, 512), T.ID[:], T.NH[:], False, True, ["ID", "NH"], "B4", 256)
+        act(T.AQ[:], ps("B4", 256, 512), ["B4", ("PF", 8)], ["AQ"], 256, func=AF.Abs, bias=T.PF[:, 8:9])
+        act(T.MK[:], T.AQ[:], ["AQ"], ["MK"], 256, func=AF.Relu, scale=-1.0, bias=2.5)
+        mm(ps("B4", 0, 256), T.ID[:], TX[:], True, False, ["ID", X], "B4", 256)
+        mm(ps("B4", 0, 256), T.ID[:], T.NH[:], False, True, ["ID", "NH"], "B4", 256)
+        act(T.XA[:], ps("B4", 0, 256), ["B4"], ["XA"], 256)
+        calls[-1]["soon"] = SOON[2]
+        for o in range(2):
+            if "kl" in ONV:
+                ts(T.KL[:, :, 4 * o:4 * o + 4], T.KB[:, :, 16 * o], 1.0 / 8192, OP.mult, ["KB"], [("KL", o)], 1.25, OP.add)
+            else:
+                act(T.KL[:, :, 4 * o:4 * o + 4], T.KB[:, :, 16 * o], ["KB"], [("KL", o)], 8, func=AF.Identity, scale=1.0 / 8192, bias=1.25)
+            cp(T.CI[:, :, 4 * o:4 * o + 4], T.KC[:, :, 16 * o], ["KC"], [("CI", o)])
+        ts(T.CI[:], T.CI[:], 255, OP.bitwise_and, ["CI"], ["CI"])
+        cp(T.CL[:], T.CI[:], ["CI"], ["CL"])
+        if "dm" in ONV:
+            ts(T.D16[:], T.SUB[:], 0.5, OP.mult, ["SUB"], ["D16"], 1535.75, OP.add, 128)
+            ts(T.DM[:], T.D16[:], -1536.0, OP.add, ["D16"], ["DM"], n=128)
+        else:
+            act(T.D16[:], T.SUB[:], ["SUB"], ["D16"], 256, func=AF.Identity, scale=0.5, bias=1535.75)
+            act(T.DM[:], T.D16[:], ["D16"], ["DM"], 256, func=AF.Identity, bias=-1536.0)
+        ts(T.TB[top, :], ps("B6", 0, 64, top), 1.0, OP.min, ["B6"], ["TB"])
+        for r in range(4):
+            mm(ps("B6", 256 + 64 * r, 320 + 64 * r), T.RX[top, 128 * r:128 * r + 128], T.TB[top, :], True, True, ["RX", "TB"], "B6", 64)
+        cp(T.TW[:], ps("B6", 256, 512), ["B6"], ["TW"], 256)
+        for h in (1, 0):
+            s, b = half(h), ENDS[h]
+            tt(T.GT[:, s], T.TW[:].indirect(T.CL[:, 8 * h:8 * h + 8]), T.MK[:, s], OP.mult, ["TW", "CL", "MK"], [("GT", h)], gathered(128))
+            terms = [(0, "ID", TX[:, s], X), (0, "IDN", T.FX[:, s], "FX"), (128, "BO", T.FH[:, 4 * h:4 * h + 4, :], "FH"),
+                     (128, "ID128", T.NH[:, s], "NH"), (0, "ID", T.FC[:, s], "FC"), (0, "BO64", T.GT[:, s], "GT"), (128, "BO8192", T.GT[:, s], "GT")]
+            if t < 2 and h in AHEAD:
+                terms[5:5] = [(256, "ID", T.H16[:, s], "H16"), (256, "ONES", T.CT[:, 512:640], "CT"), (256, "BO12288", T.GT[:, s], "GT")]
+            for i, (o, l, src, key) in enumerate(terms):
+                mm(ps(b, o, o + 128), T[l][:, 0:128], src, i == 0, i == len(terms) - 1, [l, (key, h) if key != "CT" else key], b, 128)
+            tt(T[xn][:, s], T.XA[:, s], ps(b, 0, 128), OP.min, ["XA", b], [(xn, h)], 128)
+            if t < 2:
+                if h in AHEAD:
+                    tt(T.PR[:, s], ps(b, 256, 384), T.HI[:, s], OP.max, [b, ("HI", h)], [("PR", h)], 128)
+                    ts(T.HI[:, s], T.PR[:, s], 4095, OP.bitwise_and, [("PR", h)], [("HI", h)], n=128)
+                else:
+                    hashed([xn], h)
+                cp(T[hn][:, s], T.HI[:, s], [("HI", h)], [(hn, h)], 128)
+                sem = ("aw", "ax")[h] + str(t + 1)
+                if sem in RELAY and FUSED:
+                    send(dst, T[H1][:, s], T[hn][:, s], [(hn, h), (xn, h)], [(H1, h), ("with", t, h)], ("az", "ay")[h] + str(t + 1),
+                         also=(T[X1][:, s], T[xn][:, s], sem))
+                    do("far", [("with", t, h)], [(X1, h)], 1, "lands", (dst, sem), FARX - FAR)
+                else:
+                    send(dst, T[X1][:, s], T[xn][:, s], [(xn, h)], [(X1, h)], sem, FARX if sem in RELAY else FAR)
+                    send(dst, T[H1][:, s], T[hn][:, s], [(hn, h)], [(H1, h)], ("az", "ay")[h] + str(t + 1))
+            for o, a, c in ((0, 0, 0), (128, 16, 16), (129, 16, 0)):
+                tt(T.EQ[:, 256 * h + o:256 * h + o + 127:2], T.KB[:, 4 * h:4 * h + 4, a:a + 16], T[b][:, 4:8, c:c + 16], OP.is_equal,
+                   [("KB", h), b], [("EQ", h, o)])
+            s2 = slice(256 * h, 256 * h + 256)
+            do("v", ["RR", ("EQ", h)], [("SC", h)], cycles(128), "scan", dict(out=T.SC[:, s2], data0=T.RR[:], data1=T.EQ[:, s2], initial=0.0,
+                                                                            op0=OP.mult, op1=OP.add))
+            if t not in WHOLE:
+                tt(T.Y[:, h, :], T.SC[:, 256 * h + 31:256 * h + 256:32], T.KL[:, h, :], OP.add, [("SC", h), "KL"], [("Y", h)])
+                for o in range(2):
+                    ts(T.OFU[:, 8 * h + o:8 * h + 8:2], T.Y[:, h, 4 * o:4 * o + 4], 8192.0, OP.mult, [("Y", h), ("PF", 11 + o)],
+                       [("OFU", h, o)], T.PF[:, 11 + o:12 + o], OP.min)
+        if t in WHOLE:
+            tt(T.Y[:], T.SC[:, 31::32], T.KL[:], OP.add, ["SC", "KL"], ["Y"])
+            for o in range(2):
+                ts(T.OFU[:, o::2], T.Y[:, :, 4 * o:4 * o + 4], 8192.0, OP.mult, ["Y", ("PF", 11 + o)], [("OFU", 0, o), ("OFU", 1, o)],
+                   T.PF[:, 11 + o:12 + o], OP.min)
+        if t == 2:
+            send(dst, T[X1][:], T[xn][:], [xn], [X1], "ax3", FARX)
+        for i, (l, src) in enumerate((("ID", "ONES"), ("IDN64", "NH"), ("BON", "GT"))):
+            mm(ps("B2", 0, 256), T[l][:], T[src][:], i == 0, i == 2, [l, src], "B2", 256)
+        tt(T.GD[:], T.DM[:], ps("B2", 0, 256), OP.mult, ["DM", "B2"], ["GD"], 256)
+        mm(ps("B3", 0, 256), T.ID[:], TM[:], True, False, ["ID", M], "B3", 256)
+        mm(ps("B3", 0, 256), T.ID[:], T.GD[:], False, True, ["ID", "GD"], "B3", 256)
+        act(T[mn][:], ps("B3", 0, 256), ["B3"], [mn], 256)
+        in_line("gather")
+        scatter("LX", xn)
+        if t < 2:
+            scatter("LM", mn)
+        send(dst, T[M1][:], T[mn][:], [mn] + ([H1] if t < 2 and "am" + str(t + 1) not in RELAY else []), [M1], "am" + str(t + 1), FARM if t < 2 else FARE)
+        if t == 0:
+            calls[-1]["behind"] = [i for i, c in enumerate(calls[:-1]) if c["name"] == "send"]
+            lines["sent"] = [len(calls) - 1]
+            lowest(2)
+            iota(T.NUM[:], [[-1, 256]], -1, 0, ["NUM"], 256)
+            in_line("sent")
+
+    scatter("EB", "NUM")
+    for j in range(8):
+        mm(ps("B6", 0, 512), T.ID[:], T.LM[:, 512 * j:512 * j + 512], j == 0, j == 7, ["ID", "LM", xn], "B6", 512)
+    for i, (l, src) in enumerate((("IDN", "SUB"), ("ID", "DM"))):
+        mm(ps("B4", 0, 256), T[l][:], T[src][:], i == 0, i == 1, [l, src], "B4", 256)
+    act(ps("B6", 0, 512), ps("B6", 0, 512), ["B6"], ["B6", "B3", "sum"], 700, accum_out=ps("B3", 0, 1))
+    dma("y", T.yl[:], T.LX[:, 0:W], ["LX"], ["yl"], LAST)
+    tt(T.PB[:], T.EB[:, 0:W].indirect(T.LF[:, 0:16]), T.NUM[:], OP.is_equal, ["EB", "NUM", "LF"], ["PB"], gathered(256))
+    cp(T.WD[:, 256:257], ps("B3", 0, 1), ["B3"], [("WD", 1)])
+    tt(T.WD[:, 0:256], T.PB[:], ps("B4", 0, 256), OP.mult, ["PB", "B4"], [("WD", 0)], 256)
+    do("v", ["WD"], ["YM"], cycles(257), "reduce", dict(out=T.PF[:, 15:16], in_=T.WD[:], axis=AxisListType.X, op=OP.add))
+    for out, src in (("yx", "X3"), ("ym", "YM"), ("yg", "M3")):
+        dma("s", T[out][:], T.PF[:, 15:16] if src == "YM" else T[src][:], [src, mn, "sum"], [out], 1600)
+        in_line("stores")
+
     que = {"v": g.vector, "s": g.scalar, "t": g.tensor, "g": g, "y": g.sync}
     clock = {q: {} for q in que}
     count = {"qv": 0, "qs": 0, "qt": 0, "qg": 0}
-    lastw, readers, touch = {}, {}, {}
-    dmas, sent = [], []
+    done, touch, others, n_dma, n_sent = {}, {}, [], 0, 0
 
     def wait(q, tok):
-        sem, n, snap = tok[0], tok[1], tok[2]
+        sem, n, snap = tok
         if clock[q].get(sem, 0) >= n:
             return
         que[q].wait_ge(T.sem[sem], n)
@@ -101,50 +701,44 @@ def rank_program(g, core, T, topo):
                 clock[q][s] = m
         clock[q][sem] = n
 
-    def bank(k):
-        b = k[0] if isinstance(k, tuple) else k
-        return b if b in BANKS else None
-
-    def before(q, reads, writes, dma=False):
+    if not _ORDER:
+        _ORDER.extend(in_order(calls))
+    for i in _ORDER:
+        c = calls[i]
+        q, name, kw = c["q"], c["name"], c["kw"]
+        if name == "lands":
+            done[i] = (kw[1], len(topo.engines(helper(core), kw[0])), {})
+            others.append(done[i])
+            continue
         toks = {}
-
-        def need(tok):
+        for tok in ([done[p] for p in c["after"] if not q == calls[p]["q"] == "t"]
+                    + [tok for b in c["banks"] for e, tok in touch.get(b, {}).items() if e != q]):
             if tok[0] not in toks or toks[tok[0]][1] < tok[1]:
                 toks[tok[0]] = tok
-        for k in reads:
-            if k in lastw:
-                need(lastw[k])
-        for k in writes:
-            if k in lastw and (dma or lastw[k][3] != q):
-                need(lastw[k])
-            for tok in readers.get(k, {}).values():
-                if dma or tok[3] != q:
-                    need(tok)
-        for k in list(reads) + list(writes):
-            for e, tok in touch.get(bank(k), {}).items():
-                if e != q:
-                    need(tok)
         for tok in toks.values():
             wait(q, tok)
-
-    def after(tok, reads, writes):
-        for k in writes:
-            lastw[k] = tok
-            readers[k] = {}
-        for k in reads:
-            if k not in writes:
-                readers.setdefault(k, {})[tok[0]] = tok
-        for k in list(reads) + list(writes):
-            if bank(k):
-                touch.setdefault(bank(k), {})[tok[3]] = tok
-
-    BANKS = ["B%d" % i for i in range(8)]
-
-    def do(q, reads, writes, name, **kw):
-        before(q, reads, writes)
-        sem = "q" + q
-        count[sem] += 1
-        ins = None
+        if name == "send":
+            off_chip = topo.engines(core, kw[0])
+            if kw[4]:
+                rest = [e for e in topo.engines(core, helper(core)) if e not in off_chip][:len(off_chip)]
+                g.remote_dma_fused([RemoteDMATransfer(dst_ids=[DstId(rid=topo.addr(to)[0], pnc=topo.addr(to)[1])], dst=out, src=src,
+                                                      remote_sem=T.sem[sem], dma_engine_mask=sum(1 << e for e in engines))
+                                    for to, engines, (out, src, sem) in ((kw[0], off_chip, kw[1:4]), (helper(core), rest, kw[4]))],
+                                   local_sem=T.sem.ls)
+                n_sent += len(rest)
+            else:
+                write(helper(core) if kw[3] in [x[4] for x in HANDED] else kw[0], kw[1], kw[2], kw[3], topo.mask(core, kw[0]))
+            done[i] = (kw[3], len(off_chip), {})
+            n_sent += done[i][1]
+            others.append(done[i])
+            continue
+        if name == "dma":
+            sem = "d%d" % n_dma
+            n_dma += 1
+            que[q].dma_start(*kw).then_inc(T.sem[sem], 16)
+            done[i] = (sem, 16, dict(clock[q]))
+            others.append(done[i])
+            continue
         if name == "copy":
             ins = g.vector.tensor_copy(**kw)
         elif name == "tt":
@@ -154,9 +748,9 @@ def rank_program(g, core, T, topo):
         elif name == "act":
             ins = g.scalar.activation(**kw)
         elif name == "mm":
-            ins = g.tensor.matmul(kw["out"], kw["l"], kw["r"], kw["start"], kw["stop"])
+            ins = g.tensor.matmul(*kw)
         elif name == "fill":
-            ins = g.vector.memset(kw["ap"], kw["c"])
+            ins = g.vector.memset(*kw)
         elif name == "iota":
             ins = g.iota(**kw)
         elif name == "pick":
@@ -165,374 +759,16 @@ def rank_program(g, core, T, topo):
             ins = g.vector.tensor_reduce(**kw)
         elif name == "turn":
             ins = g.vector.transpose(**kw)
-        elif name == "scan":
+        else:
             ins = g.vector.tensor_tensor_scan(**kw)
+        sem = "q" + q
+        count[sem] += 1
         ins.then_inc(T.sem[sem], 1)
-        after((sem, count[sem], dict(clock[q]), q), reads, writes)
-
-    def dma(q, out, in_, reads, writes):
-        before(q, reads, writes, True)
-        sem = "d%d" % len(dmas)
-        que[q].dma_start(out, in_).then_inc(T.sem[sem], 16)
-        tok = (sem, 16, dict(clock[q]), "dma")
-        dmas.append(tok)
-        after(tok, reads, writes)
-
-    def send(dst, out, src, read, write, sem):
-        rid, pid, _eng = topo.addr(dst)
-        before("g", [read], [])
-        g.remote_dma(out, src, T.sem[sem], T.sem.ls, pid, rid, topo.mask(core, dst))
-        lastw[write] = (sem, len(topo.engines(core, dst)), {}, "remote")
-        sent.append(lastw[write])
-
-    def cp(out, in_, r, w):
-        do("v", r, w, "copy", out=out, in_=in_)
-
-    def tt(out, a, b, op, r, w):
-        do("v", r, w, "tt", out=out, in0=a, in1=b, op=op)
-
-    def ts(out, a, s1, op0, r, w, s2=None, op1=None):
-        if op1 is None:
-            do("v", r, w, "ts", out=out, in0=a, scalar1=s1, scalar2=None, op0=op0)
-        else:
-            do("v", r, w, "ts", out=out, in0=a, scalar1=s1, scalar2=s2, op0=op0, op1=op1)
-
-    def tr(out, in_, r, w):
-        do("v", r, w, "turn", out=out, in_=in_)
-
-    def fill(ap, c, w):
-        do("v", [], w, "fill", ap=ap, c=c)
-
-    def act(out, in_, r, w, func=AF.Copy, **kw):
-        do("s", r, w, "act", out=out, in_=in_, func=func, **kw)
-
-    def mm(out, l, r, start, stop, rd, wr):
-        do("t", rd, wr, "mm", out=out, l=l, r=r, start=start, stop=stop)
-
-    def iota(out, pattern, base, cm, w, small=True):
-        if small:
-            do("g", [], w, "iota", out=out, pattern=pattern, base=base, channel_multiplier=cm,
-               allow_small_or_imprecise_dtypes=True)
-        else:
-            do("g", [], w, "iota", out=out, pattern=pattern, base=base, channel_multiplier=cm)
-
-    def pick(out, in_, pattern, op, other, r, w, base=0):
-        do("g", r, w, "pick", out=out, in_=in_, pattern=pattern, compare_op=op, fill=other, base=base, channel_multiplier=-1)
-
-    def some(steps, n):
-        for _ in range(n):
-            next(steps, None)
-
-    def half(h):
-        return slice(128 * h, 128 * h + 128)
-
-    dma("y", T.X0[:], T.xw[:], [], [("X0", 0), ("X0", 1)])
-    dma("s", T.WI[:], T.wts[:], [], ["WI"])
-    dma("y", T.LX[:, 0:W], T.lex[:], [], ["LX"])
-    dma("s", T.THI[:], T.th[:], [], ["THI"])
-    dma("y", T.LM[:, 0:W], T.mng[:], ["LX"], ["LM"])
-    dma("y", T.M0[:], T.gw[:], [], ["M0"])
-
-    col = [[1, 128]]
-    iota(T.PI[:, 0:1], [[0, 1]], 0, 1, ["PI"], False)
-    iota(T.MG[:], [[1, 8], [0, 16]], 0, 0, ["MG"])
-    fill(T.ONES[:], 1.0, ["ONES"])
-    ts(T.PI[:, 1:2], T.PI[:, 0:1], 4, OP.arith_shift_right, ["PI"], ["PI1"])
-    ts(T.PI[:, 2:3], T.PI[:, 0:1], 15, OP.bitwise_and, ["PI"], ["PI2"])
-    fill(T.CN[:], -65536.0, ["CN"])
-    fill(T.C5120[:], 5120.0, ["C5120"])
-    cp(T.PF[:, 0:2], T.PI[:, 1:3], ["PI1", "PI2"], ["PF"])
-    fill(T.ZERO[:], 0.0, ["ZERO"])
-    pG, pL = T.PF[:, 0:1], T.PF[:, 1:2]
-    pick(T.ID[:], T.ONES[:, 0:128], col, OP.is_equal, 0.0, ["ONES"], ["ID"])
-    ts(T.BO[:], T.MG[:], pG, OP.is_equal, ["MG", "PF"], ["BO"])
-    fill(T.SK[:, 0:1024], 0.0, ["SK"])
-    for e in (2, 3):
-        act(T.SK[:, 512 * e:512 * e + 512], T.ONES[:], ["ONES"], ["SK1"], scale=0.0)
-    pick(T.MNE[:], T.BO[:], col, OP.not_equal, 0.0, ["BO"], ["MNE"])
-    pick(T.BOX[:], T.BO[:], col, OP.not_equal, -15.0, ["BO"], ["BOX"])
-    ts(T.BO64[:], T.BO[:], 64.0, OP.mult, ["BO"], ["BO64"])
-    ts(T.IDN4096[:], T.ID[:], -4096.0, OP.mult, ["ID"], ["IDN4096"])
-    iota(T.T3[:], [[1, 4]], 0, 0, ["T3"])
-    iota(T.PC[:], [[-1, 2], [100, 2]], 0, 0, ["PC"])
-    iota(T.JI[:], [[1, 16], [-100, 2]], 0, 0, ["JI"])
-    for e in range(8):
-        pick(T.SK[:, 16 * e:16 * e + 129 * 15 + 1:129], T.BOX[:, 16 * e:16 * e + 16], [[0, 16]], OP.is_ge, 0.0, ["BOX", "SK", "SK1"],
-             [("SK", e)], 127)
-    lastw["SK"] = lastw[("SK", 7)]
-    pick(T.SL[:], T.BO[:], col, OP.is_gt, 0.0, ["BO"], ["SL"])
-
-    def lowest(t):
-        nm = "LT%d" % t
-        pick(T[nm][:], T.SL[:], col, OP.not_equal, -1.0, ["SL"], [nm])
-        for src, op, other, base in (("BO64", OP.is_gt, 1.0, t), (None, OP.is_ge, 0.0, 15), (None, OP.not_equal, -16.0, t)):
-            pick(T[nm][:, t::16], T[src][:, ::16] if src else T[nm][:, t::16], [[16, 8]], op, other, [nm, "BO64"], [nm], base)
-    lowest(0)
-    iota(T.MP[:], [[2, 4], [100, 2], [0, 16]], 0, 0, ["MP"])
-    iota(T.IO64[:], [[1, 64]], 0, 0, ["IO64"])
-    pick(T.RX[:], T.ONES[:], [[1, 4], [0, 8], [4, 16]], OP.is_equal, 0.0, ["ONES"], ["RX"])
-    lowest(1)
-    lowest(2)
-    iota(T.NUM[:], [[-1, 256]], -1, 0, ["NUM"])
-    cp(T.WF[:], T.WI[:], ["WI"], ["WF"])
-    ts(T.ID128[:], T.ID[:], 128.0, OP.mult, ["ID"], ["ID128"])
-    ts(T.W1[:], T.MNE[:], T.WF[:, 0:1], OP.mult, ["MNE", "WF"], ["W1"])
-    ts(T.W2[:], T.MNE[:], T.WF[:, 1:2], OP.mult, ["MNE", "WF"], ["W2"])
-    ts(T.W32[:], T.MNE[:], T.WF[:, 0:1], OP.mult, ["MNE", "WF"], ["W32"], 32.0, OP.mult)
-    ts(T.IDN[:], T.ID[:], -1.0, OP.mult, ["ID"], ["IDN"])
-    ts(T.BO8192[:], T.BO[:], 8192.0, OP.mult, ["BO"], ["BO8192"])
-    ts(T.B15[:], T.BO[:, ::16], 1.5, OP.mult, ["BO"], ["B15"])
-    ts(T.BNA[:], T.BO[:, ::16], -1.0 / 4096, OP.mult, ["BO"], ["BNA"])
-    ts(T.PF[:, 8:9], pL, -4.0, OP.mult, ["PF"], ["SQB"], -1.5, OP.add)
-
-    def last_constants():
-        yield ts(T.RC[:], T.JI[:], pL, OP.is_equal, ["JI", "PF"], ["RC"], -2.0, OP.mult)
-        yield ts(T.RA[:], T.JI[:], pL, OP.is_gt, ["JI", "PF"], ["RA"], 2.0 ** -16 - 1, OP.mult)
-        yield ts(T.RB[:], T.JI[:], pL, OP.is_gt, ["JI", "PF"], ["RB"], 2.0 ** 16 - 1, OP.mult)
-        yield ts(T.RC[:], T.RC[:], 1.0, OP.add, ["RC"], ["RC"])
-        yield ts(T.PD[:], T.PC[:], pG, OP.add, ["PC", "PF"], ["PD"])
-        yield fill(T.RR[:, 0:1], 0.0, ["RR0"])
-        yield tt(T.RA[:], T.RA[:], T.RC[:], OP.add, ["RA", "RC"], ["RA"])
-        yield tt(T.RB[:], T.RB[:], T.RC[:], OP.add, ["RB", "RC"], ["RB"])
-        yield ts(T.THR[:], T.T3[:], pL, OP.not_equal, ["T3", "PF"], ["THR"], -0.5, OP.mult)
-        yield ts(T.THF[:], T.THI[:], -2048.0, OP.add, ["THI"], ["THF"], 1.0 / 4096, OP.mult)
-        tt(T.RR[:, 1:32], T.RA[:, 0:31], T.RB[:, 1:32], OP.mult, ["RA", "RB"], ["RR"])
-        for n in (32, 64, 128, 256):
-            pick(T.RR[:, n:2 * n], T.RR[:, 0:n], [[0, n]], OP.is_ge, 0.0, ["RR", "RR0"], ["RR"], 127)
-        yield
-        for i in range(4):
-            yield ts(T["PM%d" % i][:], T.MP[:], T.PD[:, i:i + 1], OP.is_equal, ["MP", "PD"], ["PM%d" % i])
-        yield ts(T.THB[:], T.BO[:, ::16], T.THF[:], OP.mult, ["BO", "THF"], ["THB"])
-        for i in range(4):
-            yield ts(T["PN%d" % i][:], T["PM%d" % i][:], 64.0, OP.mult, ["PM%d" % i], ["PN%d" % i])
-        yield ts(T.PF[:, 11:12], pL, float(W), OP.add, ["PF"], ["SPARE"])
-        yield ts(T.PF[:, 12:13], pL, float(W + 16), OP.add, ["PF"], ["SPARE"])
-        yield fill(T.EQ[:, 1:256:2], 0.0, ["EQ0"])
-
-    chores = last_constants()
-
-    def scatter(lex, src):
-        for c in range(7, -1, -1):
-            yield cp(T[lex][:].indirect(T.OFU[:, 2 * c:2 * c + 2]), T[src][:, 32 * c:32 * c + 32], ["OFU", lex, src], [lex])
-
-    ZB = ("B4", "B0")
-
-    def hash_sums(X):
-        TX = T[X]
-        for b in ZB:
-            mm(T[b][:, 0:4, :], T.CN[:], T.ONES[:, 0:128], True, False, ["CN", "ONES"], [b])
-        mm(T.B3[:, 0:256], T.C5120[:], T.ONES[:, 0:256], True, False, ["C5120", "ONES"], ["B3"])
-
-        def sums(b, o, w0, n, alone):
-            for j, w in ((0, "W1"), (1, "W2")):
-                mm(T[b][:, o + n * j:o + n * j + n], T[w][:], TX[:, w0:w0 + n], alone, alone, [w, (X, w0 // 128)], [b])
-
-        def times32(h):
-            mm(T[ZB[h]][:, 0:4, :], T.W32[:], TX[:, half(h)], False, True, ["W32", (X, h)], [ZB[h]])
-        sums("B7", 0, 0, 64, True)
-        sums("B7", 128, 64, 64, True)
-        times32(0)
-        sums("B5", 0, 128, 128, True)
-        sums("B3", 0, 128, 128, False)
-        act(T.Q[:], T.B5[:, 0:256], ["B5"], ["Q"], func=AF.Identity, scale=1.0 / 4096, bias=159.5 + 1.0 / 8192)
-        times32(1)
-        mm(T.B1[:, 0:256], T.ID[:], TX[:], True, True, ["ID", (X, 0), (X, 1)], ["B1"])
-        mm(T.B3[:, 0:256], T.IDN4096[:], T.Q[:], False, True, ["IDN4096", "Q"], ["B3"])
-        act(T.UP[:], T.B3[:, 128:256], ["B3"], ["UP"])
-
-    def hashes(c):
-        s, u, z = slice(64 * c, 64 * c + 64), slice(128 * c, 128 * c + 128), slice(2 * (c % 2), 2 * (c % 2) + 2)
-        if c < 2:
-            yield cp(T.UI[:, u], T.B7[:, u], ["B7"], [("UI", c)])
-            yield ts(T.UI[:, u], T.UI[:, u], 4095, OP.bitwise_and, [("UI", c)], [("UI", c)])
-            yield tt(T.PR[:, s], T.UI[:, 128 * c:128 * c + 64], T.UI[:, 128 * c + 64:128 * c + 128], OP.mult, [("UI", c)], [("PR", c)])
-        else:
-            u = slice(64 * c - 128, 64 * c - 64)
-            yield tt(T.PR[:, s], T.UP[:, u], T.B3[:, u], OP.mult, ["UP", "B3"], [("PR", c)])
-        yield tt(T.ZI[:, s], T.PR[:, s], T[ZB[c // 2]][:, z, :], OP.add, [("PR", c), ZB[c // 2]], [("ZI", c)])
-        yield ts(T.HI[:, s], T.ZI[:, s], 5, OP.arith_shift_right, [("ZI", c)], [("HI", c)], 4095, OP.bitwise_and)
-        yield cp(T.HU[:, s], T.HI[:, s], [("HI", c)], [("HU", c)])
-
-    hash_sums("X0")
-    some(zip(hashes(0), hashes(1)), 6)
-    some(chores, 8)
-    late = iter(())
-
-    for t in range(3):
-        xn, mn = "XN%d" % t, "MN%d" % t
-        X, M, X1, M1 = "X%d" % t, "M%d" % t, "X%d" % (t + 1), "M%d" % (t + 1)
-        TX, TM = T[X], T[M]
-        dst = T.cores[(rank + (3 if t < 2 else 2)) % n_ranks]
-
-        def compare(c):
-            o = 1024 * c
-            for k in range(16):
-                tt(T.EB[:, o + 64 * k:o + 64 * k + 64], T.CB[:, o + k:o + 1024:16], T.B1[:, 64 * c:64 * c + 64], OP.not_equal,
-                   [("CB", c), "CBV", "B1"], [("EB", c, k // 2)])
-                if k % 2 == 1:
-                    for j in (k - 1, k):
-                        mm(T.B2[:, 64 * c:64 * c + 64], T.SK[:, 128 * j:128 * j + 128],
-                           T.EB[:, o + 64 * j:o + 64 * j + 64], j == 0, j == 15, ["SK", ("EB", c, j // 2)], ["B2"])
-
-        for i, _ in enumerate(zip(hashes(2), hashes(3))):
-            some(chores, i < 3)
-        def gather(how, w0, w1, key):
-            how(T.CB[:, 16 * w0:16 * w1], T.LX[:, 0:W].indirect(T.HU[:, w0:w1]), ["LX", ("HU", w0 // 64)], [key])
-        for c in range(3):
-            gather(act, 64 * c, min(64 * c + 64, 256 - SHARE[t]), ("CB", c))
-        gather(cp, 192, 256, ("CB", 3))
-        if SHARE[t] > 64:
-            gather(cp, 256 - SHARE[t], 192, "CBV")
-        ts(T.H16[:], T.HU[:], -2048.0, OP.add, [("HU", c) for c in range(4)], ["H16"])
-        mm(T.B6[:, 256:512], T.ID[:], T.H16[:], True, True, ["ID", "H16"], [("B6", "H")])
-        for c in ORDER:
-            compare(c)
-        ts(T.PB[:], T.B2[:, 0:256], -11.5, OP.is_le, ["B2"], ["PB"])
-        lt = "LT%d" % t
-        mm(T.B2[:, 256:512], T[lt][:], T.PB[:], True, True, [lt, "PB"], ["B2"])
-        mm(T.B3[:, 0:256], T.BO[:], T.PB[:], True, True, ["BO", "PB"], ["B3"])
-        some(late, 2)
-        some(chores, 4)
-        ts(T.FB[:], T.B2[:, 256:512], T.THR[:, t:t + 1], OP.is_le, ["B2", "THR"], ["FB"])
-        act(T.NH[:], T.B3[:, 0:256], ["B3"], ["NH"], func=AF.Relu, scale=-128.0, bias=64.0)
-        some(late, 1)
-        some(chores, 2)
-        tt(T.FH[:], T.FB[:], T.B6[:, 256:512], OP.mult, ["FB", ("B6", "H")], ["FH"])
-        for i in range(4):
-            s, c = i // 2, i % 2
-            mm(T.B4[:, 0:8, 16 * s:16 * s + 16], T["PM%d" % i][:], T.FH[:, :, 16 * c:16 * c + 16], c == 0, c == 1,
-               ["PM%d" % i, "FH"], ["B4"])
-        tt(T.FX[:], T.FB[:], T.B1[:, 0:256], OP.mult, ["FB", "B1"], ["FX"])
-        for h in range(2):
-            mm(T.B3[:, 256 + 8 * h:264 + 8 * h], T.FX[:, half(h)], T.BO[:, ::16], True, False, ["FX", "BO"], ["B3"])
-            mm(T.B3[:, 256 + 8 * h:264 + 8 * h], T.NH[:, half(h)], T.BO[:, ::16], False, True, ["NH", "BO"], ["B3"])
-        some(late, 8)
-        some(chores, 5)
-        tr(T.KB[:], T.B4[:, 0:8, :], ["B4"], ["KB"])
-        mm(T.B7[:, 256:512], T.BO[:], T.FX[:], True, False, ["BO", "FX"], ["B7"])
-        mm(T.B7[:, 256:512], T.ID[:], T.NH[:], False, True, ["ID", "NH"], ["B7"])
-        mm(T.B2[:, 0:256], T.ID[:], TX[:], True, False, ["ID", X], ["B2"])
-        mm(T.B2[:, 0:256], T.ID[:], T.NH[:], False, True, ["ID", "NH"], ["B2"])
-        mm(T.B4[:, 8:16, :], T.ZERO[:], T.ONES[:, 0:256], True, False, ["ZERO", "ONES"], [("B4", 1)])
-
-        def coded(pm, src):
-            for i in range(4):
-                s, c = i // 2, i % 2
-                mm(T.B4[:, 8:16, 16 * s:16 * s + 16], T[pm + str(i)][:], T[src][:, half(c)], False, src == "FC" and i == 3,
-                   [pm + str(i), src], [("B4", 1)])
-
-        def hot_x(c0, c1):
-            for c in range(c0, c1):
-                ts(T.OHX[:, 64 * c:64 * c + 64], T.IO64[:], T.B3[:, 256 + c:257 + c], OP.is_equal, ["IO64", "B3"], [("OHX", c)])
-        coded("PN", "FX")
-        mm(T.B0[:, 0:8, :], T.BO[:], T.FH[:], True, False, ["BO", "FH"], ["B0"])
-        mm(T.B0[:, 0:8, :], T.ID128[:], T.NH[:], False, False, ["ID128", "NH"], ["B0"])
-        hot_x(0, 2)
-        ts(T.LF[:], T.KB[:, :, ::16], 2048.0, OP.add, ["KB"], ["LF"])
-        hot_x(2, 4)
-        tt(T.SUB[:], T.LM[:, 0:W].indirect(T.LF[:, 0:16]), TM[:], OP.subtract, ["LM", M, "LF"], ["SUB"])
-        act(T.ABS[:], T.SUB[:], ["SUB"], ["ABS"], func=AF.Abs)
-        act(T.AQ[:], T.B7[:, 256:512], ["B7", "SQB"], ["AQ"], func=AF.Abs, bias=T.PF[:, 8:9])
-        tt(T.FC[:], T.LX[:, 0:W].indirect(T.LF[:, 0:16]), T.FB[:], OP.mult, ["LX", "LF", "FB"], ["FC"])
-        hot_x(4, 16)
-        for h in range(2):
-            mm(T.B5[:, 8 * h:8 * h + 8], T.FC[:, half(h)], T.BO[:, ::16], True, True, ["FC", "BO"], ["B5"])
-        for h in range(2):
-            o = T.B5[:, 16 + 8 * h:24 + 8 * h]
-            for i, (src, w) in enumerate((("FB", "THB"), ("FB", "B15"), ("ABS", "BNA"))):
-                mm(o, T[src][:, half(h)], T[w][:], i == 0, i == 2, [src, w], ["B5"])
-        coded("PM", "FC")
-        act(T.XA[:], T.B2[:, 0:256], ["B2"], ["XA"])
-        act(T.MK[:], T.AQ[:], ["AQ"], ["MK"], func=AF.Relu, scale=-2.0, bias=4.0)
-        act(T.D16[:], T.SUB[:], ["SUB"], ["D16"], func=AF.Identity, scale=0.5, bias=1535.75)
-        act(T.DM[:], T.D16[:], ["D16"], ["DM"], func=AF.Identity, bias=-1536.0)
-        for c in range(16):
-            s = slice(64 * c, 64 * c + 64)
-            ts(T.OHC[:, s], T.IO64[:], T.B5[:, c:c + 1], OP.is_equal, ["IO64", "B5"], [("OHC", c)], T.B5[:, 16 + c:17 + c], OP.is_ge)
-            rd = [("OHX", c), ("OHC", c)]
-            if ONE:
-                mm(T.B7[0:64, 0:64], T.OHX[:, s], T.OHC[:, s], c == 0, c == 15, rd, ["B7"])
-                continue
-            mm(T.B6[0:64, 0:64], T.OHX[:, s], T.OHC[:, s], c == 0, False, rd, ["B6"])
-            mm(T.B6[0:64, 0:64], T.OHC[:, s], T.OHX[:, s], False, c == 15, rd, ["B6"])
-        tr(T.KC[:], T.B4[:, 8:16, :], [("B4", 1)], ["KC"])
-        if ONE:
-            cp(T.TA[0:64, :], T.B7[0:64, 0:64], ["B7"], ["TA"])
-            mm(T.B6[0:64, 0:64], T.TA[0:64, :], T.ID[0:64, 0:64], True, False, ["TA", "ID"], ["B6"])
-            mm(T.B6[0:64, 0:64], T.ID[0:64, 0:64], T.TA[0:64, :], False, True, ["TA", "ID"], ["B6"])
-        for o in range(2):
-            act(T.KL[:, 8 * o:8 * o + 8], T.KB[:, :, 16 * o], ["KB"], ["KL"], func=AF.Identity, scale=1.0 / 8192, bias=1.25)
-        some(chores, 2)
-        for h in range(2):
-            cp(T.CI[:, 8 * h:8 * h + 8], T.KC[:, 16 * h::32], ["KC"], ["CI"])
-        cp(T.TB[0:64, :], T.B6[0:64, 0:64], ["B6"], ["TB"])
-        for r in range(4):
-            mm(T.B6[:, 256 + 64 * r:320 + 64 * r], T.RX[0:64, 128 * r:128 * r + 128], T.TB[0:64, :], True, True, ["RX", "TB"], ["B6"])
-        for i, (l, src) in enumerate((("ID", X), ("IDN", "FX"), ("ID", "FC"))):
-            mm(T.B1[:, 256:512], T[l][:], T[src][:], i == 0, False, [l, src], ["B1"])
-        mm(T.B3[:, 0:256], T.ID[:], T.NH[:], True, False, ["ID", "NH"], ["B3"])
-        ts(T.CI[:], T.CI[:], 255, OP.bitwise_and, ["CI"], ["CI"])
-        some(chores, 3)
-        cp(T.CL[:], T.CI[:], ["CI"], ["CL"])
-        cp(T.TW[:], T.B6[:, 256:512], ["B6"], ["TW"])
-        tt(T.GT[:], T.TW[:].indirect(T.CL[:, 0:16]), T.MK[:], OP.mult, ["TW", "CL", "MK"], ["GT"])
-        ends = [(T.B1[:, 256:512], "BO64", "B1"), (T.B0[:, 0:8, :], "BO8192", "B0"), (T.B3[:, 0:256], "BO", "B3")]
-        for o, l, b in ends if t < 2 else [ends[1], ends[0], ends[2]]:
-            mm(o, T[l][:], T.GT[:], False, True, [l, "GT"], [b])
-
-        def equal():
-            for o, a, b in ((0, 0, 0), (256, 16, 16), (257, 16, 0)):
-                tt(T.EQ[:, o:o + 255:2], T.KB[:, :, a:a + 16], T.B0[:, 0:8, b:b + 16], OP.is_equal, ["KB", "B0"], ["EQ"])
-        if t == 2:
-            equal()
-        tt(T[xn][:], T.XA[:], T.B1[:, 256:512], OP.min, ["XA", "B1"], [xn])
-        if HALVES and t < 2:
-            for h in range(2):
-                send(dst, T[X1][:, half(h)], T[xn][:, half(h)], xn, (X1, h), ("ax", "ay")[h] + str(t + 1))
-        else:
-            send(dst, T[X1][:], T[xn][:], xn, (X1, 0), "ax" + str(t + 1))
-            lastw[(X1, 1)] = lastw[(X1, 0)]
-        act(T.B5[:, 256:512], T.B3[:, 0:256], ["B3"], ["B5"], func=AF.Relu, scale=-1.0, bias=1.0)
-        if t < 2:
-            equal()
-        do("v", ["RR", "EQ", "EQ0"], ["SC"], "scan", out=T.SC[:], data0=T.RR[:], data1=T.EQ[:], initial=0.0, op0=OP.mult, op1=OP.add)
-        mm(T.B2[:, 0:256], T.ID[:], TM[:], True, False, ["ID", M], ["B2"])
-        for j in range(3 if t == 2 else 0):
-            mm(T.B6[:], T.ID[:], T.LM[:, 512 * j:512 * j + 512], j == 0, False, ["ID", "LM"], ["B6"])
-        tt(T.GD[:], T.DM[:], T.B5[:, 256:512], OP.mult, ["DM", "B5"], ["GD"])
-        mm(T.B2[:, 0:256], T.ID[:], T.GD[:], False, True, ["ID", "GD"], ["B2"])
-        act(T[mn][:], T.B2[:, 0:256], ["B2"], [mn])
-        tt(T.Y[:], T.SC[:, 31::32], T.KL[:], OP.add, ["SC", "KL"], ["Y"])
-        for o in range(2):
-            ts(T.OFU[:, o::2], T.Y[:, 8 * o:8 * o + 8], 8192.0, OP.mult, ["Y", "SPARE"], ["OFU"], T.PF[:, 11 + o:12 + o], OP.min)
-        letters, late = scatter("LX", xn), scatter("LM", mn)
-        if t < 2:
-            hash_sums(X1)
-            before("g", [(X1, 0), (X1, 1)], [])
-            send(dst, T[M1][:], T[mn][:], mn, M1, "am" + str(t + 1))
-            some(letters, 2)
-            some(zip(late, letters), BOTH[t])
-            for _ in zip(hashes(0), hashes(1)):
-                next(letters, None)
-
-    numbers = scatter("EB", "NUM")
-    send(dst, T[M1][:], T[mn][:], mn, M1, "am3")
-    for j in range(3, 8):
-        mm(T.B6[:], T.ID[:], T.LM[:, 512 * j:512 * j + 512], False, j == 7, ["ID", "LM"], ["B6"])
-    for i, (l, src) in enumerate((("IDN", "SUB"), ("ID", "DM"))):
-        mm(T.B7[:, 0:256], T[l][:], T[src][:], i == 0, i == 1, [l, src], ["B7"])
-    act(T.B6[:], T.B6[:], ["B6"], ["B6", "B3"], accum_out=T.B3[:, 256:257])
-    dma("s", T.yx[:], T.X3[:], [("X3", 0), ("X3", 1)], ["yx"])
-    some(zip(numbers, letters), 8)
-    dma("y", T.yl[:], T.LX[:, 0:W], ["LX"], ["yl"])
-    tt(T.PB[:], T.EB[:, 0:W].indirect(T.LF[:, 0:16]), T.NUM[:], OP.is_equal, ["EB", "NUM", "LF"], ["PB"])
-    cp(T.WD[:, 256:257], T.B3[:, 256:257], ["B3"], ["WD1"])
-    tt(T.WD[:, 0:256], T.PB[:], T.B7[:, 0:256], OP.mult, ["PB", "B7"], ["WD"])
-    do("v", ["WD", "WD1"], ["YM"], "reduce", out=T.YM[:], in_=T.WD[:], axis=AxisListType.X, op=OP.add)
-    dma("s", T.ym[:], T.YM[:], ["YM"], ["ym"])
-    dma("s", T.yg[:], T.M3[:], ["M3"], ["yg"])
-    for sem in ("qv", "qs", "qt", "qg"):
-        wait("g", (sem, count[sem], {}, ""))
-    for tok in dmas + sent:
+        done[i] = (sem, count[sem], dict(clock[q]))
+        for b in c["banks"]:
+            touch.setdefault(b, {})[q] = done[i]
+    for sem in count:
+        wait("g", (sem, count[sem], {}))
+    for tok in others:
         wait("g", tok)
-    g.wait_ge(T.sem.ls, sum(tok[1] for tok in sent))
+    g.wait_ge(T.sem.ls, n_sent)

@@ -4,34 +4,36 @@ from concourse.mybir import AluOpType, AxisListType, ActivationFunctionType
 OP = AluOpType
 AF = ActivationFunctionType
 W, K = 4096, 256
-SHARE = (32, 32, 32)
-CODE_FIRST = True
-CYCLE, GATHER, SCATTER = 0.83, 1.56, 3.8
+_P = ((224, 256, 1), (208, 224, 1), (192, 208, 0), (128, 192, 0), (0, 64, 0), (64, 96, 0), (96, 128, 0))
+PIECES = (_P, _P, _P)
+ONV = ("tw", "g0", "g1", "x1")
+IDLE = ()
+ZERO = 4
+LETTERS, NONE = ("B4", "B0"), ("B4", "B4")
+LAID = ("B7", "B1"), ("B2", "B0"), ("B2", "B5"), ("B7", "B5"), ("B1", "B0"), ("B7", "B6")
+TEXT = "lane1 letters1 lane0 place1 lookup1 ahead1 coded1 place0 lookup0 coded0 hot1 letters0 hot0 ahead0 table1 table0".split()
+CYCLE = 0.83
 COLUMN = 0.5
 CALL = 120
-FAR = 2600
-FARM = 5000
-FARX = 2600
-FARE = 3000
-RELAY = ("am1", "am2")
-FUSED = False
-AHEAD = (1,)
 ISSUE = 200
-LOADM = 7500
+SCAN = False
+SPLIT = 2
+LOWER = 0
+HOME = 900
+FAR, MOVING, FOLD = 1600, 700, 1.6
+LOADX, LOADM, LAST = 5000, 6200, 4000
+FIRST = 0
 SLOWG = 1.5
-ONV = ()
-WHOLE = ()
-LOADX = 5000
-ZERO = 4
-IDLE = 2
-EARLY = (0, 0)
-LAST = 2600
-ROUNDS = 2
-TRIES = 0
-SOON = (0, 2500, 500)
-STEPS = (1, 0, 3, -2, 8, -6)
-CASES = ((1, 0.85, -50, 250, 0.8, 1), (1, 1.1, 10, 150, 1.1, 1.2), (1.4, 1.3, 0, 250, 1, 1))
-PLANS = ((1, 1, 0, 180, 1, 1, 0.7),)
+CASES = ((1.2, 1.2, 0, 210, 1.3, 1, 1.56, 3.8), (1, 1, 0, 200, 1, 1, 1.56, 3.8), (1.1, 1.2, 0, 200, 1.6, 1.2, 1.9, 2.5),
+         (1.3, 1.3, -30, 220, 1.2, 1, 1.2, 5.2), (1.4, 1.4, 0, 200, 1.2, 1, 1.9, 4.5))
+PLANS = ((1.15, 1.15, 0, 210, 1.25, 1, 1.56, 3.8),)
+AT = {"offsets 1": -95, "offsets 0": -71, "gather": -102, "lane1": -91, "f 1": -70, "np 1": -63, "letters1": -43, "lane0": -67, "f 0": -42,
+      "np 0": -36, "place1": -58, "lookup1": -45, "ahead1": -34, "coded1": -44, "place0": -31, "lookup0": -22, "coded0": -24, "hot1": -40,
+      "letters0": -26, "hot0": -25, "ahead0": -17, "table1": -23, "table0": -12, "mask": -13, "codes": -3, "d16": -5, "spread": 0,
+      "ends 1": -1, "change 1": 4, "letters out 1": 4, "who 1": 18, "ends 0": 0, "change 0": 30, "letters out 0": 24, "who 0": 24,
+      "merged 1": 10, "merged 0": 28, "kept": 12, "letters 1": 29, "letters 0": 43, "rest 1": 35, "rest 0": 50, "meanings": 59, "numbers": 35, "xf 1": -62, "xf 0": -38}
+MOVE, SLACK, SEED = 1500, 250, 7
+PACKS, SHAKE, WINDOW = 3200, (300, 100, 600), 6000
 _NOTE = []
 
 _S, _ORDER = {}, []
@@ -43,52 +45,53 @@ def _sb(name, cols, dtype="bfloat16"):
 
 _sb("LX", W + 32)
 _sb("LM", W + 32)
-for _n in ("X0", "M0", "X1", "M1", "X2", "M2", "X3", "M3", "XN0", "XN1", "XN2", "MN0", "MN1", "MN2"):
+for _n in ("X0", "M0", "M1", "M2", "X3", "M3", "XN", "MN0", "MN1", "MN2"):
     _sb(_n, K)
+_sb("MA", 3 * K)
 for _n in ("MG", "MP"):
     _sb(_n, 128, "float32")
 _sb("PI", 4, "int32")
 _sb("PF", 16, "float32")
-for _n in ("THR", "T3", "PC", "LE", "LL", "QS"):
+for _n in ("T3", "PC"):
     _sb(_n, 4, "float32")
+_sb("LE", 12, "float32")
 _sb("WI", 2, "int32")
 _sb("WF", 2, "float32")
 _sb("THI", 1, "int32")
-for _n in ("BO", "BO64", "BO8192", "BON", "ID", "IDN", "ID128", "IDN64", "SL", "MNE", "BOX", "W1", "W2", "W132", "W232", "LT0", "LT1", "LT2",
-           "IDN4096"):
+for _n in ("BO", "BO64", "BON64", "BO8192", "ZR", "BON128", "BON512", "BO512", "ID", "IDN", "SL", "MNE", "BOX", "W1", "W2", "W132", "W232",
+           "LTH", "LTX", "LTF", "BT0", "BT1", "BT2", "IDN4096"):
     _sb(_n, 128)
 _sb("ONES", 256)
-_sb("CT", 640)
-_sb("BO12288", 128)
-_sb("UN", 256)
-for _n in ("THB", "B15", "BNA", "BPA"):
+_sb("CT", 1152)
+for _n in ("THB", "B30", "BNA", "BPA", "BA", "BC"):
     _sb(_n, 8, "float16")
 for _n in range(4):
     _sb("PM%d" % _n, 128, "float16")
     _sb("PN%d" % _n, 128, "float16")
 _sb("SK", 2048)
 _sb("RX", 512)
-_sb("QX", 512, "float16")
 _sb("IO64", 64)
-_sb("QB", 8, "float32")
-_sb("QQ", 192, "float32")
-_sb("NUM", 256)
-for _n in ("JI", "RA", "RB", "RC"):
-    _sb(_n, 32, "float32")
-_sb("RR", 256)
+for _n in ("NUM", "SN"):
+    _sb(_n, 256, "float32")
+_sb("WN", W + 32, "float32")
+_sb("RW", 64, "float32")
+_sb("RR", 50)
 for _n in ("EQ", "SC"):
-    _sb(_n, 512)
+    _S[_n] = ("sbuf", [128, 8, 50], "float32")
 for _n in ("PR", "ZI", "HI"):
     _sb(_n, 256, "int32")
 _sb("UP", 256, "float32")
 _sb("Q", 512)
-for _n in ("H0", "H1", "H2", "HN0", "HN1"):
+for _n in ("H0", "H1", "H2"):
     _sb(_n, 256, "uint16")
-for _n in ("H16", "FB", "FX", "FC", "D16", "FQ"):
+for _n in ("P0", "P1", "P2", "X1", "X2", "N16", "FC", "D16", "RL"):
     _sb(_n, 256, "float16")
-for _n in ("PB", "NH", "XA", "SUB", "RL", "AQ", "MK", "TW", "GT", "DM"):
+for _n in range(2):
+    _sb("OUT%d" % _n, 1024, "float16")
+    _sb("HN%d" % _n, 512, "uint16")
+_sb("XF", 512, "float16")
+for _n in ("XR", "PB", "NP", "XA", "SUB", "MK", "TW", "GT"):
     _sb(_n, 256)
-_sb("GD", 256)
 _sb("CB", W)
 _sb("EB", W + 32)
 _S["FH"] = ("sbuf", [128, 8, 32], "float16")
@@ -96,8 +99,6 @@ _S["KB"] = ("sbuf", [128, 8, 32], "float32")
 _S["KC"] = ("sbuf", [128, 8, 32], "float32")
 _S["CI"] = ("sbuf", [128, 2, 8], "int32")
 _sb("WD", 257, "float32")
-_S["KL"] = ("sbuf", [128, 2, 8], "float32")
-_S["Y"] = ("sbuf", [128, 2, 8], "float32")
 for _n in ("LF", "CL", "OFU"):
     _sb(_n, 16, "uint16")
 _sb("OHX", 1024)
@@ -105,21 +106,28 @@ _sb("OHC", 1024)
 _sb("TB", 64)
 BANKS = ["B%d" % _i for _i in range(8)]
 for _n in BANKS:
-    _S[_n] = ("psum", [128, 16, 32], "float32")
+    _S[_n] = ("psum", [128, 16, 32] if _n != "B0" else [128, 512], "float32")
+for _n in ("DI", "SO"):
+    _sb(_n, 256, "float32")
 SCRATCH = _S
 SEMAPHORES = (["qv", "qs", "qt", "qg", "ls"] + ["d%d" % _i for _i in range(11)]
               + [_n + str(_i) for _n in ("aw", "ax", "ay", "az", "am") for _i in range(1, 4)])
-HANDED = ([(_t, _n + str(_t + 1), _a, _b, _s + str(_t + 1)) for _t in range(2)
-           for _n, _a, _b, _s in (("X", 128, 256, "ax"), ("X", 0, 128, "aw"), ("M", 0, 256, "am")) if _s + str(_t + 1) in RELAY]
-          + [(2, "X3", 0, 256, "ax3")] * ("end" in RELAY))
+HANDED = {"am1": (0, "M1", 0, 256), "am2": (1, "M2", 0, 256)}
+AHEAD = (0, 1)
+SCALED = 7
+FOLDS = ()
+HALF = ()
+SPARE = True
 
 
 def in_order(calls):
     n = len(calls)
-    queue, banks, needs = [c["q"] for c in calls], [c["banks"] for c in calls], [c["after"] | set(c["behind"]) for c in calls]
+    queue = [c["q"] for c in calls]
+    banks = [c["banks"] if c["q"] != "t" else () for c in calls]
 
-    def priced(slow, column, call, hop, far, load):
-        cost = [c["cost"] * (column if c["q"] == "t" else slow) + (call if c["name"] == "act" else 0) for c in calls]
+    def priced(slow, column, call, hop, far, load, gather, scatter):
+        cost = [(c["cost"] + CYCLE * (gather * c["picks"] + scatter * c["puts"])) * (column if c["q"] == "t" else far if c["name"] == "send" else slow)
+                + (call if c["name"] == "act" else 0) for c in calls]
         late = [c["late"] * {"send": far, "dma": load}.get(c["name"], 1) for c in calls]
         before, later = [[] for _ in calls], [[] for _ in calls]
         for i, c in enumerate(calls):
@@ -129,114 +137,111 @@ def in_order(calls):
         return cost, late, before, later, hop
 
     def length(order, cost, late, before, later, hop):
-        end, held, last, bank = [0] * n, [None] * n, {}, {b: {} for b in BANKS}
+        end, last, bank, total = [0] * n, {q: 0 for q in queue}, {b: [0, 0] for b in BANKS}, 0
         for i in order:
-            q, at, by = queue[i], 0, None
+            q = queue[i]
+            at = last[q]
             for p, gap in before[i]:
                 if end[p] + gap > at:
-                    at, by = end[p] + gap, p
-            if q in last and end[last[q]] > at:
-                at, by = end[last[q]], last[q]
+                    at = end[p] + gap
             for b in banks[i]:
-                for e, p in bank[b].items():
-                    if e != q and end[p] + hop > at:
-                        at, by = end[p] + hop, p
-                bank[b][q] = i
-            end[i], held[i], last[q] = at + cost[i], by, i
-        i = max(range(n), key=lambda i: end[i] + late[i])
-        total, chain = end[i] + late[i], []
-        while held[i] is not None:
-            if held[i] not in needs[i]:
-                chain.append((held[i], i))
-            i = held[i]
-        return total, chain
+                if bank[b][q == "s"] > at:
+                    at = bank[b][q == "s"]
+            at += cost[i]
+            for b in banks[i]:
+                bank[b][q != "s"] = at + hop
+            end[i] = last[q] = at
+            if at + late[i] > total:
+                total = at + late[i]
+        return total
 
-    def mended(order):
-        def total(order):
-            found = [length(order, *case) for case in cases]
-            return sum(x[0] / case[0] for x, case in zip(found, CASES)), [pair for x in found for pair in x[1]]
-        best, chain = total(order)
-        tried, left = set(), TRIES
-        while left:
-            move = next(((u, v, k) for u, v in chain for k in STEPS if (u, v, k) not in tried), None)
-            if move is None:
-                break
-            tried.add(move)
-            u, v, k = move
-            a, b = order.index(u), order.index(v)
-            if k > 0:
-                ahead = [x for x in range(a, max(a - 150, -1), -1) if queue[order[x]] == queue[u]][:k]
-                a, moved = ahead[-1], {v}
-                for i in reversed(order[a:b]):
-                    if any(i in needs[j] for j in moved):
-                        moved.add(i)
-                first, then = moved, set(order[a:b + 1]) - moved
-            else:
-                b, moved = [x for x in range(b, min(b + 150, n)) if queue[order[x]] == queue[v]][:1 - k][-1], {u}
-                for i in order[a + 1:b + 1]:
-                    if needs[i] & moved:
-                        moved.add(i)
-                first, then = set(order[a:b + 1]) - moved, moved
-            if u in first or v in then:
-                continue
-            left -= 1
-            other = order[:a] + [i for i in order[a:b + 1] if i in first] + [i for i in order[a:b + 1] if i in then] + order[b + 1:]
-            found = total(other)
-            if found[0] < best:
-                order, (best, chain) = other, found
-        _NOTE.append(("mended", TRIES - left, [round(length(order, *case)[0] / c[0] / 1000, 2) for c, case in zip(CASES, cases)]))
-        return order
-
-    def lay_out(way, waits, frees, first, cost, hop, yields):
-        end, left, free, bank = [None] * n, [len(w) for w in waits], {}, {}
-        open_ = {i for i in range(n) if not left[i]}
-
-        def ready(i, guess):
-            c = calls[i]
-            return max([(guess[p] + cost[p] if end[p] is None else end[p]) + gap for p, gap in waits[i]]
-                       + [e + hop for b in c["banks"] for q, e in bank.get(b, {}).items() if q != c["q"]] + [first[i]])
-
-        while open_:
-            at = {i: max(ready(i, None), free.get(calls[i]["q"], 0)) for i in open_}
-            now = min(at.values())
-            q = calls[min(open_, key=lambda i: (at[i], i))]["q"]
-            soon, front = dict(at), set(open_)
-            for _ in range(3):
-                front = {j for i in front for j, gap in frees[i] if all(end[p] is not None or p in soon for p, gap in waits[j])}
-                soon.update({j: ready(j, soon) for j in front})
-            mine = sorted((i for i in soon if calls[i]["q"] == q), key=lambda i: (-way[i], i))
-            for k, i in enumerate(mine):
-                if i in at and at[i] == now and all(now + cost[i] - soon[p] <= yields * (soon[p] - now) for p in mine[:k]):
+    def packed(rank, waits, frees, first, cost, hop):
+        end, left, taken, bank = [0] * n, [len(w) for w in waits], {q: [] for q in queue}, {b: ([], []) for b in BANKS}
+        todo = sorted(((rank[i], i) for i in range(n) if not left[i]), reverse=True)
+        while todo:
+            i = todo.pop()[1]
+            q, c, at = queue[i], cost[i], first[i]
+            for p, gap in waits[i]:
+                if end[p] + gap > at:
+                    at = end[p] + gap
+            mine, others = taken[q], [x for b in banks[i] for x in bank[b][q == "s"]]
+            k = len(mine)
+            while k and mine[k - 1][1] > at:
+                k -= 1
+            while True:
+                while k < len(mine) and mine[k][0] < at + c:
+                    if mine[k][1] > at:
+                        at = mine[k][1]
+                    k += 1
+                clash = [e for s, e in others if s < at + c + hop and at < e + hop]
+                if not clash:
                     break
-            else:
-                free[q] = min(soon[p] for p in mine if soon[p] > now)
-                continue
-            end[i] = free[q] = now + cost[i]
-            for b in calls[i]["banks"]:
-                bank.setdefault(b, {})[q] = end[i]
-            open_.remove(i)
+                at = max(clash) + hop
+            mine.insert(k, (at, at + c))
+            end[i] = at + c
+            for b in banks[i]:
+                bank[b][q != "s"].append((at, at + c))
             for j, gap in frees[i]:
                 left[j] -= 1
                 if not left[j]:
-                    open_.add(j)
+                    k, x = len(todo), (rank[j], j)
+                    while k and todo[k - 1] < x:
+                        k -= 1
+                    todo.insert(k, x)
         return end
 
-    cases, best = [priced(*case) for case in CASES], None
-    for plan in PLANS:
-        cost, late, before, later, hop = priced(*plan[:6])
-        way = [0] * n
-        for i in range(n - 1, -1, -1):
-            way[i] = cost[i] + calls[i].get("soon", 0) + max([way[j] + gap for j, gap in later[i]] + [late[i]])
-        for r in range(ROUNDS):
-            if r:
-                way = lay_out(end, later, before, late, cost, hop, plan[6])
-            end = lay_out(way, before, later, [0] * n, cost, hop, plan[6])
-            order = sorted(range(n), key=lambda i: (end[i] - cost[i], i))
-            total = [length(order, *case)[0] / CASES[k][0] for k, case in enumerate(cases)]
-            _NOTE.append((plan, r, [round(x / 1000, 2) for x in total]))
-            if best is None or sum(total) < best[0]:
-                best = (sum(total), order)
-    return mended(best[1])
+    cases, plans, best, draw, zero = [priced(*case) for case in CASES], [priced(*plan) for plan in PLANS], None, SEED, [0] * n
+    steps, kept = {}, None
+    for i, c in enumerate(calls):
+        steps.setdefault(c["step"], []).append(i)
+    twins = [{(k[1:], j): i for k, v in steps.items() if k[0] == t for j, i in enumerate(v)} for t in range(3)]
+    first = [steps[t, "spread"][0] for t in range(3)]
+    steps = list(steps.values())
+    for r in range(PACKS):
+        cost, late, before, later, hop = plans[r % len(plans)]
+        if best is None:
+            way = [0] * n
+            for i in range(n - 1, -1, -1):
+                way[i] = cost[i] + max([way[j] + gap for j, gap in later[i]] + [late[i]])
+            for step in steps:
+                key, top = calls[step[0]]["step"], max(way[i] for i in step)
+                at = 16200 * (key[0] + 1) + 100 * AT[" ".join(str(x) for x in key[1:])] if key[0] in (0, 1, 2) else (way[0] - top) * (1.2 if key == "sum" else 0.5)
+                for i in step:
+                    way[i] -= top + at
+        else:
+            start, size = list(best[2]), SHAKE[r // len(plans) % len(SHAKE)]
+            draw = (draw * 1103515245 + 12345) % 2 ** 31
+            if r % 15 == 14:
+                a, b = ((0, 1), (1, 0), (1, 2), (2, 1))[(draw >> 8) % 4]
+                shift = start[first[b]] - start[first[a]]
+                for key, i in twins[a].items():
+                    if key in twins[b]:
+                        start[twins[b][key]] = best[2][i] + shift
+            elif r % 3:
+                for i in steps[(draw >> 8) % len(steps)]:
+                    start[i] += MOVE * ((draw >> 18) % 64 - 31.5) / 32
+            else:
+                lo = (draw >> 8) % int(max(start) + WINDOW) - WINDOW
+                for i in range(n):
+                    if lo < start[i] < lo + WINDOW:
+                        draw = (draw * 1103515245 + 12345) % 2 ** 31
+                        start[i] += size * ((draw >> 8) % 1024 - 512) / 512
+            way = packed([-x for x in start], later, before, late, cost, hop) if r % 3 < 2 else [c - x for c, x in zip(cost, start)]
+        end = packed([-x for x in way], before, later, zero, cost, hop)
+        if best and max(end) > max(best[2]) + 300:
+            continue
+        order = sorted(range(n), key=lambda i: (end[i] - cost[i], i))
+        total, slack = [], SLACK * (1 - r / PACKS)
+        for k, case in enumerate(cases):
+            total.append(length(order, *case) / CASES[k][0])
+            if best and sum(total) > sum(best[3][:k + 1]) + slack + 150 * (len(cases) - 1 - k):
+                break
+        else:
+            best = (sum(total), order, end, total)
+            if kept is None or best[0] < kept[0]:
+                kept = best
+                _NOTE[:] = [(r, round(sum(total) / len(total) / 1000, 2), [round(x / 1000, 2) for x in total])]
+    return kept[1]
 
 
 def rank_program(g, core, T, topo):
@@ -252,20 +257,24 @@ def rank_program(g, core, T, topo):
 
     def write(dst, out, src, sem, mask):
         rid, pid, _eng = topo.addr(dst)
-        g.remote_dma(out, src, T.sem[sem], T.sem.ls, pid, rid, mask)
+        if isinstance(src, list):
+            g.remote_dma_fused([RemoteDMATransfer(dst_ids=[DstId(rid=rid, pnc=pid)], dsts=[out], srcs=src, alu_op=2, remote_sem=T.sem[sem],
+                                                  dma_engine_mask=mask)], local_sem=T.sem.ls)
+        else:
+            g.remote_dma(out, src, T.sem[sem], T.sem.ls, pid, rid, mask)
 
     if T.rank_of(core) is None:
         for c in topo.cores_of(core):
             if T.rank_of(c) is not None and helper(c) == core:
                 n = 0
-                for t, name, c0, c1, sem in HANDED:
+                for sem, (t, name, c0, c1) in HANDED.items():
                     dst = target(c, t)
                     g.wait_ge(T.sem[sem], len(topo.engines(c, dst)))
                     write(dst, T[name][:, c0:c1], T[name][:, c0:c1], sem, topo.mask(core, dst))
                     n += len(topo.engines(core, dst))
                 g.wait_ge(T.sem.ls, n)
         return
-    calls, known, lines = [], {}, {}
+    calls, known, lines, step = [], {}, {}, [None]
 
     def do(q, reads, writes, cost, name, kw, late=0):
         after = set()
@@ -281,20 +290,30 @@ def rank_program(g, core, T, topo):
             for other in [o for o in known[k[0]] if o[:len(k)] == k]:
                 del known[k[0]][other]
             known[k[0]][k] = ([len(calls)], [])
-        calls.append({"q": q, "name": name, "kw": kw, "cost": cost, "late": late, "after": after, "behind": [],
+        calls.append({"q": q, "name": name, "kw": kw, "cost": cost, "late": late, "after": after, "behind": [], "picks": 0, "puts": 0,
+                      "step": step[0] or writes[0][0],
                       "banks": {k[0] for k in reads + writes if k[0] in BANKS}})
 
     def in_line(name):
         calls[-1]["behind"] = lines.get(name, [])
         lines[name] = [len(calls) - 1]
 
+    def indirect(kind, n):
+        calls[-1].update({kind: n, "cost": 50 if calls[-1]["q"] == "v" else CALL})
+
     def dma(q, out, in_, reads, writes, late):
         do(q, reads, writes, 50, "dma", (out, in_), late)
         if q == "y":
             in_line(q)
 
-    def send(dst, out, src, reads, writes, sem, late=FAR, also=None):
-        do("g", reads, writes, ISSUE, "send", (dst, out, src, sem, also), late)
+    def send(dst, out, src, reads, writes, sem, size=1):
+        size *= FOLD if isinstance(src, list) else 1
+        if sem in HANDED:
+            do("g", reads, writes, ISSUE, "send", (dst, out, src, sem), 1.7 * FAR + 1.6 * size * MOVING + HOME * (sem[2] == "3"))
+            in_line("handed")
+        else:
+            do("g", reads, writes, ISSUE + size * MOVING + FIRST * (sem == "ax1"), "send", (dst, out, src, sem), FAR + HOME * (sem[2] == "3") + LOWER * (sem[1] == "z"))
+
 
     def cycles(n):
         return max(64, n) * CYCLE
@@ -333,16 +352,29 @@ def rank_program(g, core, T, topo):
         do("g", r, w, SLOWG * (170 + 2 * n * CYCLE), "pick", dict(out=out, in_=in_, pattern=pattern, compare_op=op, fill=other, base=base,
                                                        channel_multiplier=cm))
 
-    def gathered(n):
-        return 60 + GATHER * n
-
     def half(h):
         return slice(128 * h, 128 * h + 128)
 
     def ps(b, c0, c1, p=slice(None)):
+        if b == "B0":
+            return T[b][p, c0:c1]
         if c0 % 32 == 0 and c1 % 32 == 0:
             return T[b][p, c0 // 32:c1 // 32, :]
         return T[b][p, c0 // 32, c0 % 32:c0 % 32 + c1 - c0]
+
+    shared = {"FX": ("XF", 256, 0), "FB": ("XF", 256, 128),
+              "UN0": ("OUT0", 512, 384), "UN1": ("OUT1", 512, 384), "MA0": ("MA", 128, 0), "MA1": ("MA", 128, 256)}
+
+    def part(name, h, c0=0, c1=128):
+        if name == "FH":
+            return T.FH[:, 4 * h:4 * h + 4, :], (name, h)
+        buf, n, o = shared.get(name, (name, 128, 0))
+        return T[buf][:, n * h + o + c0:n * h + o + c1], (name if name[:2] in ("UN", "MA") else buf, h)
+
+    def sums(b, h, terms, start=True):
+        for i, (o, l, src) in enumerate(terms):
+            ap, key = part(src, h)
+            mm(ps(b, o, o + 128), T[l][:, 0:128], ap, start and i == 0, i == len(terms) - 1, [l, key], b, 128)
 
     dma("y", T.X0[:], T.xw[:], [], ["X0"], 1500)
     dma("s", T.WI[:], T.wts[:], [], ["WI"], 1400)
@@ -357,7 +389,7 @@ def rank_program(g, core, T, topo):
     fill(T.ONES[:], 1.0, ["ONES"], 128)
     ts(T.PI[:, 1:2], T.PI[:, 0:1], 4, OP.arith_shift_right, [("PI", 0)], [("PI", 1)])
     ts(T.PI[:, 2:3], T.PI[:, 0:1], 15, OP.bitwise_and, [("PI", 0)], [("PI", 2)])
-    for a, b, c in ((0, 256, -65536.0), (256, 512, 5120.0), (512, 640, -48.0)):
+    for a, b, c in ((0, 256, -65536.0), (256, 384, 5120.0), (512, 640, -16.0), (640, 768, 16.0), (768, 1024, -12.0), (1024, 1152, -0.5)):
         fill(T.CT[:, a:b], c, [("CT", a)], (b - a) // 2)
     cp(T.PF[:, 0:2], T.PI[:, 1:3], ["PI"], [("PF", 0)])
     pG, pL, P0 = T.PF[:, 0:1], T.PF[:, 1:2], ("PF", 0)
@@ -371,11 +403,21 @@ def rank_program(g, core, T, topo):
     ts(T.W2[:], T.MNE[:], T.WF[:, 1:2], OP.mult, ["MNE", "WF"], ["W2"])
     ts(T.W132[:], T.MNE[:], T.WF[:, 0:1], OP.mult, ["MNE", "WF"], ["W132"], 32.0, OP.mult)
     ts(T.W232[:], T.MNE[:], T.WF[:, 1:2], OP.mult, ["MNE", "WF"], ["W232"], 32.0, OP.mult)
-    for nm, src, c in (("BO64", "BO", 64.0), ("IDN4096", "ID", -4096.0), ("ID128", "ID", 128.0), ("IDN", "ID", -1.0), ("IDN64", "ID", -1.0 / 64),
-                       ("BO8192", "BO", 8192.0), ("BON", "BO", -1.0), ("BO12288", "BO", 12288.0)):
-        ts(T[nm][:], T[src][:], c, OP.mult, [src], [nm])
-    for nm, c in (("B15", 1.5), ("BNA", -2.0 / 4096), ("BPA", 1.0 / 4096)):
+    pick(T.SL[:], T.BO[:], col, OP.is_gt, 0.0, ["BO"], ["SL"], 128)
+    pick(T.SL[:], T.SL[:], col, OP.not_equal, -1.0, ["SL"], ["SL"], 128)
+    for i, (nm, src, c) in enumerate((("BON64", "BO", -64.0), ("IDN", "ID", -1.0), ("BO8192", "BO", 8192.0),
+                                      ("BON128", "BO", -128.0), ("BON512", "BO", -512.0), ("BO512", "BO", 512.0), ("BO64", "BO", 64.0),
+                                      ("LTH", "SL", -4096.0), ("LTX", "SL", -64.0), ("LTF", "SL", -65.0), ("IDN4096", "ID", -4096.0))):
+        if i < SCALED:
+            act(T[nm][:], T[src][:], [src], [nm], 128, scale=c)
+        else:
+            ts(T[nm][:], T[src][:], c, OP.mult, [src], [nm])
+    for nm, c in (("B30", -3.0), ("BNA", 2.0 / 4096), ("BPA", -1.0 / 4096)):
         ts(T[nm][:], T.BO[:, ::16], c, OP.mult, ["BO"], [nm])
+    fill(T.ZR[:], 0.0, ["ZR"])
+    for t in range(3):
+        fill(T["BT%d" % t][:], 0.0, ["BT%d" % t])
+        cp(T["BT%d" % t][:, t::16], T.BO64[:, ::16], ["BO64"], ["BT%d" % t])
     for e in range(8):
         if e < ZERO:
             fill(T.SK[:, 256 * e:256 * e + 256], 0.0, [("SK", "zero", e)], 128)
@@ -384,20 +426,8 @@ def rank_program(g, core, T, topo):
     for e in range(8):
         pick(T.SK[:, 16 * e:16 * e + 129 * 15 + 1:129], T.BOX[:, 16 * e:16 * e + 16], [[0, 16]], OP.is_ge, 0.0, ["BOX", ("SK", "zero")],
              [("SK", e)], 16, 127)
-    pick(T.SL[:], T.BO[:], col, OP.is_gt, 0.0, ["BO"], ["SL"], 128)
-
-    def lowest(t):
-        nm = "LT%d" % t
-        pick(T[nm][:], T.SL[:], col, OP.not_equal, -1.0, ["SL"], [nm], 128)
-        if t == 2:
-            in_line("sent")
-        for src, op, other, base in (("BO64", OP.is_gt, 1.0, t), (None, OP.is_ge, 0.0, 15), (None, OP.not_equal, -16.0, t)):
-            pick(T[nm][:, t::16], T[src][:, ::16] if src else T[nm][:, t::16], [[16, 8]], op, other, [nm, "BO64"], [nm], 8, base)
-    lowest(0)
-    lowest(1)
     iota(T.T3[:], [[1, 4]], 0, 0, ["T3"], 4)
-    ts(T.THR[:], T.T3[:], pL, OP.not_equal, ["T3", P0], ["THR"], -0.5, OP.mult)
-    ts(T.PF[:, 10:11], T.THI[:], -2048.0, OP.add, ["THI"], [("PF", 10)], 1.0 / 4096, OP.mult)
+    ts(T.PF[:, 10:11], T.THI[:], -2041.0, OP.add, ["THI"], [("PF", 10)], -1.0 / 4096, OP.mult)
     ts(T.THB[:], T.BO[:, ::16], T.PF[:, 10:11], OP.mult, ["BO", ("PF", 10)], ["THB"])
     iota(T.PC[:], [[-1, 2], [100, 2]], 0, 0, ["PC"], 4)
     iota(T.MP[:], [[2, 4], [100, 2], [0, 16]], 0, 0, ["MP"], 128)
@@ -405,115 +435,128 @@ def rank_program(g, core, T, topo):
     for i in range(4):
         ts(T["PM%d" % i][:], T.MP[:], T.PF[:, 2 + i:3 + i], OP.is_equal, ["MP", ("PF", 2)], ["PM%d" % i], n=128)
         ts(T["PN%d" % i][:], T["PM%d" % i][:], 64.0, OP.mult, ["PM%d" % i], ["PN%d" % i])
-        calls[-1]["soon"] = EARLY[0]
-    ts(T.LE[:], T.T3[:], pL, OP.is_equal, ["T3", P0], ["LE"])
-    ts(T.LL[:], T.T3[:], pL, OP.is_gt, ["T3", P0], ["LL"])
-    iota(T.QQ[:, 0:64], [[-1, 64]], 31, 0, [("QQ", 0)], 64)
-    act(T.PF[:, 8:9], pL, [P0], [("PF", 8)], 1, func=AF.Identity, scale=-4.0, bias=-1.5)
-    act(T.PF[:, 9:10], T.LL[:, 2:3], ["LL", P0], [("PF", 9)], 1, func=AF.Identity, scale=-32.0, bias=pL)
-    for i, (e, a, b) in enumerate(((1, -2.0, T.LL[:, 3:4]), (1, -1.0, 0.0), (2, -0.25, 0.0), (2, -1.25, 1.0))):
-        act(T.QS[:, i:i + 1], T.LE[:, e:e + 1], ["LE", "LL"], [("QS", i)], 1, func=AF.Identity, scale=a, bias=b)
-    for i in range(2):
-        act(T.QQ[:, 64 * i + 64:64 * i + 128], T.QQ[:, 0:64], [("QQ", 0), "QS"], [("QQ", i + 1)], 64, func=AF.Identity,
-            scale=T.QS[:, 2 * i:2 * i + 1], bias=T.QS[:, 2 * i + 1:2 * i + 2])
-    tt(T.QQ[:, 0:64], T.QQ[:, 64:128], T.QQ[:, 128:192], OP.mult, ["QQ"], [("QQ", 0)], 128)
-    cp(T.QB[:], T.BO[:, ::16], ["BO"], ["QB"])
-    for e in range(8):
-        act(T.QX[:, 64 * e:64 * e + 64], T.QQ[:, 0:64], [("QQ", 0), "QB"], [("QX", e)], 64, func=AF.Identity, scale=T.QB[:, e:e + 1])
+    for i, c in enumerate((1.0, 64.0, -64.0)):
+        ts(T.LE[:, 4 * i:4 * i + 4], T.T3[:], pL, OP.is_equal, ["T3", P0], [("LE", i)], c, OP.mult)
+    act(T.PF[:, 8:9], pL, [P0], [("PF", 8)], 1, func=AF.Identity, scale=4.0, bias=-60.5)
     iota(T.IO64[:], [[1, 64]], 0, 0, ["IO64"], 64)
     for e in range(2):
-        pick(T.RX[:, 256 * e:256 * e + 256], T.ONES[:], [[1, 2], [0, 8], [4, 16]], OP.is_equal, 0.0, ["ONES"], [("RX", e)], 256, 2 * e)
-    ts(T.RX[:, 128:384], T.RX[:, 128:384], 0.5, OP.mult, ["RX"], ["RX"], n=128)
-    iota(T.JI[:], [[1, 16], [-100, 2]], 0, 0, ["JI"], 32)
-    ts(T.RC[:], T.JI[:], pL, OP.is_equal, ["JI", P0], ["RC"], -2.0, OP.mult)
-    ts(T.RA[:], T.JI[:], pL, OP.is_gt, ["JI", P0], ["RA"], 2.0 ** -16 - 1, OP.mult)
-    ts(T.RB[:], T.JI[:], pL, OP.is_gt, ["JI", P0], ["RB"], 2.0 ** 16 - 1, OP.mult)
-    ts(T.RC[:], T.RC[:], 1.0, OP.add, ["RC"], ["RC"])
-    tt(T.RA[:], T.RA[:], T.RC[:], OP.add, ["RA", "RC"], ["RA"])
-    tt(T.RB[:], T.RB[:], T.RC[:], OP.add, ["RB", "RC"], ["RB"])
-    fill(T.RR[:, 0:1], 0.0, [("RR", 0)])
-    tt(T.RR[:, 1:32], T.RA[:, 0:31], T.RB[:, 1:32], OP.mult, ["RA", "RB"], [("RR", 1)])
-    calls[-1]["soon"] = EARLY[1]
-    for n in (32, 64, 128):
-        pick(T.RR[:, n:2 * n], T.RR[:, 0:n], [[0, n]], OP.is_ge, 0.0, ["RR"], [("RR", n)], n, 127)
+        rx = T.RX[:, 256 * e:256 * e + 256]
+        pick(rx, T.ONES[:], [[1, 2], [0, 8], [4, 16]], OP.is_equal, 0.0, ["ONES"], [("RX", e)], 256, 2 * e)
+        pick(rx, rx, [[1, 2], [0, 8], [4, 16]], OP.not_equal, -1.0, [("RX", e)], [("RX", e)], 256, 2 * e + 4)
+    pick(T.RX[:, 15::16], T.RX[:, 15::16], [[1, 4], [0, 8]], OP.not_equal, 1.0, ["RX"], ["RX"], 32)
+    JI, RA, RB, RC = (T.RW[:, 16 * i:16 * i + 16] for i in range(4))
+    iota(JI, [[1, 16]], 0, 0, ["JI"], 16)
+    ts(RC, JI, pL, OP.is_equal, ["JI", P0], ["RC"], -2.0, OP.mult)
+    ts(RA, JI, pL, OP.is_gt, ["JI", P0], ["RA"], 2.0 ** -30, OP.mult)
+    ts(RB, JI, pL, OP.is_gt, ["JI", P0], ["RB"], 2.0 ** 30, OP.mult)
+    ts(JI, JI, pL, OP.is_le, ["JI", P0], ["JI"])
+    tt(RC, RC, JI, OP.add, ["RC", "JI"], ["RC"])
+    tt(RA, RA, RC, OP.add, ["RA", "RC"], ["RA"])
+    tt(RB, RB, RC, OP.add, ["RB", "RC"], ["RB"])
+    fill(T.RR[:, 34:50], 1.0, [("RR", 34)])
+    fill(T.RR[:, 0:18:17], 0.0, [("RR", 0)])
+    for a in (0, 17):
+        tt(T.RR[:, a + 1:a + 16], T.RW[:, 16:31], T.RW[:, 33:48], OP.mult, ["RA", "RB"], [("RR", a + 1)])
+        cp(T.RR[:, a + 16:a + 17], T.RW[:, 31:32], ["RA"], [("RR", a + 16)])
     for h in range(2):
         ts(T.PF[:, 11 + h:12 + h], pL, float(W + 16 * h), OP.add, [P0], [("PF", 11 + h)])
-        fill(T.EQ[:, 256 * h + 1:256 * h + 128:2], 0.0, [("EQ", h, "zero")])
 
     def scatter(lex, src):
         for c in range(7, -1, -1):
-            cp(T[lex][:].indirect(T.OFU[:, 2 * c:2 * c + 2]), T[src][:, 32 * c:32 * c + 32], [("OFU", c // 4), (src, c // 4)], [lex],
-               60 + 32 * SCATTER)
+            step[0] = (t, "letters" if lex == "LX" else "rest", c // 4)
+            ap, key = part(src, c // 4, 32 * (c % 4), 32 * (c % 4) + 32)
+            cp(T[lex][:].indirect(T.OFU[:, 2 * c:2 * c + 2]), ap, [("OFU", c // 4), key], [lex])
+            indirect("puts", 32)
 
-    XP, SCORE, COLS, ENDS, HASH = ("B7", "B1"), ("B2", "B0"), ("B2", "B5"), ("B7", "B1"), ("B5", "B0")
+    XP, SCORE, COLS, ENDS, HASH, HOT = LAID
 
-    def hashed(parts, h, idle=False):
+    def hashed(X, h, idle=False):
         s, b, q = half(h), HASH[h], T.Q[:, 256 * h:256 * h + 256]
         for o, ws in ((0, ("W132", "W232")), (256, ("W1", "W2"))):
-            mm(ps(b, o, o + 256), T.ONES[:, 0:128], T.CT[:, o:o + 256], True, False, ["ONES", "CT"], b, 256)
-            for X in parts:
-                for j, w in enumerate(ws):
-                    mm(ps(b, o + 128 * j, o + 128 * j + 128), T[w][:], T[X][:, s], False, (X, j) == (parts[-1], 1) and (idle or o == 0),
-                       [w, (X, h)], b, 128)
+            n = 128 if o and not idle else 256
+            mm(ps(b, o, o + n), T.ONES[:, 0:128], T.CT[:, o:o + n], True, False, ["ONES", ("CT", o)], b, n)
+            for j, w in enumerate(ws):
+                mm(ps(b, o + 128 * j, o + 128 * j + 128), T[w][:], part(X, h)[0], False, j == 1 and (idle or o == 0), [w, (X, h)], b, 128)
         if idle:
-            cp(T.ZI[:], ps(b, 256, 512), [b], ["ZI"], 256)
-            ts(T.ZI[:], T.ZI[:], 4095, OP.bitwise_and, ["ZI"], ["ZI"], n=256)
-            tt(T.PR[:, s], T.ZI[:, 0:128], T.ZI[:, 128:256], OP.mult, ["ZI"], [("PR", h)], 256)
-        else:
-            act(q, ps(b, 0, 256), [b], [("Q", h)], 256, func=AF.Identity, scale=2.0 ** -17, bias=223.5 + 1.0 / 8192)
-            mm(ps(b, 256, 512), T.IDN4096[:], q, False, True, ["IDN4096", ("Q", h)], b, 256)
-            act(T.UP[:, s], ps(b, 384, 512), [b], [("UP", h)], 128)
-            tt(T.PR[:, s], T.UP[:, s], ps(b, 256, 384), OP.mult, [("UP", h), b], [("PR", h)], 128)
+            z = T.PR if h else T.ZI
+            cp(z[:], ps(b, 256, 512), [b], [z.name], 256)
+            ts(z[:], z[:], 4095, OP.bitwise_and, [z.name], [z.name], n=256)
+            tt(T.UP[:, s], z[:, 0:128], z[:, 128:256], OP.mult, [z.name], [("UP", h)], 256)
+            tt(T.HI[:, s], T.UP[:, s], ps(b, 0, 128), OP.add, [("UP", h), b], [("HI", h)], 128)
+            ts(T.HI[:, s], T.HI[:, s], 5, OP.arith_shift_right, [("HI", h)], [("HI", h)], 4095, OP.bitwise_and, 128)
+            return
+        act(q, ps(b, 0, 256), [b], [("Q", h)], 256, func=AF.Identity, scale=2.0 ** -17, bias=223.5 + 1.0 / 8192)
+        mm(ps(b, 256, 512), T.IDN4096[:], q, False, True, ["IDN4096", ("Q", h)], b, 256)
+        act(T.UP[:, s], ps(b, 384, 512), [b], [("UP", h)], 128, func=AF.Identity, bias=160.0 * 4096)
+        tt(T.PR[:, s], T.UP[:, s], ps(b, 256, 384), OP.mult, [("UP", h), b], [("PR", h)], 128)
         tt(T.ZI[:, s], T.PR[:, s], ps(b, 0, 128), OP.add, [("PR", h), b], [("ZI", h)], 128)
         ts(T.HI[:, s], T.ZI[:, s], 5, OP.arith_shift_right, [("ZI", h)], [("HI", h)], 4095, OP.bitwise_and, 128)
-        calls[-1]["soon"] = SOON[h]
 
     for h in (1, 0):
-        hashed(["X0"], h, h == IDLE)
+        hashed("X0", h, h in IDLE)
         cp(T.H0[:, half(h)], T.HI[:, half(h)], [("HI", h)], [("H0", h)], 128)
 
     for t in range(3):
-        xn, mn = "XN%d" % t, "MN%d" % t
-        X, M, X1, M1 = "X%d" % t, "M%d" % t, "X%d" % (t + 1), "M%d" % (t + 1)
-        H, H1, hn = "H%d" % t, "H%d" % (t + 1), "HN%d" % t
-        TX, TM = T[X], T[M]
-        dst = target(core, t)
-        lt, top = "LT%d" % t, slice(0, 64)
-
-        cut = 256 - SHARE[t]
-        for w0, w1 in ((224, 256), (192, 224), (128, 192), (0, 64), (64, 96), (96, 128)):
-            args = (T.CB[:, 16 * w0:16 * w1], T.LX[:, 0:W].indirect(T[H][:, w0:w1]), ["LX", (H, w0 // 128)], [("CB", w0 // 64, w0)])
-            if w0 >= cut:
-                cp(*args, gathered(16 * (w1 - w0)))
-            else:
-                act(*args, GATHER * 16 * (w1 - w0))
-                in_line("gather")
+        mn, ma, un, out = "MN%d" % t, "MA%d" % t, "UN%d" % t, "OUT%d" % t
+        X, P, H, M, M1 = "X%d" % t, "P%d" % t, "H%d" % t, "M%d" % t, "M%d" % (t + 1)
+        TM = T[M]
         for h in (1, 0):
-            ts(T.H16[:, half(h)], T[H][:, half(h)], -2048.0, OP.add, [(H, h)], [("H16", h)])
-            mm(ps(XP[h], 128 * h, 128 * h + 128), T.ID[:], TX[:, half(h)], True, True, ["ID", (X, h)], XP[h], 128)
-            mm(ps(XP[h], 256, 384), T.ID[:], T.H16[:, half(h)], True, True, ["ID", ("H16", h)], XP[h], 128)
+            step[0] = (t, "offsets", h)
+            if t and h in HALF:
+                ts(T[H][:, half(h)], T[P][:, half(h)], 2048.0, OP.add, [(P, h)], [(H, h)])
+            else:
+                ts(T[P][:, half(h)], T[H][:, half(h)], -2048.0, OP.add, [(H, h)], [(P, h)])
+        dst = target(core, t)
+        top = slice(0, 64)
+        step[0] = (t, "gather")
+
+        for w0, w1, on_vector in PIECES[t]:
+            args = (T.CB[:, 16 * w0:16 * w1], T.LX[:, 0:W].indirect(T[H][:, w0:w1]), ["LX", (H, w0 // 128)],
+                    [("CB", w) for w in range(w0 // 8, w1 // 8)])
+            if on_vector:
+                cp(*args)
+            else:
+                act(*args, 0)
+                in_line("gather")
+            indirect("picks", 16 * (w1 - w0))
+        for h in (1, 0):
+            mm(ps(XP[h], 128, 192), T.ID[:], part(X, h, 0, 64)[0], True, True, ["ID", part(X, h)[1]], XP[h], 64)
             for j in range(2):
-                mm(T[XP[h]][:, 4 - 4 * h:8 - 4 * h, j::2], T.ID[:], TX[:, 128 * h + 64:128 * h + 128], True, True, ["ID", (X, h)], XP[h], 64)
+                mm(T[XP[h]][:, 0:4, j::2], T.ID[:], part(X, h, 64, 128)[0], True, True, ["ID", part(X, h)[1]], XP[h], 64)
 
         def lane(h):
-            b, s = SCORE[h], half(h)
+            b, s, z = SCORE[h], half(h), XP[h]
             for w0, n in ((224, 32), (192, 32), (128, 64)) if h else ((0, 64), (64, 32), (96, 32)):
-                m = 64 // n
-                x0 = w0 if m == 1 else 2 * w0 - 384 * h
+                m, w = 64 // n, w0 // 64 * 64
+                x0 = 128 if m == 1 else 2 * (w0 - w)
                 for k in range(16 // m):
-                    o, part = 16 * w0 + 64 * k, ("CB", w0 // 64) + ((w0,) if m > 1 else ())
-                    tt(T.EB[:, o:o + 64], T.CB[:, 16 * w0 + k:16 * (w0 + n):16 // m], ps(XP[h], x0, x0 + 64), OP.not_equal, [part, XP[h]],
-                       [("EB", o)])
-                    for j in range(m):
-                        mm(ps(b, w0 % 128, w0 % 128 + n), T.SK[:, 128 * (k + 8 * j):128 * (k + 8 * j + 1)], T.EB[:, o + j:o + 64:m],
-                           k + 8 * j == 0, k + 8 * j == 15, ["SK", ("EB", o)], b, n)
+                    o, words = 16 * w + 64 * m * k, [("CB", x) for x in range(w0 // 8, (w0 + n) // 8)]
+                    e = o + 2 * (w0 - w)
+                    tt(T.EB[:, e:e + 64], T.CB[:, 16 * w0 + k:16 * (w0 + n):16 // m], ps(z, x0, x0 + 64), OP.not_equal, words + [z],
+                       [("EB", o, e)])
+                    for j in range(m if w0 not in (224, 64) else 0):
+                        mm(ps(b, w % 128, w % 128 + 64), T.SK[:, 128 * (k + 8 * j):128 * (k + 8 * j + 1)], T.EB[:, o + j:o + 64 * m:m],
+                           k + 8 * j == 0, k + 8 * j == 15, ["SK", ("EB", o)], b, 64)
+            step[0] = (t, "f", h)
             ts(T.PB[:, s], ps(b, 0, 128), -11.5, OP.is_le, [b], [("PB", h)], n=128)
-            mm(ps(b, 128, 256), T[lt][:], T.PB[:, s], True, True, [lt, ("PB", h)], b, 128)
-            mm(ps(b, 256, 384), T.BO[:], T.PB[:, s], True, True, ["BO", ("PB", h)], b, 128)
-            ts(T.FB[:, s], ps(b, 128, 256), T.THR[:, t:t + 1], OP.is_le, [b, "THR"], [("FB", h)], n=128)
-            act(T.NH[:, s], ps(b, 256, 384), [b], [("NH", h)], 128, func=AF.Relu, scale=-128.0, bias=64.0)
-            tt(T.FH[:, 4 * h:4 * h + 4, :], T.FB[:, s], ps(XP[h], 256, 384), OP.mult, [("FB", h), XP[h]], [("FH", h)], 128)
-            tt(T.FX[:, s], T.FB[:, s], ps(XP[h], 128 * h, 128 * h + 128), OP.mult, [("FB", h), XP[h]], [("FX", h)], 128)
+            sums(z, h, ((384, "ID", P), (384, "LTH", "PB")))
+            ts(T.FH[:, 4 * h:4 * h + 4, :], ps(z, 384, 512), -4096.0, OP.add, [z], [("FH", h)], -2048.0, OP.max, 128)
+            step[0] = (t, "xf", h)
+            sums(b, h, ((256, "ID", X), (256, "LTX", "PB"), (384, "LTF", "PB")))
+            act(T.XF[:, 256 * h:256 * h + 256], ps(b, 256, 512), [b], [("XF", h)], 256, func=AF.Relu, bias=-64.0)
+            calls[-1]["behind"] = lines["gather"]
+            step[0], c = (t, "np", h), NONE[h]
+            mm(ps(c, 128, 256), T.ID[:], T.CB[:, 2048 * h + t:2048 * h + 2048:16], True, False,
+               ["ID"] + [("CB", x) for x in range(16 * h, 16 * h + 16)], c, 128)
+            mm(ps(c, 128, 256), T.IDN[:], part(X, h)[0], False, False, ["IDN", part(X, h)[1]], c, 128)
+            mm(ps(c, 128, 256), T.BON128[:], T.PB[:, s], False, True, ["BON128", ("PB", h)], c, 128)
+            act(T.NP[:, s], ps(c, 128, 256), [c, "LE"], [("NP", h)], 128, func=AF.Relu, scale=T.LE[:, t:t + 1], bias=T.LE[:, 4 + t:5 + t])
+            calls[-1]["behind"] = lines["gather"]
+
+        def letters(h):
+            b = LETTERS[h]
+            sums(b, h, ((256, "ID", X), (256, "BT%d" % t, "FB"), (256, "ID", "NP")))
+            act(T.XA[:, half(h)], ps(b, 256, 384), [b, "LE"], [("XA", h)], 128, func=AF.Identity, bias=T.LE[:, 8 + t:9 + t])
 
         def place_f(h):
             c4 = slice(4 * h, 4 * h + 4)
@@ -522,163 +565,204 @@ def rank_program(g, core, T, topo):
                 mm(T.B3[:, c4, 16 * s:16 * s + 16], T["PM%d" % i][:], T.FH[:, c4, 16 * c:16 * c + 16], c == 0, c == 1,
                    ["PM%d" % i, ("FH", h)], "B3", 64)
             tr(T.KB[:, c4, :], T.B3[:, c4, :], ["B3"], [("KB", h)])
-            ts(T.LF[:, 8 * h:8 * h + 8], T.KB[:, c4, ::16], 2048.0, OP.add, [("KB", h)], [("LF", h)])
+            ts(T.LF[:, 8 * h:8 * h + 8], T.KB[:, c4, ::16], 32768.0, OP.add, [("KB", h)], [("LF", h)])
 
         def lookup_f(h):
-            s, places = half(h), T.LF[:, 8 * h:8 * h + 8]
-            tt(T.SUB[:, s], T.LM[:, 0:W].indirect(places), TM[:, s], OP.subtract, ["LM", M, ("LF", h)], [("SUB", h)], gathered(128))
-            tt(T.FC[:, s], T.LX[:, 0:W].indirect(places), T.FB[:, s], OP.mult, ["LX", ("LF", h), ("FB", h)], [("FC", h)], gathered(128))
-            ts(T.RL[:, s], T.SUB[:, s], 0.0, OP.max, [("SUB", h)], [("RL", h)])
-            for o, src, w in ((8, "FB", "THB"), (8, "FB", "B15"), (8, "NH", "B15"), (8, "SUB", "BPA"), (0, "FC", "BO"), (8, "RL", "BNA")):
-                mm(ps(COLS[h], o, o + 8), T[src][:, s], T[w][:, ::16] if w == "BO" else T[w][:], w == "THB", w == "BNA", [(src, h), w],
-                   COLS[h], 8)
+            s, places, b = half(h), T.LF[:, 8 * h:8 * h + 8], COLS[h]
+            if "g%d" % h not in ONV:
+                for name, lex in (("GG", "LM"), ("CC", "LX")):
+                    act(T[name][:, s], T[lex][:, 0:W].indirect(places), [lex, ("LF", h)], [(name, h)], 0)
+                    indirect("picks", 128)
+                sums(b, h, ((256, "LTX", "PB"), (128, "IDN", M), (256, "ID", "CC"), (128, "ID", "GG")))
+                act(T.RL[:, s], ps(b, 128, 256), [b], [("RL", h)], 128, func=AF.Abs)
+                act(T.FC[:, s], ps(b, 256, 384), [b], [("FC", h)], 128, func=AF.Relu, bias=-64.0)
+                act(T.D16[:, s], ps(b, 128, 256), [b], [("D16", h)], 128, func=AF.Identity, scale=0.5, bias=1535.75)
+                for o, src, w in ((8, "FB", "THB"), (8, "FB", "BC"), (8, "NP", "B30"), (0, "FC", "BO"), (8, "RL", "BA")):
+                    ap, key = part(src, h)
+                    mm(ps(b, o, o + 8), ap, T[w][:, ::16] if w == "BO" else T[w][:], w == "THB", w == "BA", [key, w], b, 8)
+                return
+            tt(T.SUB[:, s], T.LM[:, 0:W].indirect(places), TM[:, s], OP.subtract, ["LM", M, ("LF", h)], [("SUB", h)])
+            indirect("picks", 128)
+            tt(T.FC[:, s], T.LX[:, 0:W].indirect(places), part("FB", h)[0], OP.mult, ["LX", ("LF", h), ("XF", h)], [("FC", h)])
+            indirect("picks", 128)
+            ts(T.RL[:, s], T.SUB[:, s], 0.0, OP.max, [("SUB", h)], [("RL", h)], -63.75, OP.add)
+            for o, src, w in ((8, "FB", "THB"), (8, "NP", "B30"), (8, "SUB", "BPA"), (0, "FC", "BO"), (8, "RL", "BNA")):
+                ap, key = part(src, h)
+                mm(ps(COLS[h], o, o + 8), ap, T[w][:, ::16] if w == "BO" else T[w][:], w == "THB", w == "BNA", [key, w], COLS[h], 8)
 
         def hot_x(h):
-            o, b = ps("B4", 128 * h, 128 * h + 128), ("B1", "B6")[h]
-            mm(o, T.BO[:], T.FX[:, half(h)], True, True, ["BO", ("FX", h)], "B4", 128)
-            act(T.FQ[:, half(h)], o, ["B4", ("PF", 9), "LL"], [("FQ", h)], 128, func=AF.Square, scale=T.LL[:, 2:3], bias=T.PF[:, 9:10])
-            mm(ps(b, 0, 512), T.FQ[:, half(h)], T.QX[:], True, True, [("FQ", h), "QX"], b, 512)
-            for c0, c1 in ((0, 512),) if h or "one" in ONV else ((0, 256), (256, 512)):
-                act(T.OHX[:, 512 * h + c0:512 * h + c1], ps(b, c0, c1), [b], [("OHX", h, e) for e in range(c0 // 256, c1 // 256)], c1 - c0,
-                    func=AF.Relu, bias=1.0)
+            b = HOT[h]
+            mm(ps(b, 0, 8), part("FX", h)[0], T.BO[:, ::16], True, True, ["BO", ("XF", h)], b, 8)
+            for e in range(8):
+                ts(T.OHX[:, 512 * h + 64 * e:512 * h + 64 * e + 64], T.IO64[:], ps(b, e, e + 1), OP.is_equal, ["IO64", b], [("OHX", h, e)])
 
         def coded(h):
-            for pm, src in (("PN", "FX"), ("PM", "FC")):
+            for pm, src, o in (("PN", "XF", 256 * h), ("PM", "FC", 128 * h)):
                 for i in range(4):
-                    s, w0 = i // 2, 128 * h + 64 * (i % 2)
-                    mm(T.B3[:, 8 + 4 * h:12 + 4 * h, 16 * s:16 * s + 16], T[pm + str(i)][:], T[src][:, w0:w0 + 64], src == "FX" and i == 0,
+                    s, w0 = i // 2, o + 64 * (i % 2)
+                    mm(T.B3[:, 8 + 4 * h:12 + 4 * h, 16 * s:16 * s + 16], T[pm + str(i)][:], T[src][:, w0:w0 + 64], src == "XF" and i == 0,
                        src == "FC" and i == 3, [pm + str(i), (src, h)], "B3", 64)
             tr(T.KC[:, 4 * h:4 * h + 4, :], T.B3[:, 8 + 4 * h:12 + 4 * h, :], ["B3"], [("KC", h)])
 
         def table(h):
             for e in range(8):
                 s, b = slice(512 * h + 64 * e, 512 * h + 64 * e + 64), COLS[h]
-                ts(T.OHC[:, s], T.IO64[:], ps(b, e, e + 1), OP.is_equal, ["IO64", b], [("OHC", h, e)], ps(b, 8 + e, 9 + e), OP.is_ge)
-                rd = [("OHX", h, e // 4), ("OHC", h, e)]
+                ts(T.OHC[:, s], T.IO64[:], ps(b, e, e + 1), OP.not_equal, ["IO64", b], [("OHC", h, e)], ps(b, 8 + e, 9 + e), OP.is_lt)
+                rd = [("OHX", h, e), ("OHC", h, e)]
                 mm(ps("B6", 0, 64, top), T.OHX[:, s], T.OHC[:, s], (h, e) == (1, 0), False, rd, "B6", 64)
                 mm(ps("B6", 0, 64, top), T.OHC[:, s], T.OHX[:, s], False, (h, e) == (0, 7), rd, "B6", 64)
 
         def ahead(h):
             s, b = half(h), HASH[h]
-            for i, (l, src) in enumerate((("ID", X), ("IDN", "FX"), ("IDN", "NH"), ("ID", "FC"))):
-                mm(ps(b, 384, 512), T[l][:], T[src][:, s], i == 0, i == 3, [l, (src, h)], b, 128)
-            tt(T.UN[:, s], TX[:, s], ps(b, 384, 512), OP.min, [(X, h), b], [("UN", h)], 128)
-            hashed(["NH", "UN"], h)
+            sums(b, h, ((384, "ID", X), (384, "IDN", "FX"), (384, "ID", "NP"), (384, "ID", "FC")))
+            tt(part(un, h)[0], T.XA[:, s], ps(b, 384, 512), OP.min, [("XA", h), b], [(un, h)], 128)
+            hashed(un, h)
+            if h and SCAN:
+                mm(ps(b, 128, 256), T.ONES[:, 0:128], T.CT[:, 640:768], True, False, ["ONES", ("CT", 640)], b, 128)
+                sums(b, h, ((128, "ID", P),), False)
+                tt(T.DI[:, 0::2], ps(b, 128, 256), T.HI[:, s], OP.subtract, [b, ("HI", h)], [("DI", 0)], 128)
+                cp(T.DI[:, 1::2], T.HI[:, s], [("HI", h)], [("DI", 1)], 128)
 
-        lane(1)
-        lane(0)
-        place_f(1)
-        lookup_f(1)
-        if t < 2:
-            ahead(1)
-        if CODE_FIRST:
-            coded(1)
-        place_f(0)
-        lookup_f(0)
-        if not CODE_FIRST:
-            coded(1)
-        coded(0)
+        parts = dict(lane=lane, letters=letters, place=place_f, lookup=lookup_f, ahead=ahead, coded=coded, hot=hot_x, table=table)
+        for name in TEXT:
+            h = int(name[-1])
+            if name[:-1] != "ahead" or (t < 2 and h in AHEAD):
+                step[0] = (t, name)
+                parts[name[:-1]](h)
+        step[0] = (t, "mask")
         for h in (1, 0):
-            hot_x(h)
-        for h in (1, 0):
-            table(h)
-        if t < 2 and 0 in AHEAD:
-            ahead(0)
-        mm(ps("B4", 256, 512), T.BO[:], T.FX[:], True, False, ["BO", "FX"], "B4", 256)
-        mm(ps("B4", 256, 512), T.ID[:], T.NH[:], False, True, ["ID", "NH"], "B4", 256)
-        act(T.AQ[:], ps("B4", 256, 512), ["B4", ("PF", 8)], ["AQ"], 256, func=AF.Abs, bias=T.PF[:, 8:9])
-        act(T.MK[:], T.AQ[:], ["AQ"], ["MK"], 256, func=AF.Relu, scale=-1.0, bias=2.5)
-        mm(ps("B4", 0, 256), T.ID[:], TX[:], True, False, ["ID", X], "B4", 256)
-        mm(ps("B4", 0, 256), T.ID[:], T.NH[:], False, True, ["ID", "NH"], "B4", 256)
-        act(T.XA[:], ps("B4", 0, 256), ["B4"], ["XA"], 256)
-        calls[-1]["soon"] = SOON[2]
+            sums("B4", h, ((128 * h, "BO", "FX"), (128 * h, "BON64", "FB")))
+        act(T.MK[:], ps("B4", 0, 256), ["B4", ("PF", 8)], ["MK"], 256, func=AF.Sign, scale=-1.0, bias=T.PF[:, 8:9])
+        if "kl" in ONV:
+            ts(T.EQ[:, :, 16:50:33], T.KB[:, :, ::16], 1.0 / 8192, OP.mult, ["KB"], [("EQ", 0, "h"), ("EQ", 1, "h")], 5.0, OP.add)
+        else:
+            act(T.EQ[:, :, 16:50:33], T.KB[:, :, ::16], ["KB"], [("EQ", 0, "h"), ("EQ", 1, "h")], 16, func=AF.Identity, scale=1.0 / 8192, bias=5.0)
+        step[0] = (t, "codes")
         for o in range(2):
-            if "kl" in ONV:
-                ts(T.KL[:, :, 4 * o:4 * o + 4], T.KB[:, :, 16 * o], 1.0 / 8192, OP.mult, ["KB"], [("KL", o)], 1.25, OP.add)
-            else:
-                act(T.KL[:, :, 4 * o:4 * o + 4], T.KB[:, :, 16 * o], ["KB"], [("KL", o)], 8, func=AF.Identity, scale=1.0 / 8192, bias=1.25)
             cp(T.CI[:, :, 4 * o:4 * o + 4], T.KC[:, :, 16 * o], ["KC"], [("CI", o)])
         ts(T.CI[:], T.CI[:], 255, OP.bitwise_and, ["CI"], ["CI"])
         cp(T.CL[:], T.CI[:], ["CI"], ["CL"])
-        if "dm" in ONV:
-            ts(T.D16[:], T.SUB[:], 0.5, OP.mult, ["SUB"], ["D16"], 1535.75, OP.add, 128)
-            ts(T.DM[:], T.D16[:], -1536.0, OP.add, ["D16"], ["DM"], n=128)
-        else:
+        step[0] = (t, "d16")
+        if "g1" in ONV:
             act(T.D16[:], T.SUB[:], ["SUB"], ["D16"], 256, func=AF.Identity, scale=0.5, bias=1535.75)
-            act(T.DM[:], T.D16[:], ["D16"], ["DM"], 256, func=AF.Identity, bias=-1536.0)
-        ts(T.TB[top, :], ps("B6", 0, 64, top), 1.0, OP.min, ["B6"], ["TB"])
+        else:
+            act(T.D16[:, 0:128], T.SUB[:, 0:128], [("SUB", 0)], [("D16", 0)], 128, func=AF.Identity, scale=0.5, bias=1535.75)
+        step[0] = (t, "spread")
+        ts(T.TB[top, :], ps("B6", 0, 64, top), 0.5, OP.min, ["B6"], ["TB"])
         for r in range(4):
             mm(ps("B6", 256 + 64 * r, 320 + 64 * r), T.RX[top, 128 * r:128 * r + 128], T.TB[top, :], True, True, ["RX", "TB"], "B6", 64)
-        cp(T.TW[:], ps("B6", 256, 512), ["B6"], ["TW"], 256)
+        (act if "tw" not in ONV else cp)(T.TW[:], ps("B6", 256, 512), ["B6"], ["TW"], 256)
         for h in (1, 0):
             s, b = half(h), ENDS[h]
-            tt(T.GT[:, s], T.TW[:].indirect(T.CL[:, 8 * h:8 * h + 8]), T.MK[:, s], OP.mult, ["TW", "CL", "MK"], [("GT", h)], gathered(128))
-            terms = [(0, "ID", TX[:, s], X), (0, "IDN", T.FX[:, s], "FX"), (128, "BO", T.FH[:, 4 * h:4 * h + 4, :], "FH"),
-                     (128, "ID128", T.NH[:, s], "NH"), (0, "ID", T.FC[:, s], "FC"), (0, "BO64", T.GT[:, s], "GT"), (128, "BO8192", T.GT[:, s], "GT")]
-            if t < 2 and h in AHEAD:
-                terms[5:5] = [(256, "ID", T.H16[:, s], "H16"), (256, "ONES", T.CT[:, 512:640], "CT"), (256, "BO12288", T.GT[:, s], "GT")]
-            for i, (o, l, src, key) in enumerate(terms):
-                mm(ps(b, o, o + 128), T[l][:, 0:128], src, i == 0, i == len(terms) - 1, [l, (key, h) if key != "CT" else key], b, 128)
-            tt(T[xn][:, s], T.XA[:, s], ps(b, 0, 128), OP.min, ["XA", b], [(xn, h)], 128)
-            if t < 2:
-                if h in AHEAD:
-                    tt(T.PR[:, s], ps(b, 256, 384), T.HI[:, s], OP.max, [b, ("HI", h)], [("PR", h)], 128)
+            step[0] = (t, "ends", h)
+            tt(T.GT[:, s], T.TW[:].indirect(T.CL[:, 8 * h:8 * h + 8]), T.MK[:, s], OP.mult, ["TW", "CL", "MK"], [("GT", h)])
+            indirect("picks", 128)
+            rows = [(128, "BO", "FH"), (128, "BO8192", "NP"), (128, "BO8192", "GT")]
+            if t == 2 or h not in AHEAD:
+                rows = [(0, "ID", X), (0, "IDN", "FX"), (0, "ID", "NP"), (0, "ID", "FC")] + rows + [(0, "BO64", "GT")]
+            sums(b, h, rows)
+            step[0] = (t, "change", h)
+            if t == 2:
+                tt(T.XN[:, s], T.XA[:, s], ps(b, 0, 128), OP.min, [("XA", h), b], [("XN", h)], 128)
+            elif h not in AHEAD:
+                hn, o2 = "HN%d" % t, 256 * h
+                tt(part(un, h)[0], T.XA[:, s], ps(b, 0, 128), OP.min, [("XA", h), b], [(un, h)], 128)
+                send(dst, part("X%d" % (t + 1), h)[0], part(un, h)[0], [(un, h)], [("X%d" % (t + 1), h)], ("aw", "ax")[h] + str(t + 1))
+                hashed(un, h)
+                cp(T[hn][:, o2:o2 + 128], T.HI[:, s], [("HI", h)], [(hn, h)], 128)
+                send(dst, part("H%d" % (t + 1), h)[0], T[hn][:, o2:o2 + 128], [(hn, h)], [("H%d" % (t + 1), h)], ("az", "ay")[h] + str(t + 1))
+            else:
+                o, c, sem = 512 * h, HASH[h], ("az", "ay")[h] + str(t + 1)
+                hn, o2 = "HN%d" % t, 256 * h
+                if h and SCAN:
+                    mm(T[c][:, 256:512], T.ZR[:], T.ONES[:], True, False, ["ZR", "ONES"], c, 256)
+                    mm(T[c][:, 257:512:2], T.BO[:], T.GT[:, s], False, True, ["BO", ("GT", h)], c, 128)
+                    do("v", [c, "DI"], ["SO"], cycles(256), "scan", dict(out=T.SO[:], data0=T[c][:, 256:512], data1=T.DI[:], initial=0.0,
+                                                                         op0=OP.mult, op1=OP.add))
+                    cp(T[hn][:, o2:o2 + 128], T.SO[:, 1::2], ["SO"], [(hn, h)], 128)
+                else:
+                    mm(ps(c, 128, 256), T.ONES[:, 0:128], T.CT[:, 512:640], True, False, ["ONES", ("CT", 512)], c, 128)
+                    sums(c, h, ((128, "ID", P), (128, "BO8192", "GT")), False)
+                    tt(T.PR[:, s], ps(c, 128, 256), T.HI[:, s], OP.max, [c, ("HI", h)], [("PR", h)], 128)
                     ts(T.HI[:, s], T.PR[:, s], 4095, OP.bitwise_and, [("PR", h)], [("HI", h)], n=128)
+                    cp(T[hn][:, o2:o2 + 128], T.HI[:, s], [("HI", h)], [(hn, h)], 128)
+                send(dst, part("H%d" % (t + 1), h)[0], T[hn][:, o2:o2 + 128], [(hn, h)], [("H%d" % (t + 1), h)], sem)
+                places_out = len(calls) - 1
+                step[0] = (t, "letters out", h)
+                if "x%d" % h in FOLDS:
+                    sums("B4", h, ((128 * h, "ID", X), (128 * h, "BO64", "GT")))
+                    act(T[out][:, o + 256:o + 384], ps("B4", 128 * h, 128 * h + 128), ["B4"], [(out, h, "x")], 128, func=AF.Identity, bias=-64.0)
+                    letters_out = [T[out][:, o + 256:o + 384], part(un, h)[0]]
+                elif "x%d" % h not in ONV:
+                    sums("B4", h, ((128 * h, "ID", X), (128 * h, "IDN", un), (128 * h, "BO64", "GT")))
+                    act(T.XR[:, s], ps("B4", 128 * h, 128 * h + 128), ["B4"], [("XR", h)], 128, func=AF.Relu, bias=-64.0)
+                    sums("B4", h, ((128 * h, "ID", un), (128 * h, "ID", "XR")))
+                    letters_out = T[out][:, o + 256:o + 384]
+                    act(letters_out, ps("B4", 128 * h, 128 * h + 128), ["B4"], [(out, h, "x")], 128)
                 else:
-                    hashed([xn], h)
-                cp(T[hn][:, s], T.HI[:, s], [("HI", h)], [(hn, h)], 128)
-                sem = ("aw", "ax")[h] + str(t + 1)
-                if sem in RELAY and FUSED:
-                    send(dst, T[H1][:, s], T[hn][:, s], [(hn, h), (xn, h)], [(H1, h), ("with", t, h)], ("az", "ay")[h] + str(t + 1),
-                         also=(T[X1][:, s], T[xn][:, s], sem))
-                    do("far", [("with", t, h)], [(X1, h)], 1, "lands", (dst, sem), FARX - FAR)
-                else:
-                    send(dst, T[X1][:, s], T[xn][:, s], [(xn, h)], [(X1, h)], sem, FARX if sem in RELAY else FAR)
-                    send(dst, T[H1][:, s], T[hn][:, s], [(hn, h)], [(H1, h)], ("az", "ay")[h] + str(t + 1))
-            for o, a, c in ((0, 0, 0), (128, 16, 16), (129, 16, 0)):
-                tt(T.EQ[:, 256 * h + o:256 * h + o + 127:2], T.KB[:, 4 * h:4 * h + 4, a:a + 16], T[b][:, 4:8, c:c + 16], OP.is_equal,
-                   [("KB", h), b], [("EQ", h, o)])
-            s2 = slice(256 * h, 256 * h + 256)
-            do("v", ["RR", ("EQ", h)], [("SC", h)], cycles(128), "scan", dict(out=T.SC[:, s2], data0=T.RR[:], data1=T.EQ[:, s2], initial=0.0,
-                                                                            op0=OP.mult, op1=OP.add))
-            if t not in WHOLE:
-                tt(T.Y[:, h, :], T.SC[:, 256 * h + 31:256 * h + 256:32], T.KL[:, h, :], OP.add, [("SC", h), "KL"], [("Y", h)])
-                for o in range(2):
-                    ts(T.OFU[:, 8 * h + o:8 * h + 8:2], T.Y[:, h, 4 * o:4 * o + 4], 8192.0, OP.mult, [("Y", h), ("PF", 11 + o)],
-                       [("OFU", h, o)], T.PF[:, 11 + o:12 + o], OP.min)
-        if t in WHOLE:
-            tt(T.Y[:], T.SC[:, 31::32], T.KL[:], OP.add, ["SC", "KL"], ["Y"])
-            for o in range(2):
-                ts(T.OFU[:, o::2], T.Y[:, :, 4 * o:4 * o + 4], 8192.0, OP.mult, ["Y", ("PF", 11 + o)], [("OFU", 0, o), ("OFU", 1, o)],
-                   T.PF[:, 11 + o:12 + o], OP.min)
-        if t == 2:
-            send(dst, T[X1][:], T[xn][:], [xn], [X1], "ax3", FARX)
-        for i, (l, src) in enumerate((("ID", "ONES"), ("IDN64", "NH"), ("BON", "GT"))):
-            mm(ps("B2", 0, 256), T[l][:], T[src][:], i == 0, i == 2, [l, src], "B2", 256)
-        tt(T.GD[:], T.DM[:], ps("B2", 0, 256), OP.mult, ["DM", "B2"], ["GD"], 256)
-        mm(ps("B3", 0, 256), T.ID[:], TM[:], True, False, ["ID", M], "B3", 256)
-        mm(ps("B3", 0, 256), T.ID[:], T.GD[:], False, True, ["ID", "GD"], "B3", 256)
-        act(T[mn][:], ps("B3", 0, 256), ["B3"], [mn], 256)
-        in_line("gather")
-        scatter("LX", xn)
-        if t < 2:
-            scatter("LM", mn)
-        send(dst, T[M1][:], T[mn][:], [mn] + ([H1] if t < 2 and "am" + str(t + 1) not in RELAY else []), [M1], "am" + str(t + 1), FARM if t < 2 else FARE)
-        if t == 0:
-            calls[-1]["behind"] = [i for i, c in enumerate(calls[:-1]) if c["name"] == "send"]
-            lines["sent"] = [len(calls) - 1]
-            lowest(2)
-            iota(T.NUM[:], [[-1, 256]], -1, 0, ["NUM"], 256)
-            in_line("sent")
+                    mm(ps("B4", 128 * h, 128 * h + 128), T.ONES[:, 0:128], T.CT[:, 1024:1152], True, False, ["ONES", ("CT", 1024)], "B4", 128)
+                    sums("B4", h, ((128 * h, "ID", X), (128 * h, "BO64", "GT")), False)
+                    letters_out = T[out][:, o + 256:o + 384]
+                    tt(letters_out, part(un, h)[0], ps("B4", 128 * h, 128 * h + 128), OP.max, ["B4", (un, h)], [(out, h, "x")], 128)
+                send(dst, part("X%d" % (t + 1), h)[0], letters_out, [(out, h, "x"), (un, h)], [("X%d" % (t + 1), h)], ("aw", "ax")[h] + str(t + 1))
 
-    scatter("EB", "NUM")
+            c4, step[0] = slice(4 * h, 4 * h + 4), (t, "who", h)
+            for o, a, c in ((0, 0, 0), (17, 16, 16), (33, 16, 0)):
+                tt(T.EQ[:, c4, o:o + 16], T.KB[:, c4, a:a + 16], T[b][:, 4:8, c:c + 16], OP.is_equal, [("KB", h), b], [("EQ", h, o)])
+            for j in range(4 * h, 4 * h + 4):
+                do("v", ["RR", ("EQ", h)], [("SC", h, j)], cycles(50), "scan",
+                   dict(out=T.SC[:, j, :], data0=T.RR[:], data1=T.EQ[:, j, :], initial=0.0, op0=OP.mult, op1=OP.add))
+            for o in range(2):
+                ts(T.OFU[:, 8 * h + o:8 * h + 8:2], T.SC[:, c4, 16 + 33 * o], 8192.0, OP.mult, [("SC", h), ("PF", 11 + o)],
+                   [("OFU", h, o)], T.PF[:, 11 + o:12 + o], OP.min)
+        if t == 2:
+            send(dst, T.X3[:], T.XN[:], ["XN"], ["X3"], "ax3", 1.5)
+        for h in (1, 0):
+            step[0] = (t, "merged", h)
+            sums("B2", h, [(128 * h, l, src) for l, src in (("ID", M), ("ID", "D16"), ("BON512", "NP"), ("BON512", "GT"))])
+            if t < 2 or h == 0:
+                c0, c1 = (128 * h, 128 * h + 128) if t < 2 else (0, 256)
+                act(T.MA[:, 256 * t + c0:256 * t + c1], ps("B2", c0, c1), ["B2"], [(ma, h) if t < 2 else ma], c1 - c0, func=AF.Identity, bias=-1536.0)
+        step[0] = (t, "kept")
+        for h in (1, 0):
+            sums("B3", h, [(128 * h, l, src) for l, src in (("ID", M), ("BON512", "FB"), ("BO512", "GT"))])
+        if t < 2:
+            act(T[mn][:], ps("B3", 0, 256), ["B3"], [mn], 256)
+        else:
+            tt(T[mn][:], T.MA[:, 512:768], ps("B3", 0, 256), OP.max, ["B3", ma], [mn], 256)
+        scatter("LX", un if t < 2 else "XN")
+        if t < 2:
+            scatter("LM", ma)
+        step[0] = (t, "meanings")
+        send(dst, T[M1][:], [T.MA[:, 256 * t:256 * t + 256], T[mn][:]] if t < 2 else T[mn][:], [mn, ma], [M1], "am" + str(t + 1), 1.5)
+        if t == 0:
+            iota(T.NUM[:], [[1, 256]], 32, 0, ["NUM"], 256)
+            calls[-1]["behind"] = sent = [i for i, c in enumerate(calls[:-1]) if c["name"] == "send"]
+            for e in range(4):
+                iota(T.WN[:, 1032 * e:1032 * e + 1032], [[0, 1032]], 0, 0, [("WN", e)], 1032)
+                calls[-1]["behind"] = sent
+            step[0] = (1, "numbers")
+            act(T.SN[:], T.NUM[:], ["NUM"], ["SN"], 256 + 1600, func=AF.Silu)
+
+    for c in range(7, -1, -1):
+        step[0] = (t, "rest", c // 4)
+        if c >= SPLIT:
+            act(T.WN[:].indirect(T.OFU[:, 2 * c:2 * c + 2]), T.NUM[:, 32 * c:32 * c + 32], [("OFU", c // 4), "NUM", "SN"], ["WN"], 0, func=AF.Silu)
+        else:
+            cp(T.WN[:].indirect(T.OFU[:, 2 * c:2 * c + 2]), T.SN[:, 32 * c:32 * c + 32], [("OFU", c // 4), "SN"], ["WN"])
+        indirect("puts", 32)
+    step[0] = "sum"
     for j in range(8):
-        mm(ps("B6", 0, 512), T.ID[:], T.LM[:, 512 * j:512 * j + 512], j == 0, j == 7, ["ID", "LM", xn], "B6", 512)
-    for i, (l, src) in enumerate((("IDN", "SUB"), ("ID", "DM"))):
-        mm(ps("B4", 0, 256), T[l][:], T[src][:], i == 0, i == 1, [l, src], "B4", 256)
+        mm(ps("B6", 0, 512), T.ID[:], T.LM[:, 512 * j:512 * j + 512], j == 0, j == 7, ["ID", "LM"], "B6", 512)
+    mm(ps("B4", 0, 256), T.ONES[:, 0:128], T.CT[:, 768:1024], True, False, ["ONES", ("CT", 768)], "B4", 256)
+    for h in (0, 1):
+        for l, src in (("IDN", "SUB"),) if "g%d" % h in ONV else (("IDN", "GG"), ("ID", "M2")):
+            mm(ps("B4", 128 * h, 128 * h + 128), T[l][:], T[src][:, half(h)], False, False, [l, (src, h)], "B4", 128)
+    mm(ps("B4", 0, 256), T.ID[:], T.D16[:], False, True, ["ID", "D16"], "B4", 256)
     act(ps("B6", 0, 512), ps("B6", 0, 512), ["B6"], ["B6", "B3", "sum"], 700, accum_out=ps("B3", 0, 1))
     dma("y", T.yl[:], T.LX[:, 0:W], ["LX"], ["yl"], LAST)
-    tt(T.PB[:], T.EB[:, 0:W].indirect(T.LF[:, 0:16]), T.NUM[:], OP.is_equal, ["EB", "NUM", "LF"], ["PB"], gathered(256))
+    tt(T.PB[:], T.WN[:, 0:W].indirect(T.LF[:, 0:16]), T.SN[:], OP.is_equal, ["WN", "SN", "LF"], ["PB"])
+    indirect("picks", 256)
     cp(T.WD[:, 256:257], ps("B3", 0, 1), ["B3"], [("WD", 1)])
     tt(T.WD[:, 0:256], T.PB[:], ps("B4", 0, 256), OP.mult, ["PB", "B4"], [("WD", 0)], 256)
     do("v", ["WD"], ["YM"], cycles(257), "reduce", dict(out=T.PF[:, 15:16], in_=T.WD[:], axis=AxisListType.X, op=OP.add))
@@ -706,10 +790,6 @@ def rank_program(g, core, T, topo):
     for i in _ORDER:
         c = calls[i]
         q, name, kw = c["q"], c["name"], c["kw"]
-        if name == "lands":
-            done[i] = (kw[1], len(topo.engines(helper(core), kw[0])), {})
-            others.append(done[i])
-            continue
         toks = {}
         for tok in ([done[p] for p in c["after"] if not q == calls[p]["q"] == "t"]
                     + [tok for b in c["banks"] for e, tok in touch.get(b, {}).items() if e != q]):
@@ -718,17 +798,12 @@ def rank_program(g, core, T, topo):
         for tok in toks.values():
             wait(q, tok)
         if name == "send":
-            off_chip = topo.engines(core, kw[0])
-            if kw[4]:
-                rest = [e for e in topo.engines(core, helper(core)) if e not in off_chip][:len(off_chip)]
-                g.remote_dma_fused([RemoteDMATransfer(dst_ids=[DstId(rid=topo.addr(to)[0], pnc=topo.addr(to)[1])], dst=out, src=src,
-                                                      remote_sem=T.sem[sem], dma_engine_mask=sum(1 << e for e in engines))
-                                    for to, engines, (out, src, sem) in ((kw[0], off_chip, kw[1:4]), (helper(core), rest, kw[4]))],
-                                   local_sem=T.sem.ls)
-                n_sent += len(rest)
+            mask = topo.mask(core, kw[0])
+            if kw[3] in HANDED:
+                write(helper(core), kw[1], kw[2], kw[3], topo.mask(core, helper(core)) & ~mask if SPARE else mask)
             else:
-                write(helper(core) if kw[3] in [x[4] for x in HANDED] else kw[0], kw[1], kw[2], kw[3], topo.mask(core, kw[0]))
-            done[i] = (kw[3], len(off_chip), {})
+                write(kw[0], kw[1], kw[2], kw[3], mask)
+            done[i] = (kw[3], len(topo.engines(core, kw[0])), {})
             n_sent += done[i][1]
             others.append(done[i])
             continue

from concourse.bass import DstId, RemoteDMATransfer
from concourse.mybir import AluOpType, AxisListType, ActivationFunctionType

OP = AluOpType
AF = ActivationFunctionType
W, K = 4096, 256
_P = ((224, 256, 1), (208, 224, 1), (192, 208, 0), (128, 192, 0), (0, 64, 0), (64, 96, 0), (96, 128, 0))
PIECES = (_P, _P, _P)
ONV = ("tw", "g0", "g1", "x1")
IDLE = ()
ZERO = 4
LETTERS, NONE = ("B4", "B0"), ("B4", "B4")
LAID = ("B7", "B1"), ("B2", "B0"), ("B2", "B5"), ("B7", "B5"), ("B1", "B0"), ("B7", "B6")
TEXT = "lane1 letters1 lane0 place1 lookup1 ahead1 coded1 place0 lookup0 coded0 hot1 letters0 hot0 ahead0 table1 table0".split()
CYCLE = 0.83
COLUMN = 0.5
CALL = 120
ISSUE = 200
SCAN = False
SPLIT = 2
LOWER = 0
HOME = 900
FAR, MOVING, FOLD = 1600, 700, 1.6
LOADX, LOADM, LAST = 5000, 6200, 4000
FIRST = 0
SLOWG = 1.5
CASES = ((1.2, 1.2, 0, 210, 1.3, 1, 1.56, 3.8), (1, 1, 0, 200, 1, 1, 1.56, 3.8), (1.1, 1.2, 0, 200, 1.6, 1.2, 1.9, 2.5),
         (1.3, 1.3, -30, 220, 1.2, 1, 1.2, 5.2), (1.4, 1.4, 0, 200, 1.2, 1, 1.9, 4.5))
PLANS = ((1.15, 1.15, 0, 210, 1.25, 1, 1.56, 3.8),)
AT = {"offsets 1": -95, "offsets 0": -71, "gather": -102, "lane1": -91, "f 1": -70, "np 1": -63, "letters1": -43, "lane0": -67, "f 0": -42,
      "np 0": -36, "place1": -58, "lookup1": -45, "ahead1": -34, "coded1": -44, "place0": -31, "lookup0": -22, "coded0": -24, "hot1": -40,
      "letters0": -26, "hot0": -25, "ahead0": -17, "table1": -23, "table0": -12, "mask": -13, "codes": -3, "d16": -5, "spread": 0,
      "ends 1": -1, "change 1": 4, "letters out 1": 4, "who 1": 18, "ends 0": 0, "change 0": 30, "letters out 0": 24, "who 0": 24,
      "merged 1": 10, "merged 0": 28, "kept": 12, "letters 1": 29, "letters 0": 43, "rest 1": 35, "rest 0": 50, "meanings": 59, "numbers": 35, "xf 1": -62, "xf 0": -38}
MOVE, SLACK, SEED = 1500, 250, 7
PACKS, SHAKE, WINDOW = 3200, (300, 100, 600), 6000
_NOTE = []

_S, _ORDER = {}, []


def _sb(name, cols, dtype="bfloat16"):
    _S[name] = ("sbuf", [128, cols], dtype)


_sb("LX", W + 32)
_sb("LM", W + 32)
for _n in ("X0", "M0", "M1", "M2", "X3", "M3", "XN", "MN0", "MN1", "MN2"):
    _sb(_n, K)
_sb("MA", 3 * K)
for _n in ("MG", "MP"):
    _sb(_n, 128, "float32")
_sb("PI", 4, "int32")
_sb("PF", 16, "float32")
for _n in ("T3", "PC"):
    _sb(_n, 4, "float32")
_sb("LE", 12, "float32")
_sb("WI", 2, "int32")
_sb("WF", 2, "float32")
_sb("THI", 1, "int32")
for _n in ("BO", "BO64", "BON64", "BO8192", "ZR", "BON128", "BON512", "BO512", "ID", "IDN", "SL", "MNE", "BOX", "W1", "W2", "W132", "W232",
           "LTH", "LTX", "LTF", "BT0", "BT1", "BT2", "IDN4096"):
    _sb(_n, 128)
_sb("ONES", 256)
_sb("CT", 1152)
for _n in ("THB", "B30", "BNA", "BPA", "BA", "BC"):
    _sb(_n, 8, "float16")
for _n in range(4):
    _sb("PM%d" % _n, 128, "float16")
    _sb("PN%d" % _n, 128, "float16")
_sb("SK", 2048)
_sb("RX", 512)
_sb("IO64", 64)
for _n in ("NUM", "SN"):
    _sb(_n, 256, "float32")
_sb("WN", W + 32, "float32")
_sb("RW", 64, "float32")
_sb("RR", 50)
for _n in ("EQ", "SC"):
    _S[_n] = ("sbuf", [128, 8, 50], "float32")
for _n in ("PR", "ZI", "HI"):
    _sb(_n, 256, "int32")
_sb("UP", 256, "float32")
_sb("Q", 512)
for _n in ("H0", "H1", "H2"):
    _sb(_n, 256, "uint16")
for _n in ("P0", "P1", "P2", "X1", "X2", "N16", "FC", "D16", "RL"):
    _sb(_n, 256, "float16")
for _n in range(2):
    _sb("OUT%d" % _n, 1024, "float16")
    _sb("HN%d" % _n, 512, "uint16")
_sb("XF", 512, "float16")
for _n in ("XR", "PB", "NP", "XA", "SUB", "MK", "TW", "GT"):
    _sb(_n, 256)
_sb("CB", W)
_sb("EB", W + 32)
_S["FH"] = ("sbuf", [128, 8, 32], "float16")
_S["KB"] = ("sbuf", [128, 8, 32], "float32")
_S["KC"] = ("sbuf", [128, 8, 32], "float32")
_S["CI"] = ("sbuf", [128, 2, 8], "int32")
_sb("WD", 257, "float32")
for _n in ("LF", "CL", "OFU"):
    _sb(_n, 16, "uint16")
_sb("OHX", 1024)
_sb("OHC", 1024)
_sb("TB", 64)
BANKS = ["B%d" % _i for _i in range(8)]
for _n in BANKS:
    _S[_n] = ("psum", [128, 16, 32] if _n != "B0" else [128, 512], "float32")
for _n in ("DI", "SO"):
    _sb(_n, 256, "float32")
SCRATCH = _S
SEMAPHORES = (["qv", "qs", "qt", "qg", "ls"] + ["d%d" % _i for _i in range(11)]
              + [_n + str(_i) for _n in ("aw", "ax", "ay", "az", "am") for _i in range(1, 4)])
HANDED = {"am1": (0, "M1", 0, 256), "am2": (1, "M2", 0, 256)}
AHEAD = (0, 1)
SCALED = 7
FOLDS = ()
HALF = ()
SPARE = True


def in_order(calls):
    n = len(calls)
    queue = [c["q"] for c in calls]
    banks = [c["banks"] if c["q"] != "t" else () for c in calls]

    def priced(slow, column, call, hop, far, load, gather, scatter):
        cost = [(c["cost"] + CYCLE * (gather * c["picks"] + scatter * c["puts"])) * (column if c["q"] == "t" else far if c["name"] == "send" else slow)
                + (call if c["name"] == "act" else 0) for c in calls]
        late = [c["late"] * {"send": far, "dma": load}.get(c["name"], 1) for c in calls]
        before, later = [[] for _ in calls], [[] for _ in calls]
        for i, c in enumerate(calls):
            for p, gap in ([(p, 0 if c["q"] == calls[p]["q"] == "t" else late[p] + hop) for p in c["after"]] + [(p, 0) for p in c["behind"]]):
                before[i].append((p, gap))
                later[p].append((i, gap))
        return cost, late, before, later, hop

    def length(order, cost, late, before, later, hop):
        end, last, bank, total = [0] * n, {q: 0 for q in queue}, {b: [0, 0] for b in BANKS}, 0
        for i in order:
            q = queue[i]
            at = last[q]
            for p, gap in before[i]:
                if end[p] + gap > at:
                    at = end[p] + gap
            for b in banks[i]:
                if bank[b][q == "s"] > at:
                    at = bank[b][q == "s"]
            at += cost[i]
            for b in banks[i]:
                bank[b][q != "s"] = at + hop
            end[i] = last[q] = at
            if at + late[i] > total:
                total = at + late[i]
        return total

    def packed(rank, waits, frees, first, cost, hop):
        end, left, taken, bank = [0] * n, [len(w) for w in waits], {q: [] for q in queue}, {b: ([], []) for b in BANKS}
        todo = sorted(((rank[i], i) for i in range(n) if not left[i]), reverse=True)
        while todo:
            i = todo.pop()[1]
            q, c, at = queue[i], cost[i], first[i]
            for p, gap in waits[i]:
                if end[p] + gap > at:
                    at = end[p] + gap
            mine, others = taken[q], [x for b in banks[i] for x in bank[b][q == "s"]]
            k = len(mine)
            while k and mine[k - 1][1] > at:
                k -= 1
            while True:
                while k < len(mine) and mine[k][0] < at + c:
                    if mine[k][1] > at:
                        at = mine[k][1]
                    k += 1
                clash = [e for s, e in others if s < at + c + hop and at < e + hop]
                if not clash:
                    break
                at = max(clash) + hop
            mine.insert(k, (at, at + c))
            end[i] = at + c
            for b in banks[i]:
                bank[b][q != "s"].append((at, at + c))
            for j, gap in frees[i]:
                left[j] -= 1
                if not left[j]:
                    k, x = len(todo), (rank[j], j)
                    while k and todo[k - 1] < x:
                        k -= 1
                    todo.insert(k, x)
        return end

    cases, plans, best, draw, zero = [priced(*case) for case in CASES], [priced(*plan) for plan in PLANS], None, SEED, [0] * n
    steps, kept = {}, None
    for i, c in enumerate(calls):
        steps.setdefault(c["step"], []).append(i)
    twins = [{(k[1:], j): i for k, v in steps.items() if k[0] == t for j, i in enumerate(v)} for t in range(3)]
    first = [steps[t, "spread"][0] for t in range(3)]
    steps = list(steps.values())
    for r in range(PACKS):
        cost, late, before, later, hop = plans[r % len(plans)]
        if best is None:
            way = [0] * n
            for i in range(n - 1, -1, -1):
                way[i] = cost[i] + max([way[j] + gap for j, gap in later[i]] + [late[i]])
            for step in steps:
                key, top = calls[step[0]]["step"], max(way[i] for i in step)
                at = 16200 * (key[0] + 1) + 100 * AT[" ".join(str(x) for x in key[1:])] if key[0] in (0, 1, 2) else (way[0] - top) * (1.2 if key == "sum" else 0.5)
                for i in step:
                    way[i] -= top + at
        else:
            start, size = list(best[2]), SHAKE[r // len(plans) % len(SHAKE)]
            draw = (draw * 1103515245 + 12345) % 2 ** 31
            if r % 15 == 14:
                a, b = ((0, 1), (1, 0), (1, 2), (2, 1))[(draw >> 8) % 4]
                shift = start[first[b]] - start[first[a]]
                for key, i in twins[a].items():
                    if key in twins[b]:
                        start[twins[b][key]] = best[2][i] + shift
            elif r % 3:
                for i in steps[(draw >> 8) % len(steps)]:
                    start[i] += MOVE * ((draw >> 18) % 64 - 31.5) / 32
            else:
                lo = (draw >> 8) % int(max(start) + WINDOW) - WINDOW
                for i in range(n):
                    if lo < start[i] < lo + WINDOW:
                        draw = (draw * 1103515245 + 12345) % 2 ** 31
                        start[i] += size * ((draw >> 8) % 1024 - 512) / 512
            way = packed([-x for x in start], later, before, late, cost, hop) if r % 3 < 2 else [c - x for c, x in zip(cost, start)]
        end = packed([-x for x in way], before, later, zero, cost, hop)
        if best and max(end) > max(best[2]) + 300:
            continue
        order = sorted(range(n), key=lambda i: (end[i] - cost[i], i))
        total, slack = [], SLACK * (1 - r / PACKS)
        for k, case in enumerate(cases):
            total.append(length(order, *case) / CASES[k][0])
            if best and sum(total) > sum(best[3][:k + 1]) + slack + 150 * (len(cases) - 1 - k):
                break
        else:
            best = (sum(total), order, end, total)
            if kept is None or best[0] < kept[0]:
                kept = best
                _NOTE[:] = [(r, round(sum(total) / len(total) / 1000, 2), [round(x / 1000, 2) for x in total])]
    return kept[1]


def rank_program(g, core, T, topo):
    n_ranks = len(T.cores)

    def target(c, t):
        return T.cores[(T.rank_of(c) + (3 if t < 2 else 2)) % n_ranks]

    def helper(c):
        ranks = [r for r in topo.cores_of(c) if T.rank_of(r) is not None]
        able = [h for h in topo.cores_of(c) if topo.die(h) != topo.die(c) and all(topo.may_write(h, target(r, t)) for r in ranks for t in range(3))]
        return able[ranks.index(c)]

    def write(dst, out, src, sem, mask):
        rid, pid, _eng = topo.addr(dst)
        if isinstance(src, list):
            g.remote_dma_fused([RemoteDMATransfer(dst_ids=[DstId(rid=rid, pnc=pid)], dsts=[out], srcs=src, alu_op=2, remote_sem=T.sem[sem],
                                                  dma_engine_mask=mask)], local_sem=T.sem.ls)
        else:
            g.remote_dma(out, src, T.sem[sem], T.sem.ls, pid, rid, mask)

    if T.rank_of(core) is None:
        for c in topo.cores_of(core):
            if T.rank_of(c) is not None and helper(c) == core:
                n = 0
                for sem, (t, name, c0, c1) in HANDED.items():
                    dst = target(c, t)
                    g.wait_ge(T.sem[sem], len(topo.engines(c, dst)))
                    write(dst, T[name][:, c0:c1], T[name][:, c0:c1], sem, topo.mask(core, dst))
                    n += len(topo.engines(core, dst))
                g.wait_ge(T.sem.ls, n)
        return
    calls, known, lines, step = [], {}, {}, [None]

    def do(q, reads, writes, cost, name, kw, late=0):
        after = set()
        reads, writes = [[k if isinstance(k, tuple) else (k,) for k in keys] for keys in (reads, writes)]
        for keys, overwrites in ((reads, False), (writes, True)):
            for k in keys:
                for other, (writer, readers) in known.setdefault(k[0], {}).items():
                    if other[:len(k)] == k[:len(other)]:
                        after.update(writer + (readers if overwrites else []))
        for k in reads:
            known[k[0]].setdefault(k, ([], []))[1].append(len(calls))
        for k in writes:
            for other in [o for o in known[k[0]] if o[:len(k)] == k]:
                del known[k[0]][other]
            known[k[0]][k] = ([len(calls)], [])
        calls.append({"q": q, "name": name, "kw": kw, "cost": cost, "late": late, "after": after, "behind": [], "picks": 0, "puts": 0,
                      "step": step[0] or writes[0][0],
                      "banks": {k[0] for k in reads + writes if k[0] in BANKS}})

    def in_line(name):
        calls[-1]["behind"] = lines.get(name, [])
        lines[name] = [len(calls) - 1]

    def indirect(kind, n):
        calls[-1].update({kind: n, "cost": 50 if calls[-1]["q"] == "v" else CALL})

    def dma(q, out, in_, reads, writes, late):
        do(q, reads, writes, 50, "dma", (out, in_), late)
        if q == "y":
            in_line(q)

    def send(dst, out, src, reads, writes, sem, size=1):
        size *= FOLD if isinstance(src, list) else 1
        if sem in HANDED:
            do("g", reads, writes, ISSUE, "send", (dst, out, src, sem), 1.7 * FAR + 1.6 * size * MOVING + HOME * (sem[2] == "3"))
            in_line("handed")
        else:
            do("g", reads, writes, ISSUE + size * MOVING + FIRST * (sem == "ax1"), "send", (dst, out, src, sem), FAR + HOME * (sem[2] == "3") + LOWER * (sem[1] == "z"))


    def cycles(n):
        return max(64, n) * CYCLE

    def cp(out, in_, r, w, n=0):
        do("v", r, w, cycles(n), "copy", dict(out=out, in_=in_))

    def tt(out, a, b, op, r, w, n=0):
        do("v", r, w, cycles(n), "tt", dict(out=out, in0=a, in1=b, op=op))

    def ts(out, a, s1, op0, r, w, s2=None, op1=None, n=0):
        kw = dict(out=out, in0=a, scalar1=s1, scalar2=s2, op0=op0)
        if op1 is not None:
            kw["op1"] = op1
        do("v", r, w, cycles(n), "ts", kw)

    def tr(out, in_, r, w):
        do("v", r, w, cycles(128), "turn", dict(out=out, in_=in_))

    def fill(ap, c, w, n=0):
        do("v", [], w, cycles(n), "fill", (ap, c))

    def act(out, in_, r, w, n, func=AF.Copy, **kw):
        do("s", r, w, CALL + n * CYCLE, "act", dict(out=out, in_=in_, func=func, **kw))

    def mm(out, l, r, start, stop, rd, b, n):
        do("t", rd, [b], max(64, n) * COLUMN, "mm", (out, l, r, start, stop), 60)

    def iota(out, pattern, base, cm, w, n, small=True):
        kw = dict(out=out, pattern=pattern, base=base, channel_multiplier=cm)
        if small:
            kw["allow_small_or_imprecise_dtypes"] = True
        do("g", [], w, SLOWG * (130 + 2 * n * CYCLE), "iota", kw)

    def pick(out, in_, pattern, op, other, r, w, n, base=0, cm=-1):
        do("g", r, w, SLOWG * (170 + 2 * n * CYCLE), "pick", dict(out=out, in_=in_, pattern=pattern, compare_op=op, fill=other, base=base,
                                                       channel_multiplier=cm))

    def half(h):
        return slice(128 * h, 128 * h + 128)

    def ps(b, c0, c1, p=slice(None)):
        if b == "B0":
            return T[b][p, c0:c1]
        if c0 % 32 == 0 and c1 % 32 == 0:
            return T[b][p, c0 // 32:c1 // 32, :]
        return T[b][p, c0 // 32, c0 % 32:c0 % 32 + c1 - c0]

    shared = {"FX": ("XF", 256, 0), "FB": ("XF", 256, 128),
              "UN0": ("OUT0", 512, 384), "UN1": ("OUT1", 512, 384), "MA0": ("MA", 128, 0), "MA1": ("MA", 128, 256)}

    def part(name, h, c0=0, c1=128):
        if name == "FH":
            return T.FH[:, 4 * h:4 * h + 4, :], (name, h)
        buf, n, o = shared.get(name, (name, 128, 0))
        return T[buf][:, n * h + o + c0:n * h + o + c1], (name if name[:2] in ("UN", "MA") else buf, h)

    def sums(b, h, terms, start=True):
        for i, (o, l, src) in enumerate(terms):
            ap, key = part(src, h)
            mm(ps(b, o, o + 128), T[l][:, 0:128], ap, start and i == 0, i == len(terms) - 1, [l, key], b, 128)

    dma("y", T.X0[:], T.xw[:], [], ["X0"], 1500)
    dma("s", T.WI[:], T.wts[:], [], ["WI"], 1400)
    dma("y", T.LX[:, 0:W], T.lex[:], [], ["LX"], LOADX)
    dma("s", T.THI[:], T.th[:], [], ["THI"], 1400)
    dma("y", T.M0[:], T.gw[:], ["LX"], ["M0"], 1500)
    dma("y", T.LM[:, 0:W], T.mng[:], ["LX"], ["LM"], LOADM)

    col = [[1, 128]]
    iota(T.PI[:, 0:1], [[0, 1]], 0, 1, [("PI", 0)], 1, False)
    iota(T.MG[:], [[1, 8], [0, 16]], 0, 0, ["MG"], 128)
    fill(T.ONES[:], 1.0, ["ONES"], 128)
    ts(T.PI[:, 1:2], T.PI[:, 0:1], 4, OP.arith_shift_right, [("PI", 0)], [("PI", 1)])
    ts(T.PI[:, 2:3], T.PI[:, 0:1], 15, OP.bitwise_and, [("PI", 0)], [("PI", 2)])
    for a, b, c in ((0, 256, -65536.0), (256, 384, 5120.0), (512, 640, -16.0), (640, 768, 16.0), (768, 1024, -12.0), (1024, 1152, -0.5)):
        fill(T.CT[:, a:b], c, [("CT", a)], (b - a) // 2)
    cp(T.PF[:, 0:2], T.PI[:, 1:3], ["PI"], [("PF", 0)])
    pG, pL, P0 = T.PF[:, 0:1], T.PF[:, 1:2], ("PF", 0)
    pick(T.ID[:], T.ONES[:, 0:128], col, OP.is_equal, 0.0, ["ONES"], ["ID"], 128)
    ts(T.BO[:], T.MG[:], pG, OP.is_equal, ["MG", P0], ["BO"], n=128)
    tt(T.MNE[:], T.BO[:], T.ID[:], OP.subtract, ["BO", "ID"], ["MNE"], 256)
    ts(T.BOX[:], T.ID[:], -16.0, OP.mult, ["ID"], ["BOX"])
    tt(T.BOX[:], T.BOX[:], T.BO[:], OP.add, ["BO", "BOX"], ["BOX"], 256)
    cp(T.WF[:], T.WI[:], ["WI"], ["WF"])
    ts(T.W1[:], T.MNE[:], T.WF[:, 0:1], OP.mult, ["MNE", "WF"], ["W1"])
    ts(T.W2[:], T.MNE[:], T.WF[:, 1:2], OP.mult, ["MNE", "WF"], ["W2"])
    ts(T.W132[:], T.MNE[:], T.WF[:, 0:1], OP.mult, ["MNE", "WF"], ["W132"], 32.0, OP.mult)
    ts(T.W232[:], T.MNE[:], T.WF[:, 1:2], OP.mult, ["MNE", "WF"], ["W232"], 32.0, OP.mult)
    pick(T.SL[:], T.BO[:], col, OP.is_gt, 0.0, ["BO"], ["SL"], 128)
    pick(T.SL[:], T.SL[:], col, OP.not_equal, -1.0, ["SL"], ["SL"], 128)
    for i, (nm, src, c) in enumerate((("BON64", "BO", -64.0), ("IDN", "ID", -1.0), ("BO8192", "BO", 8192.0),
                                      ("BON128", "BO", -128.0), ("BON512", "BO", -512.0), ("BO512", "BO", 512.0), ("BO64", "BO", 64.0),
                                      ("LTH", "SL", -4096.0), ("LTX", "SL", -64.0), ("LTF", "SL", -65.0), ("IDN4096", "ID", -4096.0))):
        if i < SCALED:
            act(T[nm][:], T[src][:], [src], [nm], 128, scale=c)
        else:
            ts(T[nm][:], T[src][:], c, OP.mult, [src], [nm])
    for nm, c in (("B30", -3.0), ("BNA", 2.0 / 4096), ("BPA", -1.0 / 4096)):
        ts(T[nm][:], T.BO[:, ::16], c, OP.mult, ["BO"], [nm])
    fill(T.ZR[:], 0.0, ["ZR"])
    for t in range(3):
        fill(T["BT%d" % t][:], 0.0, ["BT%d" % t])
        cp(T["BT%d" % t][:, t::16], T.BO64[:, ::16], ["BO64"], ["BT%d" % t])
    for e in range(8):
        if e < ZERO:
            fill(T.SK[:, 256 * e:256 * e + 256], 0.0, [("SK", "zero", e)], 128)
        else:
            act(T.SK[:, 256 * e:256 * e + 256], T.ONES[:], ["ONES"], [("SK", "zero", e)], 256, scale=0.0)
    for e in range(8):
        pick(T.SK[:, 16 * e:16 * e + 129 * 15 + 1:129], T.BOX[:, 16 * e:16 * e + 16], [[0, 16]], OP.is_ge, 0.0, ["BOX", ("SK", "zero")],
             [("SK", e)], 16, 127)
    iota(T.T3[:], [[1, 4]], 0, 0, ["T3"], 4)
    ts(T.PF[:, 10:11], T.THI[:], -2041.0, OP.add, ["THI"], [("PF", 10)], -1.0 / 4096, OP.mult)
    ts(T.THB[:], T.BO[:, ::16], T.PF[:, 10:11], OP.mult, ["BO", ("PF", 10)], ["THB"])
    iota(T.PC[:], [[-1, 2], [100, 2]], 0, 0, ["PC"], 4)
    iota(T.MP[:], [[2, 4], [100, 2], [0, 16]], 0, 0, ["MP"], 128)
    ts(T.PF[:, 2:6], T.PC[:], pG, OP.add, ["PC", P0], [("PF", 2)])
    for i in range(4):
        ts(T["PM%d" % i][:], T.MP[:], T.PF[:, 2 + i:3 + i], OP.is_equal, ["MP", ("PF", 2)], ["PM%d" % i], n=128)
        ts(T["PN%d" % i][:], T["PM%d" % i][:], 64.0, OP.mult, ["PM%d" % i], ["PN%d" % i])
    for i, c in enumerate((1.0, 64.0, -64.0)):
        ts(T.LE[:, 4 * i:4 * i + 4], T.T3[:], pL, OP.is_equal, ["T3", P0], [("LE", i)], c, OP.mult)
    act(T.PF[:, 8:9], pL, [P0], [("PF", 8)], 1, func=AF.Identity, scale=4.0, bias=-60.5)
    iota(T.IO64[:], [[1, 64]], 0, 0, ["IO64"], 64)
    for e in range(2):
        rx = T.RX[:, 256 * e:256 * e + 256]
        pick(rx, T.ONES[:], [[1, 2], [0, 8], [4, 16]], OP.is_equal, 0.0, ["ONES"], [("RX", e)], 256, 2 * e)
        pick(rx, rx, [[1, 2], [0, 8], [4, 16]], OP.not_equal, -1.0, [("RX", e)], [("RX", e)], 256, 2 * e + 4)
    pick(T.RX[:, 15::16], T.RX[:, 15::16], [[1, 4], [0, 8]], OP.not_equal, 1.0, ["RX"], ["RX"], 32)
    JI, RA, RB, RC = (T.RW[:, 16 * i:16 * i + 16] for i in range(4))
    iota(JI, [[1, 16]], 0, 0, ["JI"], 16)
    ts(RC, JI, pL, OP.is_equal, ["JI", P0], ["RC"], -2.0, OP.mult)
    ts(RA, JI, pL, OP.is_gt, ["JI", P0], ["RA"], 2.0 ** -30, OP.mult)
    ts(RB, JI, pL, OP.is_gt, ["JI", P0], ["RB"], 2.0 ** 30, OP.mult)
    ts(JI, JI, pL, OP.is_le, ["JI", P0], ["JI"])
    tt(RC, RC, JI, OP.add, ["RC", "JI"], ["RC"])
    tt(RA, RA, RC, OP.add, ["RA", "RC"], ["RA"])
    tt(RB, RB, RC, OP.add, ["RB", "RC"], ["RB"])
    fill(T.RR[:, 34:50], 1.0, [("RR", 34)])
    fill(T.RR[:, 0:18:17], 0.0, [("RR", 0)])
    for a in (0, 17):
        tt(T.RR[:, a + 1:a + 16], T.RW[:, 16:31], T.RW[:, 33:48], OP.mult, ["RA", "RB"], [("RR", a + 1)])
        cp(T.RR[:, a + 16:a + 17], T.RW[:, 31:32], ["RA"], [("RR", a + 16)])
    for h in range(2):
        ts(T.PF[:, 11 + h:12 + h], pL, float(W + 16 * h), OP.add, [P0], [("PF", 11 + h)])

    def scatter(lex, src):
        for c in range(7, -1, -1):
            step[0] = (t, "letters" if lex == "LX" else "rest", c // 4)
            ap, key = part(src, c // 4, 32 * (c % 4), 32 * (c % 4) + 32)
            cp(T[lex][:].indirect(T.OFU[:, 2 * c:2 * c + 2]), ap, [("OFU", c // 4), key], [lex])
            indirect("puts", 32)

    XP, SCORE, COLS, ENDS, HASH, HOT = LAID

    def hashed(X, h, idle=False):
        s, b, q = half(h), HASH[h], T.Q[:, 256 * h:256 * h + 256]
        for o, ws in ((0, ("W132", "W232")), (256, ("W1", "W2"))):
            n = 128 if o and not idle else 256
            mm(ps(b, o, o + n), T.ONES[:, 0:128], T.CT[:, o:o + n], True, False, ["ONES", ("CT", o)], b, n)
            for j, w in enumerate(ws):
                mm(ps(b, o + 128 * j, o + 128 * j + 128), T[w][:], part(X, h)[0], False, j == 1 and (idle or o == 0), [w, (X, h)], b, 128)
        if idle:
            z = T.PR if h else T.ZI
            cp(z[:], ps(b, 256, 512), [b], [z.name], 256)
            ts(z[:], z[:], 4095, OP.bitwise_and, [z.name], [z.name], n=256)
            tt(T.UP[:, s], z[:, 0:128], z[:, 128:256], OP.mult, [z.name], [("UP", h)], 256)
            tt(T.HI[:, s], T.UP[:, s], ps(b, 0, 128), OP.add, [("UP", h), b], [("HI", h)], 128)
            ts(T.HI[:, s], T.HI[:, s], 5, OP.arith_shift_right, [("HI", h)], [("HI", h)], 4095, OP.bitwise_and, 128)
            return
        act(q, ps(b, 0, 256), [b], [("Q", h)], 256, func=AF.Identity, scale=2.0 ** -17, bias=223.5 + 1.0 / 8192)
        mm(ps(b, 256, 512), T.IDN4096[:], q, False, True, ["IDN4096", ("Q", h)], b, 256)
        act(T.UP[:, s], ps(b, 384, 512), [b], [("UP", h)], 128, func=AF.Identity, bias=160.0 * 4096)
        tt(T.PR[:, s], T.UP[:, s], ps(b, 256, 384), OP.mult, [("UP", h), b], [("PR", h)], 128)
        tt(T.ZI[:, s], T.PR[:, s], ps(b, 0, 128), OP.add, [("PR", h), b], [("ZI", h)], 128)
        ts(T.HI[:, s], T.ZI[:, s], 5, OP.arith_shift_right, [("ZI", h)], [("HI", h)], 4095, OP.bitwise_and, 128)

    for h in (1, 0):
        hashed("X0", h, h in IDLE)
        cp(T.H0[:, half(h)], T.HI[:, half(h)], [("HI", h)], [("H0", h)], 128)

    for t in range(3):
        mn, ma, un, out = "MN%d" % t, "MA%d" % t, "UN%d" % t, "OUT%d" % t
        X, P, H, M, M1 = "X%d" % t, "P%d" % t, "H%d" % t, "M%d" % t, "M%d" % (t + 1)
        TM = T[M]
        for h in (1, 0):
            step[0] = (t, "offsets", h)
            if t and h in HALF:
                ts(T[H][:, half(h)], T[P][:, half(h)], 2048.0, OP.add, [(P, h)], [(H, h)])
            else:
                ts(T[P][:, half(h)], T[H][:, half(h)], -2048.0, OP.add, [(H, h)], [(P, h)])
        dst = target(core, t)
        top = slice(0, 64)
        step[0] = (t, "gather")

        for w0, w1, on_vector in PIECES[t]:
            args = (T.CB[:, 16 * w0:16 * w1], T.LX[:, 0:W].indirect(T[H][:, w0:w1]), ["LX", (H, w0 // 128)],
                    [("CB", w) for w in range(w0 // 8, w1 // 8)])
            if on_vector:
                cp(*args)
            else:
                act(*args, 0)
                in_line("gather")
            indirect("picks", 16 * (w1 - w0))
        for h in (1, 0):
            mm(ps(XP[h], 128, 192), T.ID[:], part(X, h, 0, 64)[0], True, True, ["ID", part(X, h)[1]], XP[h], 64)
            for j in range(2):
                mm(T[XP[h]][:, 0:4, j::2], T.ID[:], part(X, h, 64, 128)[0], True, True, ["ID", part(X, h)[1]], XP[h], 64)

        def lane(h):
            b, s, z = SCORE[h], half(h), XP[h]
            for w0, n in ((224, 32), (192, 32), (128, 64)) if h else ((0, 64), (64, 32), (96, 32)):
                m, w = 64 // n, w0 // 64 * 64
                x0 = 128 if m == 1 else 2 * (w0 - w)
                for k in range(16 // m):
                    o, words = 16 * w + 64 * m * k, [("CB", x) for x in range(w0 // 8, (w0 + n) // 8)]
                    e = o + 2 * (w0 - w)
                    tt(T.EB[:, e:e + 64], T.CB[:, 16 * w0 + k:16 * (w0 + n):16 // m], ps(z, x0, x0 + 64), OP.not_equal, words + [z],
                       [("EB", o, e)])
                    for j in range(m if w0 not in (224, 64) else 0):
                        mm(ps(b, w % 128, w % 128 + 64), T.SK[:, 128 * (k + 8 * j):128 * (k + 8 * j + 1)], T.EB[:, o + j:o + 64 * m:m],
                           k + 8 * j == 0, k + 8 * j == 15, ["SK", ("EB", o)], b, 64)
            step[0] = (t, "f", h)
            ts(T.PB[:, s], ps(b, 0, 128), -11.5, OP.is_le, [b], [("PB", h)], n=128)
            sums(z, h, ((384, "ID", P), (384, "LTH", "PB")))
            ts(T.FH[:, 4 * h:4 * h + 4, :], ps(z, 384, 512), -4096.0, OP.add, [z], [("FH", h)], -2048.0, OP.max, 128)
            step[0] = (t, "xf", h)
            sums(b, h, ((256, "ID", X), (256, "LTX", "PB"), (384, "LTF", "PB")))
            act(T.XF[:, 256 * h:256 * h + 256], ps(b, 256, 512), [b], [("XF", h)], 256, func=AF.Relu, bias=-64.0)
            calls[-1]["behind"] = lines["gather"]
            step[0], c = (t, "np", h), NONE[h]
            mm(ps(c, 128, 256), T.ID[:], T.CB[:, 2048 * h + t:2048 * h + 2048:16], True, False,
               ["ID"] + [("CB", x) for x in range(16 * h, 16 * h + 16)], c, 128)
            mm(ps(c, 128, 256), T.IDN[:], part(X, h)[0], False, False, ["IDN", part(X, h)[1]], c, 128)
            mm(ps(c, 128, 256), T.BON128[:], T.PB[:, s], False, True, ["BON128", ("PB", h)], c, 128)
            act(T.NP[:, s], ps(c, 128, 256), [c, "LE"], [("NP", h)], 128, func=AF.Relu, scale=T.LE[:, t:t + 1], bias=T.LE[:, 4 + t:5 + t])
            calls[-1]["behind"] = lines["gather"]

        def letters(h):
            b = LETTERS[h]
            sums(b, h, ((256, "ID", X), (256, "BT%d" % t, "FB"), (256, "ID", "NP")))
            act(T.XA[:, half(h)], ps(b, 256, 384), [b, "LE"], [("XA", h)], 128, func=AF.Identity, bias=T.LE[:, 8 + t:9 + t])

        def place_f(h):
            c4 = slice(4 * h, 4 * h + 4)
            for i in range(4):
                s, c = i // 2, i % 2
                mm(T.B3[:, c4, 16 * s:16 * s + 16], T["PM%d" % i][:], T.FH[:, c4, 16 * c:16 * c + 16], c == 0, c == 1,
                   ["PM%d" % i, ("FH", h)], "B3", 64)
            tr(T.KB[:, c4, :], T.B3[:, c4, :], ["B3"], [("KB", h)])
            ts(T.LF[:, 8 * h:8 * h + 8], T.KB[:, c4, ::16], 32768.0, OP.add, [("KB", h)], [("LF", h)])

        def lookup_f(h):
            s, places, b = half(h), T.LF[:, 8 * h:8 * h + 8], COLS[h]
            if "g%d" % h not in ONV:
                for name, lex in (("GG", "LM"), ("CC", "LX")):
                    act(T[name][:, s], T[lex][:, 0:W].indirect(places), [lex, ("LF", h)], [(name, h)], 0)
                    indirect("picks", 128)
                sums(b, h, ((256, "LTX", "PB"), (128, "IDN", M), (256, "ID", "CC"), (128, "ID", "GG")))
                act(T.RL[:, s], ps(b, 128, 256), [b], [("RL", h)], 128, func=AF.Abs)
                act(T.FC[:, s], ps(b, 256, 384), [b], [("FC", h)], 128, func=AF.Relu, bias=-64.0)
                act(T.D16[:, s], ps(b, 128, 256), [b], [("D16", h)], 128, func=AF.Identity, scale=0.5, bias=1535.75)
                for o, src, w in ((8, "FB", "THB"), (8, "FB", "BC"), (8, "NP", "B30"), (0, "FC", "BO"), (8, "RL", "BA")):
                    ap, key = part(src, h)
                    mm(ps(b, o, o + 8), ap, T[w][:, ::16] if w == "BO" else T[w][:], w == "THB", w == "BA", [key, w], b, 8)
                return
            tt(T.SUB[:, s], T.LM[:, 0:W].indirect(places), TM[:, s], OP.subtract, ["LM", M, ("LF", h)], [("SUB", h)])
            indirect("picks", 128)
            tt(T.FC[:, s], T.LX[:, 0:W].indirect(places), part("FB", h)[0], OP.mult, ["LX", ("LF", h), ("XF", h)], [("FC", h)])
            indirect("picks", 128)
            ts(T.RL[:, s], T.SUB[:, s], 0.0, OP.max, [("SUB", h)], [("RL", h)], -63.75, OP.add)
            for o, src, w in ((8, "FB", "THB"), (8, "NP", "B30"), (8, "SUB", "BPA"), (0, "FC", "BO"), (8, "RL", "BNA")):
                ap, key = part(src, h)
                mm(ps(COLS[h], o, o + 8), ap, T[w][:, ::16] if w == "BO" else T[w][:], w == "THB", w == "BNA", [key, w], COLS[h], 8)

        def hot_x(h):
            b = HOT[h]
            mm(ps(b, 0, 8), part("FX", h)[0], T.BO[:, ::16], True, True, ["BO", ("XF", h)], b, 8)
            for e in range(8):
                ts(T.OHX[:, 512 * h + 64 * e:512 * h + 64 * e + 64], T.IO64[:], ps(b, e, e + 1), OP.is_equal, ["IO64", b], [("OHX", h, e)])

        def coded(h):
            for pm, src, o in (("PN", "XF", 256 * h), ("PM", "FC", 128 * h)):
                for i in range(4):
                    s, w0 = i // 2, o + 64 * (i % 2)
                    mm(T.B3[:, 8 + 4 * h:12 + 4 * h, 16 * s:16 * s + 16], T[pm + str(i)][:], T[src][:, w0:w0 + 64], src == "XF" and i == 0,
                       src == "FC" and i == 3, [pm + str(i), (src, h)], "B3", 64)
            tr(T.KC[:, 4 * h:4 * h + 4, :], T.B3[:, 8 + 4 * h:12 + 4 * h, :], ["B3"], [("KC", h)])

        def table(h):
            for e in range(8):
                s, b = slice(512 * h + 64 * e, 512 * h + 64 * e + 64), COLS[h]
                ts(T.OHC[:, s], T.IO64[:], ps(b, e, e + 1), OP.not_equal, ["IO64", b], [("OHC", h, e)], ps(b, 8 + e, 9 + e), OP.is_lt)
                rd = [("OHX", h, e), ("OHC", h, e)]
                mm(ps("B6", 0, 64, top), T.OHX[:, s], T.OHC[:, s], (h, e) == (1, 0), False, rd, "B6", 64)
                mm(ps("B6", 0, 64, top), T.OHC[:, s], T.OHX[:, s], False, (h, e) == (0, 7), rd, "B6", 64)

        def ahead(h):
            s, b = half(h), HASH[h]
            sums(b, h, ((384, "ID", X), (384, "IDN", "FX"), (384, "ID", "NP"), (384, "ID", "FC")))
            tt(part(un, h)[0], T.XA[:, s], ps(b, 384, 512), OP.min, [("XA", h), b], [(un, h)], 128)
            hashed(un, h)
            if h and SCAN:
                mm(ps(b, 128, 256), T.ONES[:, 0:128], T.CT[:, 640:768], True, False, ["ONES", ("CT", 640)], b, 128)
                sums(b, h, ((128, "ID", P),), False)
                tt(T.DI[:, 0::2], ps(b, 128, 256), T.HI[:, s], OP.subtract, [b, ("HI", h)], [("DI", 0)], 128)
                cp(T.DI[:, 1::2], T.HI[:, s], [("HI", h)], [("DI", 1)], 128)

        parts = dict(lane=lane, letters=letters, place=place_f, lookup=lookup_f, ahead=ahead, coded=coded, hot=hot_x, table=table)
        for name in TEXT:
            h = int(name[-1])
            if name[:-1] != "ahead" or (t < 2 and h in AHEAD):
                step[0] = (t, name)
                parts[name[:-1]](h)
        step[0] = (t, "mask")
        for h in (1, 0):
            sums("B4", h, ((128 * h, "BO", "FX"), (128 * h, "BON64", "FB")))
        act(T.MK[:], ps("B4", 0, 256), ["B4", ("PF", 8)], ["MK"], 256, func=AF.Sign, scale=-1.0, bias=T.PF[:, 8:9])
        if "kl" in ONV:
            ts(T.EQ[:, :, 16:50:33], T.KB[:, :, ::16], 1.0 / 8192, OP.mult, ["KB"], [("EQ", 0, "h"), ("EQ", 1, "h")], 5.0, OP.add)
        else:
            act(T.EQ[:, :, 16:50:33], T.KB[:, :, ::16], ["KB"], [("EQ", 0, "h"), ("EQ", 1, "h")], 16, func=AF.Identity, scale=1.0 / 8192, bias=5.0)
        step[0] = (t, "codes")
        for o in range(2):
            cp(T.CI[:, :, 4 * o:4 * o + 4], T.KC[:, :, 16 * o], ["KC"], [("CI", o)])
        ts(T.CI[:], T.CI[:], 255, OP.bitwise_and, ["CI"], ["CI"])
        cp(T.CL[:], T.CI[:], ["CI"], ["CL"])
        step[0] = (t, "d16")
        if "g1" in ONV:
            act(T.D16[:], T.SUB[:], ["SUB"], ["D16"], 256, func=AF.Identity, scale=0.5, bias=1535.75)
        else:
            act(T.D16[:, 0:128], T.SUB[:, 0:128], [("SUB", 0)], [("D16", 0)], 128, func=AF.Identity, scale=0.5, bias=1535.75)
        step[0] = (t, "spread")
        ts(T.TB[top, :], ps("B6", 0, 64, top), 0.5, OP.min, ["B6"], ["TB"])
        for r in range(4):
            mm(ps("B6", 256 + 64 * r, 320 + 64 * r), T.RX[top, 128 * r:128 * r + 128], T.TB[top, :], True, True, ["RX", "TB"], "B6", 64)
        (act if "tw" not in ONV else cp)(T.TW[:], ps("B6", 256, 512), ["B6"], ["TW"], 256)
        for h in (1, 0):
            s, b = half(h), ENDS[h]
            step[0] = (t, "ends", h)
            tt(T.GT[:, s], T.TW[:].indirect(T.CL[:, 8 * h:8 * h + 8]), T.MK[:, s], OP.mult, ["TW", "CL", "MK"], [("GT", h)])
            indirect("picks", 128)
            rows = [(128, "BO", "FH"), (128, "BO8192", "NP"), (128, "BO8192", "GT")]
            if t == 2 or h not in AHEAD:
                rows = [(0, "ID", X), (0, "IDN", "FX"), (0, "ID", "NP"), (0, "ID", "FC")] + rows + [(0, "BO64", "GT")]
            sums(b, h, rows)
            step[0] = (t, "change", h)
            if t == 2:
                tt(T.XN[:, s], T.XA[:, s], ps(b, 0, 128), OP.min, [("XA", h), b], [("XN", h)], 128)
            elif h not in AHEAD:
                hn, o2 = "HN%d" % t, 256 * h
                tt(part(un, h)[0], T.XA[:, s], ps(b, 0, 128), OP.min, [("XA", h), b], [(un, h)], 128)
                send(dst, part("X%d" % (t + 1), h)[0], part(un, h)[0], [(un, h)], [("X%d" % (t + 1), h)], ("aw", "ax")[h] + str(t + 1))
                hashed(un, h)
                cp(T[hn][:, o2:o2 + 128], T.HI[:, s], [("HI", h)], [(hn, h)], 128)
                send(dst, part("H%d" % (t + 1), h)[0], T[hn][:, o2:o2 + 128], [(hn, h)], [("H%d" % (t + 1), h)], ("az", "ay")[h] + str(t + 1))
            else:
                o, c, sem = 512 * h, HASH[h], ("az", "ay")[h] + str(t + 1)
                hn, o2 = "HN%d" % t, 256 * h
                if h and SCAN:
                    mm(T[c][:, 256:512], T.ZR[:], T.ONES[:], True, False, ["ZR", "ONES"], c, 256)
                    mm(T[c][:, 257:512:2], T.BO[:], T.GT[:, s], False, True, ["BO", ("GT", h)], c, 128)
                    do("v", [c, "DI"], ["SO"], cycles(256), "scan", dict(out=T.SO[:], data0=T[c][:, 256:512], data1=T.DI[:], initial=0.0,
                                                                         op0=OP.mult, op1=OP.add))
                    cp(T[hn][:, o2:o2 + 128], T.SO[:, 1::2], ["SO"], [(hn, h)], 128)
                else:
                    mm(ps(c, 128, 256), T.ONES[:, 0:128], T.CT[:, 512:640], True, False, ["ONES", ("CT", 512)], c, 128)
                    sums(c, h, ((128, "ID", P), (128, "BO8192", "GT")), False)
                    tt(T.PR[:, s], ps(c, 128, 256), T.HI[:, s], OP.max, [c, ("HI", h)], [("PR", h)], 128)
                    ts(T.HI[:, s], T.PR[:, s], 4095, OP.bitwise_and, [("PR", h)], [("HI", h)], n=128)
                    cp(T[hn][:, o2:o2 + 128], T.HI[:, s], [("HI", h)], [(hn, h)], 128)
                send(dst, part("H%d" % (t + 1), h)[0], T[hn][:, o2:o2 + 128], [(hn, h)], [("H%d" % (t + 1), h)], sem)
                places_out = len(calls) - 1
                step[0] = (t, "letters out", h)
                if "x%d" % h in FOLDS:
                    sums("B4", h, ((128 * h, "ID", X), (128 * h, "BO64", "GT")))
                    act(T[out][:, o + 256:o + 384], ps("B4", 128 * h, 128 * h + 128), ["B4"], [(out, h, "x")], 128, func=AF.Identity, bias=-64.0)
                    letters_out = [T[out][:, o + 256:o + 384], part(un, h)[0]]
                elif "x%d" % h not in ONV:
                    sums("B4", h, ((128 * h, "ID", X), (128 * h, "IDN", un), (128 * h, "BO64", "GT")))
                    act(T.XR[:, s], ps("B4", 128 * h, 128 * h + 128), ["B4"], [("XR", h)], 128, func=AF.Relu, bias=-64.0)
                    sums("B4", h, ((128 * h, "ID", un), (128 * h, "ID", "XR")))
                    letters_out = T[out][:, o + 256:o + 384]
                    act(letters_out, ps("B4", 128 * h, 128 * h + 128), ["B4"], [(out, h, "x")], 128)
                else:
                    mm(ps("B4", 128 * h, 128 * h + 128), T.ONES[:, 0:128], T.CT[:, 1024:1152], True, False, ["ONES", ("CT", 1024)], "B4", 128)
                    sums("B4", h, ((128 * h, "ID", X), (128 * h, "BO64", "GT")), False)
                    letters_out = T[out][:, o + 256:o + 384]
                    tt(letters_out, part(un, h)[0], ps("B4", 128 * h, 128 * h + 128), OP.max, ["B4", (un, h)], [(out, h, "x")], 128)
                send(dst, part("X%d" % (t + 1), h)[0], letters_out, [(out, h, "x"), (un, h)], [("X%d" % (t + 1), h)], ("aw", "ax")[h] + str(t + 1))

            c4, step[0] = slice(4 * h, 4 * h + 4), (t, "who", h)
            for o, a, c in ((0, 0, 0), (17, 16, 16), (33, 16, 0)):
                tt(T.EQ[:, c4, o:o + 16], T.KB[:, c4, a:a + 16], T[b][:, 4:8, c:c + 16], OP.is_equal, [("KB", h), b], [("EQ", h, o)])
            for j in range(4 * h, 4 * h + 4):
                do("v", ["RR", ("EQ", h)], [("SC", h, j)], cycles(50), "scan",
                   dict(out=T.SC[:, j, :], data0=T.RR[:], data1=T.EQ[:, j, :], initial=0.0, op0=OP.mult, op1=OP.add))
            for o in range(2):
                ts(T.OFU[:, 8 * h + o:8 * h + 8:2], T.SC[:, c4, 16 + 33 * o], 8192.0, OP.mult, [("SC", h), ("PF", 11 + o)],
                   [("OFU", h, o)], T.PF[:, 11 + o:12 + o], OP.min)
        if t == 2:
            send(dst, T.X3[:], T.XN[:], ["XN"], ["X3"], "ax3", 1.5)
        for h in (1, 0):
            step[0] = (t, "merged", h)
            sums("B2", h, [(128 * h, l, src) for l, src in (("ID", M), ("ID", "D16"), ("BON512", "NP"), ("BON512", "GT"))])
            if t < 2 or h == 0:
                c0, c1 = (128 * h, 128 * h + 128) if t < 2 else (0, 256)
                act(T.MA[:, 256 * t + c0:256 * t + c1], ps("B2", c0, c1), ["B2"], [(ma, h) if t < 2 else ma], c1 - c0, func=AF.Identity, bias=-1536.0)
        step[0] = (t, "kept")
        for h in (1, 0):
            sums("B3", h, [(128 * h, l, src) for l, src in (("ID", M), ("BON512", "FB"), ("BO512", "GT"))])
        if t < 2:
            act(T[mn][:], ps("B3", 0, 256), ["B3"], [mn], 256)
        else:
            tt(T[mn][:], T.MA[:, 512:768], ps("B3", 0, 256), OP.max, ["B3", ma], [mn], 256)
        scatter("LX", un if t < 2 else "XN")
        if t < 2:
            scatter("LM", ma)
        step[0] = (t, "meanings")
        send(dst, T[M1][:], [T.MA[:, 256 * t:256 * t + 256], T[mn][:]] if t < 2 else T[mn][:], [mn, ma], [M1], "am" + str(t + 1), 1.5)
        if t == 0:
            iota(T.NUM[:], [[1, 256]], 32, 0, ["NUM"], 256)
            calls[-1]["behind"] = sent = [i for i, c in enumerate(calls[:-1]) if c["name"] == "send"]
            for e in range(4):
                iota(T.WN[:, 1032 * e:1032 * e + 1032], [[0, 1032]], 0, 0, [("WN", e)], 1032)
                calls[-1]["behind"] = sent
            step[0] = (1, "numbers")
            act(T.SN[:], T.NUM[:], ["NUM"], ["SN"], 256 + 1600, func=AF.Silu)

    for c in range(7, -1, -1):
        step[0] = (t, "rest", c // 4)
        if c >= SPLIT:
            act(T.WN[:].indirect(T.OFU[:, 2 * c:2 * c + 2]), T.NUM[:, 32 * c:32 * c + 32], [("OFU", c // 4), "NUM", "SN"], ["WN"], 0, func=AF.Silu)
        else:
            cp(T.WN[:].indirect(T.OFU[:, 2 * c:2 * c + 2]), T.SN[:, 32 * c:32 * c + 32], [("OFU", c // 4), "SN"], ["WN"])
        indirect("puts", 32)
    step[0] = "sum"
    for j in range(8):
        mm(ps("B6", 0, 512), T.ID[:], T.LM[:, 512 * j:512 * j + 512], j == 0, j == 7, ["ID", "LM"], "B6", 512)
    mm(ps("B4", 0, 256), T.ONES[:, 0:128], T.CT[:, 768:1024], True, False, ["ONES", ("CT", 768)], "B4", 256)
    for h in (0, 1):
        for l, src in (("IDN", "SUB"),) if "g%d" % h in ONV else (("IDN", "GG"), ("ID", "M2")):
            mm(ps("B4", 128 * h, 128 * h + 128), T[l][:], T[src][:, half(h)], False, False, [l, (src, h)], "B4", 128)
    mm(ps("B4", 0, 256), T.ID[:], T.D16[:], False, True, ["ID", "D16"], "B4", 256)
    act(ps("B6", 0, 512), ps("B6", 0, 512), ["B6"], ["B6", "B3", "sum"], 700, accum_out=ps("B3", 0, 1))
    dma("y", T.yl[:], T.LX[:, 0:W], ["LX"], ["yl"], LAST)
    tt(T.PB[:], T.WN[:, 0:W].indirect(T.LF[:, 0:16]), T.SN[:], OP.is_equal, ["WN", "SN", "LF"], ["PB"])
    indirect("picks", 256)
    cp(T.WD[:, 256:257], ps("B3", 0, 1), ["B3"], [("WD", 1)])
    tt(T.WD[:, 0:256], T.PB[:], ps("B4", 0, 256), OP.mult, ["PB", "B4"], [("WD", 0)], 256)
    do("v", ["WD"], ["YM"], cycles(257), "reduce", dict(out=T.PF[:, 15:16], in_=T.WD[:], axis=AxisListType.X, op=OP.add))
    for out, src in (("yx", "X3"), ("ym", "YM"), ("yg", "M3")):
        dma("s", T[out][:], T.PF[:, 15:16] if src == "YM" else T[src][:], [src, mn, "sum"], [out], 1600)
        in_line("stores")

    que = {"v": g.vector, "s": g.scalar, "t": g.tensor, "g": g, "y": g.sync}
    clock = {q: {} for q in que}
    count = {"qv": 0, "qs": 0, "qt": 0, "qg": 0}
    done, touch, others, n_dma, n_sent = {}, {}, [], 0, 0

    def wait(q, tok):
        sem, n, snap = tok
        if clock[q].get(sem, 0) >= n:
            return
        que[q].wait_ge(T.sem[sem], n)
        for s, m in snap.items():
            if clock[q].get(s, 0) < m:
                clock[q][s] = m
        clock[q][sem] = n

    if not _ORDER:
        _ORDER.extend(in_order(calls))
    for i in _ORDER:
        c = calls[i]
        q, name, kw = c["q"], c["name"], c["kw"]
        toks = {}
        for tok in ([done[p] for p in c["after"] if not q == calls[p]["q"] == "t"]
                    + [tok for b in c["banks"] for e, tok in touch.get(b, {}).items() if e != q]):
            if tok[0] not in toks or toks[tok[0]][1] < tok[1]:
                toks[tok[0]] = tok
        for tok in toks.values():
            wait(q, tok)
        if name == "send":
            mask = topo.mask(core, kw[0])
            if kw[3] in HANDED:
                write(helper(core), kw[1], kw[2], kw[3], topo.mask(core, helper(core)) & ~mask if SPARE else mask)
            else:
                write(kw[0], kw[1], kw[2], kw[3], mask)
            done[i] = (kw[3], len(topo.engines(core, kw[0])), {})
            n_sent += done[i][1]
            others.append(done[i])
            continue
        if name == "dma":
            sem = "d%d" % n_dma
            n_dma += 1
            que[q].dma_start(*kw).then_inc(T.sem[sem], 16)
            done[i] = (sem, 16, dict(clock[q]))
            others.append(done[i])
            continue
        if name == "copy":
            ins = g.vector.tensor_copy(**kw)
        elif name == "tt":
            ins = g.vector.tensor_tensor(**kw)
        elif name == "ts":
            ins = g.vector.tensor_scalar(**kw)
        elif name == "act":
            ins = g.scalar.activation(**kw)
        elif name == "mm":
            ins = g.tensor.matmul(*kw)
        elif name == "fill":
            ins = g.vector.memset(*kw)
        elif name == "iota":
            ins = g.iota(**kw)
        elif name == "pick":
            ins = g.affine_select(**kw)
        elif name == "reduce":
            ins = g.vector.tensor_reduce(**kw)
        elif name == "turn":
            ins = g.vector.transpose(**kw)
        else:
            ins = g.vector.tensor_tensor_scan(**kw)
        sem = "q" + q
        count[sem] += 1
        ins.then_inc(T.sem[sem], 1)
        done[i] = (sem, count[sem], dict(clock[q]))
        for b in c["banks"]:
            touch.setdefault(b, {})[q] = done[i]
    for sem in count:
        wait("g", (sem, count[sem], {}))
    for tok in others:
        wait("g", tok)
    g.wait_ge(T.sem.ls, n_sent)
